import numpy as np, ml_dtypes
CORES = [48,51,52,55]
N = 4
BF = ml_dtypes.bfloat16
def gentries(a):
    return np.ascontiguousarray(a.reshape(8, 16, -1).transpose(0, 2, 1)).reshape(8, -1)
def gtable(e):
    e = np.asarray(e); return np.ascontiguousarray(e.reshape(8, -1, 16).transpose(0, 2, 1)).reshape(128, -1).astype(np.int32)
W, K, L, V, C, WB = 4096, 8, 384, 5, 8, 12
SH = (N, 8, 16, W)
def join(d0, c0, d1, c1):
    return (d0 + W * c0) + 32768 * (d1 + W * c1)
def goals(rng, hub, share):
    j = rng.integers(0, hub.shape[3], SH)
    return np.where(rng.random(SH, dtype=np.float32) < share, np.take_along_axis(hub, j, 3), rng.integers(0, W, SH))
def field(rng):
    return rng.integers(0, W, (N, 8, 16, K // 2 + 1)), rng.choice(np.array([0.0, 0.25, 0.6, 0.95]), (N, 8, 16, 1))
def parts(rng):
    hub, share = field(rng)
    a = join(goals(rng, hub, share), rng.integers(0, C, SH), goals(rng, hub, share), rng.integers(0, C, SH))
    pay = (0.25 + 0.75 * rng.random(SH, dtype=np.float32)) * np.exp2(rng.integers(-1, 2, (N, 8, 16, 1)))
    ac = 4 * rng.random((N, 8, 16, L)); st = rng.integers(0, W, (N, 8, K, L)); rs = (64 * rng.random((N, 8, K, L)) ** 3).astype(np.int64)
    return a, pay, ac, st, rs
def pack(a, pay, ac, st, rs):
    return {"arcs": np.ascontiguousarray(a.reshape(N, 128, W)).astype(np.int32), "pay": np.ascontiguousarray(pay.reshape(N, 128, W)).astype(BF),
            "ac": np.ascontiguousarray(ac.reshape(N, 128, L)).astype(np.float32), "st0": np.stack([gtable(b) for b in st]), "rs0": np.ascontiguousarray(rs.reshape(N, 8, K * L)).astype(np.int32)}
def setup_inputs(rng):
    return pack(*parts(rng))
def setup_inputs_spread(rng):
    a, pay, ac, st, rs = parts(rng)
    a[:, ::2] = rng.integers(0, 2 ** 30, (N, 4, 16, W))
    pay = (0.25 + 0.75 * rng.random(SH, dtype=np.float32)) * np.exp2(rng.integers(-1, 2, (N, 8, 1, W)))
    ac = np.exp2(12 * rng.random((N, 8, 16, L)) - 6); rs = rng.integers(0, 64, (N, 8, K, L))
    return pack(a, pay, ac, st, rs)
def setup_inputs_ends(rng):
    a, pay, ac, st, rs = parts(rng); top = 2 ** 30 - 1
    low = rng.choice(np.array([0.3, 0.5, 0.7]), (N, 8, 16, 1))
    a = np.where(rng.random(SH, dtype=np.float32) < 0.72, np.where(rng.random(SH, dtype=np.float32) < low, 0, top), a)
    st = np.where(rng.random(st.shape) < 0.75, (W - 1) * rng.integers(0, 2, st.shape), st)
    rs = np.where(rng.random(rs.shape) < 0.8, 63 * rng.integers(0, 2, rs.shape), rs)
    ac = np.where(rng.random(ac.shape) < 0.5, 64.0 * rng.integers(0, 2, ac.shape), ac)
    z = [0] + [W - j for j in range(1, K + 1)]
    for j in range(K + 1):
        a[:, :, 14:, z[j]] = 0 if j == 0 else join(z[j], C - 1, z[min(j + 1, K)], C - 1)
        a[:, 1:V, 13, z[j]] = join(0, C - 1, 0, C - 1) if j == 0 else join(z[j], 0, z[j], 0)
    a[:, 7, :14, W - 1] = top
    l = np.arange(7, L, 8); kind = rng.integers(0, 3, (N, 8, len(l))); kind[:, :, -1] = np.arange(8) % 3
    for k in range(K):
        st[:, :, k, l] = z[k]
        rs[:, :, k, l] = 0 if k == 0 else np.where(kind == 0, 63, np.where(kind == 1, 62, 63 if k <= K // 2 else 62))
    ac[:, :, :14, l] = 64.0; ac[:, :, 14, l] = 64.0 * rng.integers(0, 2, kind.shape); ac[:, :, 15, l] = 0.0
    fall = l[1::4]
    ac[:, 0, :15, fall] = 64.0; ac[:, 0, 15, fall] = 0.0
    ac[:, 1:V, :, fall] = 64.0; ac[:, 1:V, 13, fall] = 0.0
    st[:, :, :, L - 2] = W - 1; rs[:, :, :, L - 2] = 63; ac[:, :, :, L - 2] = 64.0
    over = np.arange(L - 3, 0, -32); y = W // 2 + np.arange(K)
    a[:, :, :, y] = join(rng.integers(0, W, (N, 8, 16, K)), C - 1, rng.integers(0, W, (N, 8, 16, K)), C - 1)
    st[:, :, :, over] = y[:, None]; rs[:, :, :, over] = 63
    best = rng.integers(1, 16, (N, 8, 1, len(over)))
    ac[:, :, :, over] = np.where(np.arange(16)[:, None] == best, 64.0 - rng.integers(1, 5, best.shape), 64.0)
    return pack(a, pay, ac, st, rs)
def setup_inputs_corners(rng):
    a, pay, ac, st, rs = parts(rng); pay[:, :, :, W - 1] = 2.0
    j = np.arange(2 * K); hub = K * ((rng.integers(0, W // K, (N, 8, 16, 1)) + 17 * j) % (W // K)) + j % K
    n = rng.choice(np.array([1, 2, K - 1, K, K + 1, 2 * K]), (N, 8, 16, 1)); cls = np.arange(W) % K
    mode = rng.integers(0, 4, (N, 8, 16, 1)); cost = []
    for u in range(2):
        cost.append(np.where(mode == 0, 0, np.where(mode == 1, C - 1, np.where(mode == 2, (C - 1) * rng.integers(0, 2, SH), rng.integers(0, C, SH)))))
    a = join(np.take_along_axis(hub, np.minimum(cls, n - 1), 3), cost[0], np.take_along_axis(hub, np.minimum(cls + K, n - 1), 3), cost[1])
    k = np.arange(K)[:, None]; nil = np.zeros((K, L), np.int64)
    st = K * rng.integers(0, W // K, (N, 8, K, L)) + k
    ways = (nil, nil + 63, nil + np.where(k == 0, 0, 63), nil + np.where(k == K - 1, 0, 63))
    for q in range(N):
        p = rng.permutation(8); b = rng.permutation(8)
        for i in range(4): rs[q, p[i]] = ways[i]
        st[q, b[:2]] = st[q, b[:2], :1]
        st[q, b[2]] = (W - 1) * rng.integers(0, 2, (K, L))
    return pack(a, pay, ac, st, rs)
def setup_inputs_calm(rng):
    a, pay, ac, st, rs = parts(rng); hub, share = field(rng)
    hc = ((2 * np.arange(N)[:, None] + np.arange(8)) % 4)[:, :, None, None]
    c0 = (rng.random(SH) * (hc + 1)).astype(np.int64); c1 = (rng.random(SH) * (hc + 1)).astype(np.int64)
    a = join(goals(rng, hub, share), c0, goals(rng, hub, share), c1)
    rs = np.minimum(rng.integers(0, 4, rs.shape), hc); col = np.arange(L) % 4; s = ac.shape
    ac = np.where(col == 0, 1.0 * rng.integers(0, 3, s), np.where(col == 1, 1 + 2.0 ** -23 * rng.integers(0, 8, s), np.where(col == 2, 0.5 * rng.integers(0, 6, s), 0.0)))
    h = K // 2; z = rng.permutation(W - 1)[:4 * h]
    i = np.arange(4 * h); lab = np.arange(16)[:, None]
    to = np.where(i < 2 * h, 2 * h, 0) + h * (lab % 2); price = np.where(i < 2 * h, 3, 1)
    a[:, :, :, z] = join(z[to + rng.integers(0, h, (N, 8, 16, 4 * h))], price, z[to + rng.integers(0, h, (N, 8, 16, 4 * h))], price)
    l = np.arange(3, L, 8); k = np.arange(K)[:, None]; b = rng.integers(0, 2, (N, 8, 1, len(l)))
    st[:, :, :, l] = z[np.where(k < h, 0, 2 * h) + h * b + k % h]; rs[:, :, :, l] = np.where(k < h, 0, 1)
    p = rng.integers(0, 15, b.shape); q = p + 1 + 2 * (rng.random(b.shape) * ((16 - p) // 2)).astype(np.int64)
    pair = np.array([[11, 8], [8, 5], [16, 11], [5, 0]]); kind = rng.integers(0, 4, b.shape)
    base = 0.25 + 2.0 ** -21 * rng.integers(0, 2 ** 17, b.shape)
    ac[:, :, :, l] = np.where(lab == p, base + 2.0 ** -25 * pair[kind, 0], np.where(lab == q, base + 2.0 ** -25 * pair[kind, 1], 1 + rng.random((N, 8, 16, len(l)))))
    return pack(a, pay, ac, st, rs)
def check_ranges(d):
    bad = []
    for k, lo, hi in (("arcs", 0, 2 ** 30 - 1), ("st0", 0, W - 1), ("rs0", 0, 63)):
        if not (np.min(d[k]) >= lo and np.max(d[k]) <= hi): bad.append("range of " + k)
    e = np.asarray(d["ac"]).astype(np.float32)
    if not np.all((e == 0) | ((e >= 2.0 ** -51) & (e <= 64))): bad.append("range of ac (0, or from 2**-51 to 64)")
    e = np.asarray(d["pay"]).astype(np.float32)
    if not np.all((e >= 0.125) & (e <= 2)): bad.append("range of pay (from 0.125 to 2)")
    return bad
def reference(arcs, pay, ac, st0, rs0):
    A = arcs.astype(np.int32).reshape(N, 8, 16, W); P = pay.astype(np.float32).reshape(N, 8, 16, W); B = ac.astype(np.float32).reshape(N, 8, 16, L)
    s = np.stack([gentries(b) for b in st0]).astype(np.int64); r = rs0.astype(np.int32)
    no = np.arange(2 * K, dtype=np.int32)[:, None]
    ys = np.zeros((N, 8, 16, L)); ym = np.zeros((N, 8, 16, L))
    for t in range(V):
        back = (-t, -t)
        a = np.take_along_axis(np.roll(A, back, (0, 1)), s[:, :, None, :], 3)
        a = np.concatenate([a & 32767, a >> 15], axis=3).reshape(N, 8, 16, 2 * K, L)
        c = (a >> WB) + np.concatenate([r, r], axis=2).reshape(N, 8, 1, 2 * K, L)
        m = np.min(c, axis=3)
        lab = np.argmin(m.astype(np.float32) + np.roll(B, back, (0, 1)), axis=2)[:, :, None, :]
        d = np.take_along_axis(a, lab[:, :, :, None, :], 2)[:, :, 0] & (W - 1)
        x = np.take_along_axis(c, lab[:, :, :, None, :], 2)[:, :, 0] - np.take_along_axis(m, lab, 2)
        key = x * 16 + no
        dup = np.any((d[:, :, :, None] == d[:, :, None]) & (key[:, :, None] < key[:, :, :, None]), axis=3)
        o = np.argsort(np.where(dup, key + 65536, key), axis=2)[:, :, :K]
        gone = np.take_along_axis(dup, o, 2)
        s = np.where(gone, W - 1, np.take_along_axis(d, o, 2)).astype(np.int64).reshape(N, 8, K * L)
        r = np.where(gone, 64, np.take_along_axis(x, o, 2)).astype(np.int32).reshape(N, 8, K * L)
        v = np.take_along_axis(np.roll(P, back, (0, 1)), s[:, :, None, :], 3).reshape(N, 8, 16, K, L) * np.exp(r.astype(np.float64) * -0.125).reshape(N, 8, 1, K, L)
        ys = ys + np.add.reduce(v, axis=3); ym = ym + np.max(v, axis=3)
    return {"ys": ys.reshape(N, 128, L).astype(np.float32), "ym": ym.reshape(N, 128, L).astype(np.float32)}

def check_inputs(d):
    bad = list(check_ranges(d))
    if not bad:
        for name, y in reference(**d).items():
            for q in range(N):
                v = np.abs(np.asarray(y[q], np.float64)); s = np.sqrt(np.mean(v * v))
                if v.max() > 8 * s or s < 2.0 ** 0: bad.append('%s of rank %d is uneven or too small' % (name, q))
    return bad

@@ -1,0 +1,406 @@
+from concourse.mybir import AluOpType, ActivationFunctionType
+
+A = AluOpType
+F = ActivationFunctionType
+V_, L_, W_ = 5, 384, 4096
+f32, bf, i32, u16 = "float32", "bfloat16", "int32", "uint16"
+SCRATCH = {
+    "ar": ("sbuf", [128, W_], i32), "a0": ("sbuf", [128, 2, 512], i32), "a1": ("sbuf", [128, 2, 512], i32),
+    "U0": ("sbuf", [128, W_], f32), "U1": ("sbuf", [128, W_], f32), "TT": ("sbuf", [128, 2 * W_], f32),
+    "MM": ("sbuf", [128, W_], f32), "pr": ("sbuf", [128, W_], bf),
+    "acs": ("sbuf", [128, L_], f32), "acT": ("sbuf", [128, 408], f32),
+    "rsi": ("sbuf", [128, L_], i32), "sti": ("sbuf", [128, 8, 24], i32), "std": ("dram", [8, 8, 2, 8, 24], i32),
+    "G": ("sbuf", [128, 3072], bf), "GS": ("sbuf", [128, 3072], bf), "GA": ("sbuf", [128, 3072], f32),
+    "GP": ("sbuf", [128, 3072], bf), "WW": ("sbuf", [128, 3072], f32),
+    "sc": ("sbuf", [128, 408], f32), "nf": ("sbuf", [128, 408], bf), "s2": ("sbuf", [128, 2, 408], bf),
+    "d3": ("sbuf", [128, L_], bf), "p3": ("sbuf", [128, L_], bf), "d4": ("sbuf", [128, 392], bf), "p4": ("sbuf", [128, 392], bf),
+    "H": ("sbuf", [128, L_], bf), "zb": ("sbuf", [128, 392], bf), "zd": ("sbuf", [128, 49, 8], f32), "I17": ("sbuf", [128, 8, 17], bf),
+    "stf": ("sbuf", [128, 192], f32), "ix2": ("sbuf", [128, 192], u16),
+    "k1": ("sbuf", [128, 24, 16], f32), "k2": ("sbuf", [128, 24, 16], f32), "dup": ("sbuf", [128, 24, 16], f32),
+    "SB": ("sbuf", [128, 2, 24, 2, 2, 2], f32), "KS": ("sbuf", [128, 24, 8], f32), "yy": ("sbuf", [128, 24, 8], f32),
+    "kb": ("sbuf", [128, 16, 16], bf), "cb": ("sbuf", [128, 192], bf), "ng": ("sbuf", [128, 192], bf), "tn": ("sbuf", [128, 192], bf),
+    "Ib": ("sbuf", [128, 128], bf), "In": ("sbuf", [128, 128], bf), "If": ("sbuf", [128, 128], f32),
+    "sD": ("sbuf", [128, 8, 128], bf), "sL": ("sbuf", [128, 8, 17], bf), "sP": ("sbuf", [128, 128], bf),
+    "sC": ("sbuf", [128, 16], f32), "EE": ("sbuf", [128, 1024], bf),
+    "Db": ("sbuf", [128, 2, 64], bf), "Df": ("sbuf", [128, 2, 64], f32), "PM": ("sbuf", [128, 4, 128], f32),
+    "p17": ("sbuf", [128, 408], f32), "pS": ("sbuf", [128, 2, 408], bf), "p8": ("sbuf", [128, 192], bf),
+    "xi": ("sbuf", [128, 5, 192], u16), "xo": ("sbuf", [128, 5, 192], u16),
+    "ri": ("sbuf", [128, 5, L_], bf), "ro": ("sbuf", [128, 5, L_], bf),
+    "XO": ("sbuf", [128, 4, 768], f32), "XL": ("sbuf", [128, 3, 768], f32), "YO": ("sbuf", [128, 768], f32),
+    "X0": ("psum", [128, 512], f32), "X1": ("psum", [128, 512], f32),
+    "Y0": ("psum", [128, 512], f32), "Y1": ("psum", [128, 512], f32),
+    "Z0": ("psum", [128, 32, 16], f32), "Z1": ("psum", [128, 32, 16], f32),
+    "Z2": ("psum", [128, 2, 32, 2, 2, 2], f32), "Z3": ("psum", [128, 512], f32),
+}
+POOL = {"v": 30, "s": 28, "t": 30, "g": 28, "d": 20}
+SEMAPHORES = ["%s%d" % (e, i) for e in POOL for i in range(POOL[e])] + ["m1", "m2", "m3", "m4", "n1", "n2", "n3", "n4", "x1", "x2", "x3", "gone"]
+EARLY = 2
+AHEAD = 3
+PRE = 3
+FILLC = 2
+OWN = 1
+
+
+def emit(g, T, tasks):
+    Q = {"v": g.vector, "s": g.scalar, "t": g.tensor, "g": g, "y": g.sync}
+    lastw, readers, bank = {}, {}, {}
+    known = {e: 0 for e in Q}
+    for n, k in enumerate(tasks):
+        e = k["e"]
+        dep = set()
+        for r in k["r"]:
+            if r in lastw: dep.add(lastw[r])
+        for w in k["w"]:
+            if w in lastw: dep.add(lastw[w])
+            dep.update(readers.get(w, ()))
+        for b in k["b"]:
+            dep.update(m for m in bank.get(b, ()) if tasks[m]["e"] != e)
+        k["wait"] = []
+        if e != "x":
+            for m in sorted(dep, reverse=True):
+                if not known[e] >> m & 1:
+                    k["wait"].append(m); tasks[m]["sig"] = True
+                    known[e] |= tasks[m]["before"] | 1 << m
+            k["before"] = known[e]
+        else:
+            k["before"] = 0
+        for r in k["r"]: readers.setdefault(r, []).append(n)
+        for w in k["w"]:
+            lastw[w] = n; readers[w] = []
+        for b in k["b"]:
+            bank[b] = [m for m in bank.get(b, ()) if tasks[m]["e"] == e] + [n]
+    turn = {e: 0 for e in POOL}
+    count, user = {}, {}
+    for n, k in enumerate(tasks):
+        if k["e"] == "x": continue
+        q = Q[k["e"]]
+        for m in k["wait"]:
+            q.wait_ge(T.sem[tasks[m]["sem"]], tasks[m]["val"])
+        sig = k.get("sig") and k["f"]
+        if sig:
+            p = "d" if k["dma"] else k["e"]
+            for _ in range(POOL[p]):
+                k["sem"] = "%s%d" % (p, turn[p] % POOL[p]); turn[p] += 1
+                if k["sem"] not in user or k["before"] >> user[k["sem"]] & 1: break
+            else:
+                raise ValueError("no free semaphore")
+            user[k["sem"]] = n
+        for f in k["f"]:
+            ins = f(q)
+            if sig:
+                inc = 16 if k["dma"] else 1
+                ins.then_inc(T.sem[k["sem"]], inc)
+                count[k["sem"]] = count.get(k["sem"], 0) + inc
+        if sig: k["val"] = count[k["sem"]]
+
+
+def rank_program(g, core, T, topo):
+    rank = T.rank_of(core)
+    if rank is None:
+        return
+    N = len(T.cores)
+    tasks = []
+
+    def task(e, f, r=(), w=(), b=(), dma=False):
+        tasks.append({"e": e, "f": f if isinstance(f, list) else [f], "r": list(r), "w": list(w), "b": list(b), "dma": dma})
+
+    def arrival(sem, val, w):
+        tasks.append({"e": "x", "f": [], "r": [], "w": list(w), "b": [], "dma": False, "sem": sem, "val": val})
+
+    def ms(ap, c): return lambda q: q.memset(ap, c)
+    def cp(o, i): return lambda q: q.tensor_copy(o, i)
+    def tt(o, a, b, op): return lambda q: q.tensor_tensor(o, a, b, op)
+    def ts(o, a, s1, op0, s2=None, op1=None):
+        if op1 is None: return lambda q: q.tensor_scalar(o, a, s1, None, op0)
+        return lambda q: q.tensor_scalar(o, a, s1, s2, op0, op1)
+    def scan(o, a, b, op0, op1): return lambda q: q.tensor_tensor_scan(o, a, b, 0.0, op0, op1)
+    def act(o, i, fn=F.Identity, bias=0.0, scale=1.0): return lambda q: q.activation(o, i, fn, bias=bias, scale=scale)
+    def mm(o, l, r, st=True, sp=True): return lambda q: q.matmul(o, l, r, st, sp)
+    def tr(o, i, idn): return lambda q: q.transpose(o, i, idn)
+    def dma(o, i): return lambda q: q.dma_start(o, i)
+    def paint(name, ap, pat, val, base, cm):
+        task("g", lambda q: q.affine_select(ap, ap, pat, A.not_equal, val, base, cm), r=[name], w=[name])
+    def io(ap, n, val): return lambda q: q.iota(ap, [[0, n]], val, 0, allow_small_or_imprecise_dtypes=True)
+    def fill(names, ap, n, val): task("g", io(ap, n, val), w=names)
+    def ch(j): return slice(512 * j, 512 * j + 512)
+    def oc(j): return slice(32 * j, 32 * j + 32)
+    XB, YB = [T.X0, T.X1], [T.Y0, T.Y1]
+
+    for a, b in ((0, 1), (1, 2), (2, 4), (4, 6), (6, 8)):
+        task("y", dma(T.ar[:, 512 * a:512 * b], T.arcs[:, 512 * a:512 * b]), w=["ar%d" % j for j in range(a, b)], dma=True)
+    task("s", [dma(T.std[:, :, :, kk, :], T.st0[:, (7 - kk) * 24:(8 - kk) * 24]) for kk in range(8)], w=["std"], dma=True)
+    task("s", [dma(T.rsi[kk:64:8, :], T.rs0[:, (7 - kk) * L_:(8 - kk) * L_]) for kk in range(8)], w=["rsi"], dma=True)
+    task("s", dma(T.acs[:, :], T.ac[:, :]), w=["acs"], dma=True)
+    task("y", [dma(T.sti[:, q2, :], T.std[:, q2, :, :, :]) for q2 in range(8)], r=["std"], w=["sti"], dma=True)
+
+    task("v", [ms(T.If[:], 0.0), ms(T.sD[0:64, :, :], 0.0), ms(T.sD[64:66, 1:8, :], 0.0), ms(T.sD[64:66, 0, :], 512.0)], w=["If", "sD"])
+    task("v", [ms(T.Ib[:], 0.0), ms(T.sC[:], 0.0), ms(T.sL[0:64, :, :], 0.0), ms(T.sP[0:64, :], 0.0), ms(T.sL[64:66, :, 1:17], -64.5),
+               ms(T.sL[64:66, :, 0:1], 500.0), ms(T.sP[64:66, :], 39.0 / 64), ms(T.I17[:], 0.0)], w=["Ib", "sL", "sP", "sC", "I17"])
+    task("v", [ms(T[n][:], 0.0) for n in ("EE", "Db")] + [ms(T.ri[64:128, 0, :], 1.0), ms(T.dup[:, :, 0:1], 0.0), ms(T.nf[:, 0:2], 0.0)],
+         w=["EE", "Db", "ri0c", "dup", "nf"])
+
+    paint("If", T.If[:], [[-1, 128]], 1.0, 0, 1)
+    paint("sD", T.sD[0:64, 1:8, :], [[-1, 7], [-8, 8], [0, 16]], 1.0, 0, 1)
+    paint("sD", T.sD[0:64, 1:8, :], [[-1, 7], [-8, 8], [0, 16]], -1.0, -1, 1)
+    paint("Ib", T.Ib[:], [[-1, 128]], 1.0, 0, 1)
+    paint("I17", T.I17[:, :, 1:17], [[-16, 8], [-1, 16]], 1.0, 0, 1)
+    paint("sL", T.sL[0:64, :, 1:17], [[-8, 8], [0, 16]], 1.0, -7, 1)
+    task("g", [io(T.p17[:], 408, 0), io(T.pS[:], 816, 0), io(T.d3[:, 0:L_:2], 192, 1), io(T.d3[:, 1:L_:2], 192, 0),
+               io(T.p3[:], L_, 1), io(T.d4[:], 392, 0), io(T.p4[:], 392, 1)], w=["p17", "pS", "d3", "p3", "d4", "p4"])
+    task("g", [io(T.p17[:, 0:408:17], 24, 1000), io(T.p3[:, 0:L_:16], 24, 0), io(T.p4[:, 0:392:8], 49, 0)]
+         + [io(T.pS[:, 0, 1 + a:408:17], 24, 1) for a in range(1, 16, 2)]
+         + [io(T.pS[:, 1, 1 + a:408:17], 24, 4096 if a % 2 else -4096) for a in range(16)], w=["p17", "pS", "p3", "p4"])
+    task("g", lambda q: q.iota(T.kb[:, 0:8, :], [[0, 8], [1, 16]], 0, 0, allow_small_or_imprecise_dtypes=True), w=["kb"])
+    paint("sP", T.sP[0:64, 16:128], [[-8, 7], [0, 2], [1, 8]], 1.0 / 128, -7, 1)
+    paint("sP", T.sP[0:64, 0:16], [[0, 2], [1, 8]], 1.0 / 128, -63, 1)
+    paint("EE", T.EE[:], [[-1, 128], [0, 8]], 1.0, 0, 1)
+    paint("Db", T.Db[:], [[-1, 2], [-2, 64]], 1.0, 0, 1)
+    for j in range(8):
+        paint("sC", T.sC[:, 2:16], [[-16, 7], [-1, 2]], 1.0, -2 * j, 1)
+        paint("sC", T.sC[:, 0:2], [[-1, 2]], 1.0, -112 - 2 * j, 1)
+    for n, k in (("Df", 128), ("In", 128), ("zd", 392), ("p8", 192), ("PM", 512)): fill([n], T[n][:], k, 0)
+    fill(["p8"], T.p8[:, 7:192:8], 24, 1024)
+    fill(["ro%d" % t for t in range(V_)], T.ro[:], V_ * L_, 1)
+    paint("Df", T.Df[:], [[-1, 2], [-2, 64]], 8388608.0, 0, 1)
+    paint("In", T.In[:], [[-1, 128]], 64.0, 0, 1)
+    for t in range(4):
+        paint("PM", T.PM[:, t, :], [[-1, 128]], 1.0, 16 * (4 - t), 1)
+        paint("PM", T.PM[:, t, :], [[-1, 128]], 1.0, 16 * (4 - t) - 128, 1)
+
+    PB = [("X0", T.X0), ("X1", T.X1), ("Y0", T.Y0), ("Y1", T.Y1)]
+
+    def bits(j):
+        task("v", [ts(T.a0[:, j % 2, :], T.ar[:, ch(j)], 32767, A.bitwise_and), ts(T.a1[:, j % 2, :], T.ar[:, ch(j)], 15, A.logical_shift_right)],
+             r=["ar%d" % j], w=["a%d" % (j % 2)])
+    bits(0)
+    for j in range(8):
+        n, P = PB[j % 4]
+        task("v", [cp(P[:], T.a1[:, j % 2, :]), cp(T.U0[:, ch(j)], T.a0[:, j % 2, :])], r=["a%d" % (j % 2)], w=[n, "U0%d" % j], b=[n])
+        if j < 7: bits(j + 1)
+        task("s", act(T.TT[:, ch(j)], T.U0[:, ch(j)]), r=["U0%d" % j], w=["TT%d" % j])
+        task("v", tt(T.MM[:, ch(j)], P[:], T.U0[:, ch(j)], A.min), r=[n, "U0%d" % j], w=["MM%d" % j], b=[n])
+        task("s", [act(T.U1[:, ch(j)], P[:]), act(T.TT[:, ch(8 + j)], P[:])], r=[n], w=["U1%d" % j, "TU%d" % j], b=[n])
+        if j % 2:
+            c = slice(512 * j - 512, 512 * j + 512)
+            task("y", [dma(T.TT[0:128:2, W_ + c.start:W_ + c.stop], T.U0[1:128:2, c]), dma(T.TT[1:128:2, c], T.U1[0:128:2, c])],
+                 r=["U0%d" % j, "U1%d" % j, "U0%d" % (j - 1), "U1%d" % (j - 1)],
+                 w=["TT%d" % j, "TT%d" % (j - 1), "TU%d" % j, "TU%d" % (j - 1)], dma=True)
+        if j == 1:
+            task("t", [tr(T.Z0[:, 8 * c:8 * c + 8, :], T.acs[:, 128 * c:128 * c + 128], T.If[:]) for c in range(3)],
+                 r=["acs", "If"], w=["Z0"], b=["Z0"])
+        if j == 3:
+            task("s", [act(T.acT[:, 1 + a:408:17], T.Z0[:, 0:24, a]) for a in range(16)] + [act(T.acT[:, 0:408:17], T.Z0[:, 0:24, 0], scale=0.0)],
+                 r=["Z0"], w=["acT"], b=["Z0"])
+        if j == 5:
+            task("v", [cp(T.xi[:, 0, q2:192:8], T.sti[:, q2, :]) for q2 in range(8)] + [cp(T.ri[0:64, 0, :], T.rsi[0:64, :]),
+                      ts(T.sP[64:65, :], T.kb[64:65, 0:8, :], 1.0 / 2048, A.mult)], r=["sti", "rsi", "ri0c", "kb"], w=["xi0", "ri0", "sP"])
+    task("y", [dma(T.pr[16:128, :], T.pay[0:112, :]), dma(T.pr[0:16, :], T.pay[112:128, :])], w=["pr"], dma=True)
+    MMs, TTs = ["MM%d" % j for j in range(8)], ["TT%d" % j for j in range(8)]
+
+    def spread(bank, n, R, t, name, j):
+        task("t", [mm(bank[:, kk:512:8], T.sD[0:66, kk, :], R[0:66, t, 64 * j:64 * j + 64]) for kk in range(8)],
+             r=["sD", name], w=[n], b=[n])
+
+    def prep(t, j):
+        n = "Y%d" % (j % 2)
+        spread(YB[j % 2], n, T.ro, t, "ro%d" % t, j)
+        task("s", act(T.GP[:, ch(j)], T.pr[:, 0:W_].indirect(T.xo[:, t, oc(j)])), r=["pr", "xo%d" % t], w=["GP%d" % j])
+        task("s", act(T.WW[:, ch(j)], YB[j % 2][:], F.Exp, scale=-0.125), r=[n], w=["WW%d" % j], b=[n])
+
+    def horner(j):
+        task("v", [scan(T.U0[:, ch(j)], T.WW[:, ch(j)], T.GP[:, ch(j)], A.mult, A.add),
+                   scan(T.U1[:, ch(j)], T.WW[:, ch(j)], T.GP[:, ch(j)], A.mult, A.max)],
+             r=["WW%d" % j, "GP%d" % j], w=["SO%d" % j, "U0%d" % j, "U1%d" % j])
+    SOs = ["SO%d" % j for j in range(6)]
+    sent = [0]
+
+    def send(out, src, sem, to, r):
+        dst = T.cores[to]
+        rid, pid, _ = topo.addr(dst)
+        task("g", lambda q: q.remote_dma(out, src, T.sem[sem], T.sem.gone, pid, rid, topo.mask(core, dst)), r=r)
+        sent[0] += len(topo.engines(core, dst))
+
+    def compact(t, a, b):
+        task("s", [act(T.XO[:, t, h * L_ + 64 * a:h * L_ + 64 * b], (T.U0, T.U1)[h][:, 512 * a + 7:512 * b:8]) for h in range(2)],
+             r=SOs[a:b], w=["XO%d%d" % (t, a)])
+
+    def hand_back(t):
+        compact(t, EARLY, 6)
+        if t: send(T.XL[:, t - 1, :], T.XO[:, t, :], "x%d" % t, (rank - t) % N, ["XO%d0" % t, "XO%d%d" % (t, EARLY)])
+
+    def gather_parts(t, first, last):
+        if t: arrival("x%d" % t, len(topo.engines(T.cores[(rank + t) % N], core)), ["XL%d" % t])
+        so = (T.XO, 0) if t == 0 else (T.XL, t - 1)
+        task("t", [mm(XB[h][:, 0:L_], T.PM[:, t, :], so[0][:, so[1], h * L_:h * L_ + L_], first, last) for h in range(2)],
+             r=["PM"] + (["XO00", "XO0%d" % EARLY] if t == 0 else ["XL%d" % t]), w=["X0", "X1"], b=["X0", "X1"])
+
+    ALL, REV = slice(None), slice(None, None, -1)
+
+    def side(mem, pp, dims, fix, rev=()):
+        ix = [0] * (3 - len(dims)) + [fix[d] if d in fix else REV if d in rev else ALL for d in dims]
+        return (T.Z2 if mem == 0 else T.SB)[(ALL, pp, slice(0, 24)) + tuple(ix)]
+
+    def layer(pp, allbits, s, flip, nxt, only_min=False):
+        din = [d for d in allbits if d != s]
+        dout = [d for d in allbits if d != nxt and not (only_min and d == s)]
+        low = [d for d in din if d < s] if flip else []
+        f = []
+        for mx in range(1 if only_min else 2):
+            for v in range(2):
+                o = 1 - v if nxt in low else v
+                a = side(0, pp, din, {nxt: o if mx else v}, low if mx else ())
+                b = side(1, pp, din, {nxt: v if mx else o}, () if mx else low)
+                f.append(tt(side(v, 1 - pp, dout, {s: mx}), a, b, A.max if mx else A.min))
+        task("v", f, r=["so%d" % pp], w=["so%d" % (1 - pp)], b=["Z2"])
+
+    B4, B3 = [3, 2, 1, 0], [2, 1, 0]
+
+    def network(steps):
+        pp = 0
+        for n in range(len(steps) - 1):
+            layer(pp, B4, steps[n][0], steps[n][1], steps[n + 1][0]); pp = 1 - pp
+        return pp
+    EIGHT = [(0, 0), (1, 1), (0, 0), (2, 1), (1, 0), (0, 0), (3, 1)]
+    UP = 128.5 + 2.0 ** -13
+
+    def visit(t):
+        xi, ri = "xi%d" % t, "ri%d" % t
+        late = list(range(EARLY, 6)) if t >= 2 else []
+        for j in late[:AHEAD]: horner(j)
+        late = late[AHEAD:]
+        if t:
+            n = len(topo.engines(T.cores[(rank - 1) % N], core))
+            arrival("m%d" % t, n, [xi]); arrival("n%d" % t, n, [ri])
+        for j in range(6 - OWN, 6):
+            task("v", ts(T.G[:, ch(j)], T.MM[:, 0:W_].indirect(T.xi[:, t, oc(j)]), 2.0 ** -12, A.mult, UP, A.add),
+                 r=MMs + [xi], w=["G%d" % j])
+        for i in range(4): spread(PB[i][1], PB[i][0], T.ri, t, ri, i)
+        for j in range(6):
+            n, P = PB[j % 4]
+            if j < 6 - OWN:
+                task("s", act(T.G[:, ch(j)], T.MM[:, 0:W_].indirect(T.xi[:, t, oc(j)]), bias=UP, scale=2.0 ** -12),
+                     r=MMs + [xi], w=["G%d" % j])
+            if j == 1: task("v", cp(T.stf[:], T.xi[:, t, :]), r=[xi], w=["stf"])
+            if j == 2 and late: horner(late.pop(0))
+            task("v", scan(T.GS[:, ch(j)], P[:], T.G[:, ch(j)], A.add, A.min), r=[n, "G%d" % j], w=["GS%d" % j], b=[n])
+            if j < 2: spread(P, n, T.ri, t, ri, j + 4)
+            if j == 4 and t >= 1:
+                for i in range(EARLY): prep(t - 1, i)
+            if j % 2:
+                c = j // 2
+                task("t", [mm(T.Z3[:, 136 * c:136 * c + 136], T.ri[0:66, t, 128 * c:128 * c + 128], T.sL[0:66, :, :], True, False),
+                           mm(T.Z3[:, 136 * c:136 * c + 136], T.GS[:, 1024 * c + 7:1024 * c + 1024:8], T.I17[:], False, True)],
+                     r=[ri, "sL", "I17", "GS%d" % j, "GS%d" % (j - 1)], w=["Z3%d" % c] + (["Z3"] if c == 0 else []), b=["Z3"])
+        for j in late: horner(j)
+        task("t", [mm(T.Z1[:, 8 * c:8 * c + 8, :], T.ri[0:66, t, 128 * c:128 * c + 128], T.sP[0:66, :]) for c in range(3)],
+             r=[ri, "sP"], w=["Z1"], b=["Z1"])
+        task("v", tt(T.sc[:], T.Z3[:, 0:408], T.acT[:], A.add), r=["Z3", "Z30", "Z31", "Z32", "acT"], w=["sc"], b=["Z3"])
+        task("t", mm(T.Z3[:, 0:192], T.If[:], T.stf[:], True, False), r=["If", "stf"], w=["Z3"], b=["Z3"])
+        task("v", scan(T.X0[:, 0:408], T.p17[:], T.sc[:], A.add, A.min), r=["sc", "p17"], w=["X0"], b=["X0"])
+        task("v", tt(T.nf[:, 1:408], T.X0[:, 0:407], T.sc[:, 1:408], A.is_le), r=["sc", "X0"], w=["nf"], b=["X0"])
+        task("v", [scan(T.s2[:, 1, :], T.nf[:], T.pS[:, 1, :], A.mult, A.add), scan(T.s2[:, 0, :], T.nf[:], T.pS[:, 0, :], A.mult, A.add)],
+             r=["nf", "pS"], w=["s2"])
+        task("v", [cp(T.d4[:, 8:392:16], T.s2[:, 1, 16:408:17]), ts(T.d3[:, 0:L_:16], T.s2[:, 0, 16:408:17], 1.0, A.add)], r=["s2"], w=["d3", "d4"])
+        task("v", scan(T.zb[:], T.p4[:], T.d4[:], A.mult, A.add), r=["d4", "p4"], w=["zb"])
+        task("v", scan(T.H[:], T.p3[:], T.d3[:], A.mult, A.add), r=["d3", "p3"], w=["H"])
+        task("v", ts(T.H[:], T.H[:], 9.0, A.is_equal), w=["H"])
+
+        def mask(j):
+            n = "X%d" % (j % 2)
+            task("t", mm(XB[j % 2][:], T.H[:, 128 * (j // 2):128 * (j // 2) + 128], T.EE[:, ch(j % 2)]), r=["H", "EE"], w=[n], b=[n])
+        task("t", [mm(T.Z3[:, 64 * c:64 * c + 64], T.zb[:, 128 * c + 8 - 8 * b:128 * c + 136 - 8 * b], T.Db[:, b, :], False, c == 2 and b == 1)
+                   for c in range(3) for b in range(2)], r=["zb", "Db"], w=["Z3"], b=["Z3"])
+        mask(0); mask(1)
+        task("v", cp(T.ix2[:], T.Z3[:, 0:192]), r=["Z3"], w=["ix2"], b=["Z3"])
+        early = list(range(EARLY)) if t >= 1 else []
+        for j in range(6 - OWN, 6):
+            task("v", cp(T.GA[:, ch(j)], T.TT[:, 0:2 * W_].indirect(T.ix2[:, oc(j)])), r=TTs + ["ix2"], w=["GA%d" % j])
+        for j in range(6):
+            n = "X%d" % (j % 2)
+            if j < 6 - OWN:
+                task("s", act(T.GA[:, ch(j)], T.TT[:, 0:2 * W_].indirect(T.ix2[:, oc(j)])), r=TTs + ["ix2"], w=["GA%d" % j])
+            if early and j == FILLC: horner(early.pop(0))
+            task("v", tt(T.GA[:, ch(j)], XB[j % 2][:], T.GA[:, ch(j)], A.mult), r=[n], w=["GA%d" % j], b=[n])
+            if j < 4: mask(j + 2)
+            if j % 2:
+                c = j // 2
+                task("t", [mm(T.Z0[:, 8 * c:8 * c + 8, 7 - kk:16:8] if c < 2 else T.Z3[:, 7 - kk:128:8],
+                              T.GA[:, 1024 * c + kk:1024 * c + 1024:8], T.sC[:]) for kk in range(8)],
+                     r=["sC", "GA%d" % j, "GA%d" % (j - 1)], w=[["Z00", "Z0"], ["Z01"], ["Z3"]][c], b=["Z0" if c < 2 else "Z3"])
+        task("s", act(T.kb[:], T.Z0[:, 0:16, :], bias=UP, scale=2.0 ** -12), r=["Z0", "Z00", "Z01"], w=["kb"], b=["Z0"])
+        task("s", act(T.kb[:], T.kb[:], bias=-129.0), w=["kb"])
+        task("s", act(T.k1[:, 0:16, :], T.kb[:], scale=4096.0 - 2.0 ** -7), r=["kb"], w=["k1", "k1Z0"])
+        for j in early: horner(j)
+        if t >= 2: hand_back(t - 2)
+        if t >= 1:
+            compact(t - 1, 0, EARLY)
+            for j in range(EARLY, EARLY + PRE): prep(t - 1, j)
+        if t == V_ - 1:
+            for s in range(3): gather_parts(s, s == 0, False)
+        Z0, Z1, zz = T.Z0[:, 0:24, :], T.Z1[:, 0:24, :], ["Z0", "Z00", "Z01", "Z02"]
+        big = 1.5 * 2.0 ** 35
+        k3, P3 = T.k1[:, 16:24, :], T.Z3[:, 0:128]
+        task("v", ts(k3, P3, -2047.5, A.add, big, A.add), r=["Z3"], w=["k1Z3"], b=["Z3"])
+        task("v", ts(k3, k3, big, A.subtract, 1.0 - 2.0 ** -19, A.mult), w=["k1Z3"])
+        task("v", tt(k3, P3, k3, A.subtract), r=["Z3"], w=["k1Z3"], b=["Z3"])
+        task("v", tt(T.k1[:, 0:16, :], T.Z0[:, 0:16, :], T.k1[:, 0:16, :], A.subtract), r=zz, w=["k1Z0"], b=["Z0"])
+        task("v", [tt(side(v, 0, [3, 2, 1], {}), T.Z1[:, 0:24, v:16:2], T.k1[:, :, v:16:2], A.add) for v in range(2)],
+             r=["k1Z0", "k1Z3", "Z1"], w=["so0"], b=["Z1", "Z2"])
+        pp = network(EIGHT + [(2, 0), (1, 0), (0, 0)])
+        task("v", [tt(T.k1[:, :, mx:16:2], side(0, pp, [3, 2, 1], {}), side(1, pp, [3, 2, 1], {}), A.max if mx else A.min) for mx in range(2)],
+             r=["so%d" % pp], w=["k1", "k1Z0", "k1Z3"], b=["Z2"])
+        task("v", ts(Z0, T.k1[:], 8388608.0, A.add, 8388607.5, A.subtract), r=["k1"], w=zz, b=["Z0"])
+        task("s", act(T.k2[:], T.k1[:], bias=8388608.0), r=["k1"], w=["k2"])
+        task("s", act(T.k2[:], T.k2[:], bias=-4096.0 * 2.0 ** -23, scale=2.0 ** -23), w=["k2"])
+        task("v", [tt(Z1, T.k1[:], Z0, A.subtract), tt(T.dup[:, :, 1:16], T.k1[:, :, 1:16], T.Z0[:, 0:24, 0:15], A.is_lt)],
+             r=zz + ["k1"], w=["Z1", "dup"], b=["Z0", "Z1"])
+        task("v", tt(Z0, Z1, T.k2[:], A.add), r=["Z1", "k2"], w=zz, b=["Z0", "Z1"])
+        task("v", [tt(side(v, 0, [3, 2, 1], {}), T.Z0[:, 0:24, v:16:2], T.dup[:, :, v:16:2], A.max) for v in range(2)],
+             r=zz + ["dup"], w=["so0"], b=["Z0", "Z2"])
+        if t >= 1:
+            for j in range(EARLY + PRE, 6): prep(t - 1, j)
+        pp = network(EIGHT)
+        layer(pp, B4, 3, 1, 2, only_min=True); pp = 1 - pp
+        layer(pp, B3, 2, 0, 1); pp = 1 - pp
+        layer(pp, B3, 1, 0, 0); pp = 1 - pp
+        task("v", [tt(T.KS[:, :, 1 - mx:8:2], side(0, pp, [2, 1], {}, [2, 1]), side(1, pp, [2, 1], {}, [2, 1]), A.max if mx else A.min) for mx in range(2)],
+             r=["so%d" % pp], w=["KS"], b=["Z2"])
+        task("v", ts(T.yy[:], T.KS[:], 2047.5 * 2.0 ** -23, A.add, 4096.0, A.add), r=["KS"], w=["yy"])
+        task("v", [ts(T.Z0[:, 0:24, 0:8], T.yy[:], 4096.0, A.subtract),
+                   ts(T.cb[:], T.yy[:], 4096.0 - (115 - 0.46875) / 128, A.subtract, 128.0, A.mult)], r=["yy"], w=zz + ["cb"], b=["Z0"])
+        task("v", tt(T.zd[:, 1:49:2, :], T.KS[:], T.Z0[:, 0:24, 0:8], A.subtract), r=zz + ["KS"], w=["zd"], b=["Z0"])
+        task("t", [mm(T.Z3[:, 64 * c:64 * c + 64], T.zd[:, 16 * c + 1 - b:16 * c + 17 - b, :], T.Df[:, b, :], b == 0, b == 1)
+                   for c in range(3) for b in range(2)], r=["zd", "Df"], w=["Z3"], b=["Z3"])
+        task("v", [scan(T.Y0[:, 191::-1], T.p8[:, ::-1], T.cb[:, ::-1], A.add, A.min), ts(T.ng[:], T.cb[:], 242.5, A.is_lt)],
+             r=["cb", "p8"], w=["Y0", "ng"], b=["Y0"])
+        task("v", tt(T.Y0[:, 192:384], T.Y0[:, 0:192], T.cb[:], A.subtract), r=["cb"], w=["Y0"], b=["Y0"])
+        task("v", tt(T.tn[:], T.Y0[:, 192:384], T.ng[:], A.mult), r=["ng", "Y0"], w=["tn"], b=["Y0"])
+        task("v", ts(T.xo[:, t, :], T.Z3[:, 0:192], 4095.0, A.add), r=["Z3"], w=["xo%d" % t], b=["Z3"])
+        if t < V_ - 1: send(T.xi[:, t + 1, :], T.xo[:, t, :], "m%d" % (t + 1), (rank + 1) % N, ["xo%d" % t])
+        f = []
+        for c in range(3):
+            f += [mm(T.Z1[0:64, 8 * c:8 * c + 8, :], T.ng[:, 64 * c:64 * c + 64], T.In[:], True, False),
+                  mm(T.Z1[0:64, 8 * c:8 * c + 8, :], T.tn[:, 64 * c:64 * c + 64], T.Ib[:], False, True)]
+        task("t", f, r=["ng", "tn", "In", "Ib"], w=["Z1"], b=["Z1"])
+        task("s", act(T.ro[0:64, t, :], T.Z1[0:64, 0:24, :], bias=64.0, scale=-1.0), r=["Z1"], w=["ro%d" % t], b=["Z1"])
+        if t < V_ - 1: send(T.ri[:, t + 1, :], T.ro[:, t, :], "n%d" % (t + 1), (rank + 1) % N, ["ro%d" % t])
+
+    for t in range(V_): visit(t)
+
+    t = V_ - 1
+    for j in range(EARLY): prep(t, j)
+    for j in range(EARLY, 6): horner(j)
+    prep(t, EARLY)
+    hand_back(t - 1)
+    for j in range(6):
+        if j > EARLY: prep(t, j)
+        horner(j)
+    gather_parts(t - 1, False, True)
+    task("v", tt(T.YO[:, 0:L_], T.X0[:, 0:L_], T.U0[:, 7:3072:8], A.add), r=SOs + ["X0"], w=["YO0"], b=["X0"])
+    task("v", tt(T.YO[:, L_:768], T.X1[:, 0:L_], T.U1[:, 7:3072:8], A.add), r=SOs + ["X1"], w=["YO1"], b=["X1"])
+    cut = 16 * (V_ % 8)
+    task("y", [dma(T.ys[0:128 - cut, :], T.YO[cut:128, 0:L_]), dma(T.ys[128 - cut:128, :], T.YO[0:cut, 0:L_])], r=["YO0"], w=["ys"], dma=True)
+    task("s", [dma(T.ym[0:128 - cut, :], T.YO[cut:128, L_:768]), dma(T.ym[128 - cut:128, :], T.YO[0:cut, L_:768])], r=["YO1"], w=["ym"], dma=True)
+    task("y", [], r=["ys", "ym"])
+    emit(g, T, tasks)
+    g.wait_ge(T.sem.gone, sent[0])

@@ -1,74 +1,98 @@
-from concourse.mybir import AluOpType, ActivationFunctionType
+from concourse.mybir import AluOpType, ActivationFunctionType, AxisListType
 
 A = AluOpType
 F = ActivationFunctionType
 V_, L_, W_ = 5, 384, 4096
-f32, bf, i32, u16 = "float32", "bfloat16", "int32", "uint16"
+f32, bf, f16, i32, u16 = "float32", "bfloat16", "float16", "int32", "uint16"
+BATCHES = ((0, 2), (2, 3))
 SCRATCH = {
-    "ar": ("sbuf", [128, W_], i32), "a0": ("sbuf", [128, 2, 512], i32), "a1": ("sbuf", [128, 2, 512], i32),
-    "U0": ("sbuf", [128, W_], f32), "U1": ("sbuf", [128, W_], f32), "TT": ("sbuf", [128, 2 * W_], f32),
-    "MM": ("sbuf", [128, W_], f32), "pr": ("sbuf", [128, W_], bf),
-    "acs": ("sbuf", [128, L_], f32), "acT": ("sbuf", [128, 408], f32),
+    "ar": ("sbuf", [128, W_], i32), "a0": ("sbuf", [128, W_], i32), "a1": ("sbuf", [128, 2, 512], i32),
+    "U1": ("sbuf", [128, W_], f32), "TT": ("sbuf", [128, 2 * W_], f32), "MM": ("sbuf", [128, W_], f32), "pr": ("sbuf", [128, W_], bf),
+    "acs": ("sbuf", [128, L_], f32), "acT": ("sbuf", [128, L_], f32),
     "rsi": ("sbuf", [128, L_], i32), "sti": ("sbuf", [128, 8, 24], i32), "std": ("dram", [8, 8, 2, 8, 24], i32),
     "G": ("sbuf", [128, 3072], bf), "GS": ("sbuf", [128, 3072], bf), "GA": ("sbuf", [128, 3072], f32),
-    "GP": ("sbuf", [128, 3072], bf), "WW": ("sbuf", [128, 3072], f32),
-    "sc": ("sbuf", [128, 408], f32), "nf": ("sbuf", [128, 408], bf), "s2": ("sbuf", [128, 2, 408], bf),
-    "d3": ("sbuf", [128, L_], bf), "p3": ("sbuf", [128, L_], bf), "d4": ("sbuf", [128, 392], bf), "p4": ("sbuf", [128, 392], bf),
-    "H": ("sbuf", [128, L_], bf), "zb": ("sbuf", [128, 392], bf), "zd": ("sbuf", [128, 49, 8], f32), "I17": ("sbuf", [128, 8, 17], bf),
-    "stf": ("sbuf", [128, 192], f32), "ix2": ("sbuf", [128, 192], u16),
-    "k1": ("sbuf", [128, 24, 16], f32), "k2": ("sbuf", [128, 24, 16], f32), "dup": ("sbuf", [128, 24, 16], f32),
-    "SB": ("sbuf", [128, 2, 24, 2, 2, 2], f32), "KS": ("sbuf", [128, 24, 8], f32), "yy": ("sbuf", [128, 24, 8], f32),
-    "kb": ("sbuf", [128, 16, 16], bf), "cb": ("sbuf", [128, 192], bf), "ng": ("sbuf", [128, 192], bf), "tn": ("sbuf", [128, 192], bf),
-    "Ib": ("sbuf", [128, 128], bf), "In": ("sbuf", [128, 128], bf), "If": ("sbuf", [128, 128], f32),
-    "sD": ("sbuf", [128, 8, 128], bf), "sL": ("sbuf", [128, 8, 17], bf), "sP": ("sbuf", [128, 128], bf),
-    "sC": ("sbuf", [128, 16], f32), "EE": ("sbuf", [128, 1024], bf),
-    "Db": ("sbuf", [128, 2, 64], bf), "Df": ("sbuf", [128, 2, 64], f32), "PM": ("sbuf", [128, 4, 128], f32),
-    "p17": ("sbuf", [128, 408], f32), "pS": ("sbuf", [128, 2, 408], bf), "p8": ("sbuf", [128, 192], bf),
-    "xi": ("sbuf", [128, 5, 192], u16), "xo": ("sbuf", [128, 5, 192], u16),
-    "ri": ("sbuf", [128, 5, L_], bf), "ro": ("sbuf", [128, 5, L_], bf),
+    "GP": ("sbuf", [128, 3072], bf), "WW": ("sbuf", [128, 3072], f32), "S1": ("sbuf", [128, 3072], f32),
+    "sc": ("sbuf", [128, L_], f32), "nf": ("sbuf", [128, L_], bf), "UU": ("sbuf", [128, L_], bf), "UT": ("sbuf", [128, L_], bf),
+    "MH": ("sbuf", [128, L_], bf), "sth": ("sbuf", [128, 192], f16), "ix2": ("sbuf", [128, 192], u16), "kb": ("sbuf", [128, L_], bf),
+    "k1": ("sbuf", [128, L_], f32), "DD": ("sbuf", [128, 24, 17], f16), "pen": ("sbuf", [128, L_], f32),
+    "SB": ("sbuf", [128, 24, 2, 2, 2, 2], f32), "KS": ("sbuf", [128, 24, 8], f32), "cb": ("sbuf", [128, 24, 8], bf), "zd": ("sbuf", [128, 49, 8], f16),
+    "Z": ("sbuf", [128, 1024], bf), "Zf": ("sbuf", [128, 256], f32), "I2": ("sbuf", [128, 256], f32), "If4": ("sbuf", [128, 128], f32),
+    "Ib": ("sbuf", [128, 3, 128], bf), "Ih": ("sbuf", [128, 4, 128], f16), "Db": ("sbuf", [128, 2, 64], bf), "Dh": ("sbuf", [128, 2, 64], f16),
+    "sD": ("sbuf", [128, 8, 128], bf), "sL": ("sbuf", [128, 8, 16], bf), "sP": ("sbuf", [128, 8, 2, 8], bf),
+    "Bk": ("sbuf", [128, 9, 16], bf), "sM": ("sbuf", [128, 8, 16], bf), "sC": ("sbuf", [128, 8, 2], f32), "col": ("sbuf", [128, 8], f32),
+    "Lh": ("sbuf", [128, 8, 16], bf), "Lm": ("sbuf", [128, 8, 8, 2], bf), "Lp": ("sbuf", [128, 2, 8, 2, 8], bf),
+    "p16": ("sbuf", [128, 256], f32), "pU": ("sbuf", [128, 256], bf),
+    "xi": ("sbuf", [128, V_, 192], u16), "xo": ("sbuf", [128, V_, 192], u16),
+    "ri": ("sbuf", [128, V_, L_], bf), "ro": ("sbuf", [128, V_, L_], bf),
     "XO": ("sbuf", [128, 4, 768], f32), "XL": ("sbuf", [128, 3, 768], f32), "YO": ("sbuf", [128, 768], f32),
-    "X0": ("psum", [128, 512], f32), "X1": ("psum", [128, 512], f32),
-    "Y0": ("psum", [128, 512], f32), "Y1": ("psum", [128, 512], f32),
-    "Z0": ("psum", [128, 32, 16], f32), "Z1": ("psum", [128, 32, 16], f32),
-    "Z2": ("psum", [128, 2, 32, 2, 2, 2], f32), "Z3": ("psum", [128, 512], f32),
+    "K0": ("psum", [128, 512], f32), "M0": ("psum", [128, 512], f32), "K1": ("psum", [128, 512], f32), "M1": ("psum", [128, 512], f32),
+    "D0": ("psum", [128, 512], f32), "D1": ("psum", [128, 512], f32), "AC": ("psum", [128, 512], f32),
+    "S": ("psum", [128, 32, 2, 2, 2, 2], f32),
 }
-POOL = {"v": 30, "s": 28, "t": 30, "g": 28, "d": 20}
-SEMAPHORES = ["%s%d" % (e, i) for e in POOL for i in range(POOL[e])] + ["m1", "m2", "m3", "m4", "n1", "n2", "n3", "n4", "x1", "x2", "x3", "gone"]
-EARLY = 2
-AHEAD = 3
-PRE = 3
-FILLC = 2
-OWN = 1
+POOL = {"v": 30, "s": 28, "t": 28, "g": 21, "d": 20}
+SEMAPHORES = (["%s%d" % (e, i) for e in POOL for i in range(POOL[e])] + ["gone"]
+              + ["%s%d%d" % (n, t, b) for n, k in (("m", 5), ("n", 5), ("x", 4)) for t in range(1, k) for b in range(2)])
+LEAD = 0
+SLACK = 300
+STAG = 5
+HOP, LOCAL, REMOTE, GATHER = 110, 2600, 3200, 1.56
+
+
+def needs(tasks):
+    lastw, readers, out = {}, {}, []
+    for n, k in enumerate(tasks):
+        dep = set(lastw[r] for r in k["r"] + k["w"] if r in lastw)
+        for w in k["w"]: dep.update(readers.get(w, ()))
+        out.append(dep)
+        for r in k["r"]: readers.setdefault(r, []).append(n)
+        for w in k["w"]:
+            lastw[w] = n; readers[w] = []
+    return out
+
+
+def arrange(tasks):
+    dep = needs(tasks)
+    for n, k in enumerate(tasks): dep[n].update(k["after"])
+    n_ = len(tasks)
+    way, users = [0] * n_, [[] for _ in tasks]
+    for n in range(n_ - 1, -1, -1):
+        way[n] = tasks[n]["c"] + tasks[n]["lat"] + max([HOP + way[u] for u in users[n]] + [0])
+        for m in dep[n]: users[m].append(n)
+    left, ready, done = [len(d) for d in dep], [0] * n_, []
+    free, bank, open_ = {}, {}, [n for n in range(n_) if not dep[n]]
+    while open_:
+        def start(n):
+            k = tasks[n]
+            return max([ready[n], free.get(k["e"], 0)] + [t + HOP for b in k["b"] for e, t in bank.get(b, {}).items() if e != k["e"]])
+        first, n = min((start(n), n) for n in open_)
+        n = max((m for m in open_ if tasks[m]["e"] == tasks[n]["e"] and start(m) <= first + SLACK), key=lambda m: (way[m] + tasks[m]["lead"], -m))
+        k = tasks[n]
+        end = start(n) + k["c"]
+        if k["e"] != "x": free[k["e"]] = end
+        for b in k["b"]: bank.setdefault(b, {})[k["e"]] = end
+        open_.remove(n); done.append(k)
+        for u in users[n]:
+            ready[u] = max(ready[u], end + k["lat"] + HOP); left[u] -= 1
+            if not left[u]: open_.append(u)
+    return done
 
 
 def emit(g, T, tasks):
     Q = {"v": g.vector, "s": g.scalar, "t": g.tensor, "g": g, "y": g.sync}
-    lastw, readers, bank = {}, {}, {}
-    known = {e: 0 for e in Q}
-    for n, k in enumerate(tasks):
+    bank, known = {}, {e: 0 for e in Q}
+    for n, (k, dep) in enumerate(zip(tasks, needs(tasks))):
         e = k["e"]
-        dep = set()
-        for r in k["r"]:
-            if r in lastw: dep.add(lastw[r])
-        for w in k["w"]:
-            if w in lastw: dep.add(lastw[w])
-            dep.update(readers.get(w, ()))
         for b in k["b"]:
             dep.update(m for m in bank.get(b, ()) if tasks[m]["e"] != e)
-        k["wait"] = []
+            bank[b] = [m for m in bank.get(b, ()) if tasks[m]["e"] == e] + [n]
+        k["wait"], k["before"] = [], 0
         if e != "x":
             for m in sorted(dep, reverse=True):
+                if e == "t" and tasks[m]["e"] == "t": continue
                 if not known[e] >> m & 1:
                     k["wait"].append(m); tasks[m]["sig"] = True
                     known[e] |= tasks[m]["before"] | 1 << m
             k["before"] = known[e]
-        else:
-            k["before"] = 0
-        for r in k["r"]: readers.setdefault(r, []).append(n)
-        for w in k["w"]:
-            lastw[w] = n; readers[w] = []
-        for b in k["b"]:
-            bank[b] = [m for m in bank.get(b, ()) if tasks[m]["e"] == e] + [n]
     turn = {e: 0 for e in POOL}
     count, user = {}, {}
     for n, k in enumerate(tasks):
@@ -83,7 +107,8 @@ def emit(g, T, tasks):
                 k["sem"] = "%s%d" % (p, turn[p] % POOL[p]); turn[p] += 1
                 if k["sem"] not in user or k["before"] >> user[k["sem"]] & 1: break
             else:
-                raise ValueError("no free semaphore")
+                k["sem"] = min((user[s], s) for s in user if s[0] == p)[1]
+                q.wait_ge(T.sem[k["sem"]], count[k["sem"]])
             user[k["sem"]] = n
         for f in k["f"]:
             ins = f(q)
@@ -99,13 +124,15 @@ def rank_program(g, core, T, topo):
     if rank is None:
         return
     N = len(T.cores)
-    tasks = []
+    tasks, lead = [], [0]
 
-    def task(e, f, r=(), w=(), b=(), dma=False):
-        tasks.append({"e": e, "f": f if isinstance(f, list) else [f], "r": list(r), "w": list(w), "b": list(b), "dma": dma})
+    def task(e, f, c, r=(), w=(), b=(), dma=0):
+        f = f if isinstance(f, list) else [f]
+        tasks.append({"e": e, "f": f, "r": list(r), "w": list(w), "b": list(b), "dma": dma > 0, "c": c, "lat": dma, "after": [], "lead": lead[0]})
+        return len(tasks) - 1
 
-    def arrival(sem, val, w):
-        tasks.append({"e": "x", "f": [], "r": [], "w": list(w), "b": [], "dma": False, "sem": sem, "val": val})
+    def arrival(sem, val, w, like):
+        tasks.append({"e": "x", "f": [], "r": [], "w": list(w), "b": [], "dma": False, "sem": sem, "val": val, "c": 0, "lat": REMOTE, "after": [like], "lead": 0})
 
     def ms(ap, c): return lambda q: q.memset(ap, c)
     def cp(o, i): return lambda q: q.tensor_copy(o, i)
@@ -113,294 +140,254 @@ def rank_program(g, core, T, topo):
     def ts(o, a, s1, op0, s2=None, op1=None):
         if op1 is None: return lambda q: q.tensor_scalar(o, a, s1, None, op0)
         return lambda q: q.tensor_scalar(o, a, s1, s2, op0, op1)
+    def red(o, i): return lambda q: q.tensor_reduce(o, i, AxisListType.X, A.add)
     def scan(o, a, b, op0, op1): return lambda q: q.tensor_tensor_scan(o, a, b, 0.0, op0, op1)
     def act(o, i, fn=F.Identity, bias=0.0, scale=1.0): return lambda q: q.activation(o, i, fn, bias=bias, scale=scale)
     def mm(o, l, r, st=True, sp=True): return lambda q: q.matmul(o, l, r, st, sp)
-    def tr(o, i, idn): return lambda q: q.transpose(o, i, idn)
     def dma(o, i): return lambda q: q.dma_start(o, i)
-    def paint(name, ap, pat, val, base, cm):
-        task("g", lambda q: q.affine_select(ap, ap, pat, A.not_equal, val, base, cm), r=[name], w=[name])
-    def io(ap, n, val): return lambda q: q.iota(ap, [[0, n]], val, 0, allow_small_or_imprecise_dtypes=True)
-    def fill(names, ap, n, val): task("g", io(ap, n, val), w=names)
+    def load(e, fs, kib, r=(), w=()): task(e, fs, 60 * len(fs), r=r, w=w, dma=LOCAL + 4 * kib)
+    def paint(name, ap, n, pat, val, base, cm, src=None, op=A.not_equal):
+        task("g", lambda q: q.affine_select(ap, ap if src is None else src, pat, op, val, base, cm), 200 + 2 * n, r=[name, "Z"], w=[name])
     def ch(j): return slice(512 * j, 512 * j + 512)
-    def oc(j): return slice(32 * j, 32 * j + 32)
-    XB, YB = [T.X0, T.X1], [T.Y0, T.Y1]
+    ALL, REV = slice(None), slice(None, None, -1)
+    def back(a, b): return slice(b - 1, a - 1 if a else None, -1)
 
     for a, b in ((0, 1), (1, 2), (2, 4), (4, 6), (6, 8)):
-        task("y", dma(T.ar[:, 512 * a:512 * b], T.arcs[:, 512 * a:512 * b]), w=["ar%d" % j for j in range(a, b)], dma=True)
-    task("s", [dma(T.std[:, :, :, kk, :], T.st0[:, (7 - kk) * 24:(8 - kk) * 24]) for kk in range(8)], w=["std"], dma=True)
-    task("s", [dma(T.rsi[kk:64:8, :], T.rs0[:, (7 - kk) * L_:(8 - kk) * L_]) for kk in range(8)], w=["rsi"], dma=True)
-    task("s", dma(T.acs[:, :], T.ac[:, :]), w=["acs"], dma=True)
-    task("y", [dma(T.sti[:, q2, :], T.std[:, q2, :, :, :]) for q2 in range(8)], r=["std"], w=["sti"], dma=True)
+        lead[0] = 10 ** 6 * (8 - a)
+        load("y", [dma(T.ar[:, 512 * a:512 * b], T.arcs[:, 512 * a:512 * b])], 256 * b, w=["ar%d" % j for j in range(a, b)])
+    lead[0] = 0
+    load("s", [dma(T.std[:, :, :, k, :], T.st0[:, k * 24:k * 24 + 24]) for k in range(8)], 300, w=["std"])
+    load("s", [dma(T.rsi[0:64, :], T.rs0[:, :])], 100, w=["rsi"])
+    load("s", [dma(T.acs[:, :], T.ac[:, :])], 200, w=["acs"])
+    load("y", [dma(T.sti[:, q2, :], T.std[:, q2, :, :, :]) for q2 in range(8)], 300, r=["std"], w=["sti"])
 
-    task("v", [ms(T.If[:], 0.0), ms(T.sD[0:64, :, :], 0.0), ms(T.sD[64:66, 1:8, :], 0.0), ms(T.sD[64:66, 0, :], 512.0)], w=["If", "sD"])
-    task("v", [ms(T.Ib[:], 0.0), ms(T.sC[:], 0.0), ms(T.sL[0:64, :, :], 0.0), ms(T.sP[0:64, :], 0.0), ms(T.sL[64:66, :, 1:17], -64.5),
-               ms(T.sL[64:66, :, 0:1], 500.0), ms(T.sP[64:66, :], 39.0 / 64), ms(T.I17[:], 0.0)], w=["Ib", "sL", "sP", "sC", "I17"])
-    task("v", [ms(T[n][:], 0.0) for n in ("EE", "Db")] + [ms(T.ri[64:128, 0, :], 1.0), ms(T.dup[:, :, 0:1], 0.0), ms(T.nf[:, 0:2], 0.0)],
-         w=["EE", "Db", "ri0c", "dup", "nf"])
+    task("v", [ms(T.Z[:], 0.0), ms(T.Zf[:], 0.0)], 768, w=["Z"])
+    task("v", [ms(T.sD[64:66, 0:7, :], 0.0), ms(T.sD[64:66, 7, :], 512.0), ms(T.sD[0:64, 7, :], 0.0), ms(T.sL[64:66], -15.5),
+               ms(T.ri[64:128, 0, :], 1.0), ms(T.Bk[:], 1.0), ms(T.sP[0:64], 0.0), ms(T.Lp[:], 0.0),
+               ms(T.p16[:], 0.0), ms(T.pU[:], 0.0), ms(T.nf[:, 0:L_:128], 0.0)],
+         1700, w=["sDc", "sLc", "ri0c", "Bk", "sP", "sK0", "Lp", "p16", "pU", "nf0", "nf1"])
+    task("v", [ms(T.p16[:, 0:256:16], 1000.0), ms(T.pU[:, 15:256:16], -4.0), ms(T.pU[:, 0:256:16], 1.0)], 192, w=["p16", "pU"])
+    task("v", [ms(T.sP[64:66], -25.0 / 64), cp(T.zd[:], T.Z[:, 0:392]), ts(T.DD[:, :, 0], T.Z[:, 0:24], -4096.0, A.add)],
+         450, r=["Z"], w=["sPc", "sK", "zd0", "zd1", "DD0", "DD1"])
+    paint("I2", T.I2[:], 256, [[0, 2], [-1, 128]], 1.0, 0, 1, T.Zf[:])
+    paint("sD", T.sD[0:64, 0:7, :], 896, [[-1, 7], [-8, 8], [0, 16]], 1.0, 0, 1, T.Z[0:64, 0:896])
+    paint("sD", T.sD[0:64, 0:7, :], 896, [[-1, 7], [-8, 8], [0, 16]], -1.0, -1, 1)
+    paint("sL", T.sL[0:64], 128, [[-8, 8], [0, 16]], -1.0, 0, 1, T.Z[0:64, 0:128])
+    paint("Bk", T.Bk[:, 1:9, :], 128, [[-16, 8], [0, 16]], 0.0, 0, 1, op=A.is_ge)
+    paint("Bk", T.Bk[:, 1:9, :], 128, [[16, 8], [0, 16]], 0.0, 15, -1, op=A.is_ge)
+    paint("Bk", T.Bk[:, 0, :], 16, [[0, 16]], 0.0, -112, 1, op=A.is_ge)
+    paint("Lh", T.Lh[:], 128, [[-1, 128]], 1.0, 0, 1, T.Z[:, 0:128])
+    paint("Lh", T.Lh[:, :, 0:15], 120, [[-16, 8], [-1, 15]], -1.0, -1, 1)
+    paint("Lm", T.Lm[:], 128, [[-2, 64], [0, 2]], 1.0, 0, 1, T.Z[:, 0:128])
+    paint("Lm", T.Lm[:, :, 0:7, :], 112, [[-16, 8], [-2, 7], [0, 2]], -1.0, -2, 1)
+    paint("Lh", T.Lh[:, :, 0], 8, [[-16, 8]], -2.0, -1, 1)
+    paint("Lm", T.Lm[:, :, 0, :], 16, [[-16, 8], [0, 2]], -1.0, -1, 1)
+    for a, b, base in ((1, 8, 0), (0, 1, -56)):
+        paint("sP", T.sP[0:64, a:b, :, 1:8], 98, [[-8, b - a], [0, 14]], 1.0 / 128, base, 1)
+        paint("sP", T.sP[0:64, a:b, :, 1:8], 98, [[-8, b - a], [0, 2], [-1, 7]], -1.0 / 128, base - 1, 1)
+    task("g", lambda q: q.iota(T.kb[:, 0:128], [[0, 8], [1, 16]], 0, 0, allow_small_or_imprecise_dtypes=True), 400, w=["kb0"])
+    paint("Db", T.Db[:], 128, [[-1, 2], [-2, 64]], 4096.0, 0, 1, T.Z[:, 0:128])
+    I1 = T.I2[:, 0:128]
+    task("s", [act(T.Ib[:, n, :], I1, scale=s) for n, s in enumerate((1.0, -4096.0, 2.0 ** -7))] + [act(T.If4[:], I1, scale=4096.0)], 512, r=["I2"], w=["Ib"])
+    task("v", [ts(T.Ih[:, n, :], I1, s, A.mult) for n, s in enumerate((1.0, -1.0, -4096.0, 2.0 ** -12))]
+         + [red(T.col[:, u:u + 1], T.I2[:, u:128:2]) for u in range(2)] + [red(T.col[:, 2 + u:3 + u], T.I2[:, u:128:16]) for u in range(2)], 800, r=["I2"], w=["Ih", "col"])
+    task("v", [ts(T.col[:, 4:5], T.col[:, 1:2], 8192.0, A.mult, -4096.0, A.add), ts(T.col[:, 6:7], T.col[:, 2:3], 6144.0, A.mult),
+               ts(T.col[:, 7:8], T.col[:, 3:4], -2048.0, A.mult)], 192, r=["col"], w=["col4"])
+    task("v", ts(T.col[:, 5:6], T.col[:, 4:5], T.col[:, 6:7], A.add, T.col[:, 7:8], A.add), 64, r=["col4"], w=["col5"])
+    task("v", [cp(T.Dh[:], T.Db[:]), ts(T.sP[64:65], T.kb[64:65, 0:128], 1.0 / 2048, A.mult)], 128, r=["Db", "kb0", "sPc"], w=["Dh", "sPc"])
+    task("s", [act(T.sC[:, :, u], T.Bk[:, 0:8, 0], scale=T.col[:, u:u + 1]) for u in range(2)] + [act(T.sM[:], T.Bk[:, 0:8, :], scale=-1.0 / 128)]
+         + [act(T.Lp[:, b, :, b, :], T.Bk[:, 1:9, 0:8], scale=T.col[:, 5:6]) for b in range(2)], 400, r=["Bk", "col", "col5", "Lp"], w=["sC", "Lp"])
+    task("s", [act(T.ro[64:128, t, :], T.Z[64:128, 0:L_], bias=1.0) for t in range(V_)], V_ * L_, r=["Z"], w=["roc"])
+    task("t", [lambda q, c=c: q.transpose(T.AC[:, 128 * c:128 * c + 128], T.acs[:, 128 * c:128 * c + 128], I1) for c in range(3)], 1536,
+         r=["acs", "I2"], w=["AC"], b=["AC"])
+    task("s", act(T.acT[:], T.AC[:, 0:L_]), 384, r=["AC"], w=["acT"], b=["AC"])
+    task("v", [cp(T.xi[:, 0, q2:192:8], T.sti[:, q2, :]) for q2 in range(8)] + [ts(T.ri[0:64, 0, :], T.rsi[0:64, :], -1.0, A.mult, 98.0, A.add)], 900,
+         r=["sti", "rsi", "ri0c"], w=["xi00", "xi01", "ri00", "ri01"])
 
-    paint("If", T.If[:], [[-1, 128]], 1.0, 0, 1)
-    paint("sD", T.sD[0:64, 1:8, :], [[-1, 7], [-8, 8], [0, 16]], 1.0, 0, 1)
-    paint("sD", T.sD[0:64, 1:8, :], [[-1, 7], [-8, 8], [0, 16]], -1.0, -1, 1)
-    paint("Ib", T.Ib[:], [[-1, 128]], 1.0, 0, 1)
-    paint("I17", T.I17[:, :, 1:17], [[-16, 8], [-1, 16]], 1.0, 0, 1)
-    paint("sL", T.sL[0:64, :, 1:17], [[-8, 8], [0, 16]], 1.0, -7, 1)
-    task("g", [io(T.p17[:], 408, 0), io(T.pS[:], 816, 0), io(T.d3[:, 0:L_:2], 192, 1), io(T.d3[:, 1:L_:2], 192, 0),
-               io(T.p3[:], L_, 1), io(T.d4[:], 392, 0), io(T.p4[:], 392, 1)], w=["p17", "pS", "d3", "p3", "d4", "p4"])
-    task("g", [io(T.p17[:, 0:408:17], 24, 1000), io(T.p3[:, 0:L_:16], 24, 0), io(T.p4[:, 0:392:8], 49, 0)]
-         + [io(T.pS[:, 0, 1 + a:408:17], 24, 1) for a in range(1, 16, 2)]
-         + [io(T.pS[:, 1, 1 + a:408:17], 24, 4096 if a % 2 else -4096) for a in range(16)], w=["p17", "pS", "p3", "p4"])
-    task("g", lambda q: q.iota(T.kb[:, 0:8, :], [[0, 8], [1, 16]], 0, 0, allow_small_or_imprecise_dtypes=True), w=["kb"])
-    paint("sP", T.sP[0:64, 16:128], [[-8, 7], [0, 2], [1, 8]], 1.0 / 128, -7, 1)
-    paint("sP", T.sP[0:64, 0:16], [[0, 2], [1, 8]], 1.0 / 128, -63, 1)
-    paint("EE", T.EE[:], [[-1, 128], [0, 8]], 1.0, 0, 1)
-    paint("Db", T.Db[:], [[-1, 2], [-2, 64]], 1.0, 0, 1)
     for j in range(8):
-        paint("sC", T.sC[:, 2:16], [[-16, 7], [-1, 2]], 1.0, -2 * j, 1)
-        paint("sC", T.sC[:, 0:2], [[-1, 2]], 1.0, -112 - 2 * j, 1)
-    for n, k in (("Df", 128), ("In", 128), ("zd", 392), ("p8", 192), ("PM", 512)): fill([n], T[n][:], k, 0)
-    fill(["p8"], T.p8[:, 7:192:8], 24, 1024)
-    fill(["ro%d" % t for t in range(V_)], T.ro[:], V_ * L_, 1)
-    paint("Df", T.Df[:], [[-1, 2], [-2, 64]], 8388608.0, 0, 1)
-    paint("In", T.In[:], [[-1, 128]], 64.0, 0, 1)
-    for t in range(4):
-        paint("PM", T.PM[:, t, :], [[-1, 128]], 1.0, 16 * (4 - t), 1)
-        paint("PM", T.PM[:, t, :], [[-1, 128]], 1.0, 16 * (4 - t) - 128, 1)
-
-    PB = [("X0", T.X0), ("X1", T.X1), ("Y0", T.Y0), ("Y1", T.Y1)]
-
-    def bits(j):
-        task("v", [ts(T.a0[:, j % 2, :], T.ar[:, ch(j)], 32767, A.bitwise_and), ts(T.a1[:, j % 2, :], T.ar[:, ch(j)], 15, A.logical_shift_right)],
-             r=["ar%d" % j], w=["a%d" % (j % 2)])
-    bits(0)
-    for j in range(8):
-        n, P = PB[j % 4]
-        task("v", [cp(P[:], T.a1[:, j % 2, :]), cp(T.U0[:, ch(j)], T.a0[:, j % 2, :])], r=["a%d" % (j % 2)], w=[n, "U0%d" % j], b=[n])
-        if j < 7: bits(j + 1)
-        task("s", act(T.TT[:, ch(j)], T.U0[:, ch(j)]), r=["U0%d" % j], w=["TT%d" % j])
-        task("v", tt(T.MM[:, ch(j)], P[:], T.U0[:, ch(j)], A.min), r=[n, "U0%d" % j], w=["MM%d" % j], b=[n])
-        task("s", [act(T.U1[:, ch(j)], P[:]), act(T.TT[:, ch(8 + j)], P[:])], r=[n], w=["U1%d" % j, "TU%d" % j], b=[n])
+        n = ("D0", "D1", "M0", "M1")[j % 4]
+        task("v", [ts(T.a0[:, ch(j)], T.ar[:, ch(j)], 32767, A.bitwise_and), ts(T.a1[:, j % 2, :], T.ar[:, ch(j)], 15, A.logical_shift_right)], 1024,
+             r=["ar%d" % j], w=["a0%d" % j, "a1%d" % (j % 2)])
+        task("v", cp(T[n][:], T.a1[:, j % 2, :]), 512, r=["a1%d" % (j % 2)], w=[n], b=[n])
+        task("v", tt(T.MM[:, ch(j)], T.a0[:, ch(j)], T[n][:], A.min), 512, r=[n, "a0%d" % j], w=["MM%d" % j], b=[n])
+        task("s", [act(T.U1[:, ch(j)], T[n][:]), act(T.TT[:, ch(8 + j)], T[n][:])], 1024, r=[n], w=["U1%d" % j, "TU%d" % j], b=[n])
+        task("v", cp(T.TT[:, ch(j)], T.a0[:, ch(j)]), 512, r=["a0%d" % j], w=["TT%d" % j])
         if j % 2:
-            c = slice(512 * j - 512, 512 * j + 512)
-            task("y", [dma(T.TT[0:128:2, W_ + c.start:W_ + c.stop], T.U0[1:128:2, c]), dma(T.TT[1:128:2, c], T.U1[0:128:2, c])],
-                 r=["U0%d" % j, "U1%d" % j, "U0%d" % (j - 1), "U1%d" % (j - 1)],
-                 w=["TT%d" % j, "TT%d" % (j - 1), "TU%d" % j, "TU%d" % (j - 1)], dma=True)
-        if j == 1:
-            task("t", [tr(T.Z0[:, 8 * c:8 * c + 8, :], T.acs[:, 128 * c:128 * c + 128], T.If[:]) for c in range(3)],
-                 r=["acs", "If"], w=["Z0"], b=["Z0"])
-        if j == 3:
-            task("s", [act(T.acT[:, 1 + a:408:17], T.Z0[:, 0:24, a]) for a in range(16)] + [act(T.acT[:, 0:408:17], T.Z0[:, 0:24, 0], scale=0.0)],
-                 r=["Z0"], w=["acT"], b=["Z0"])
-        if j == 5:
-            task("v", [cp(T.xi[:, 0, q2:192:8], T.sti[:, q2, :]) for q2 in range(8)] + [cp(T.ri[0:64, 0, :], T.rsi[0:64, :]),
-                      ts(T.sP[64:65, :], T.kb[64:65, 0:8, :], 1.0 / 2048, A.mult)], r=["sti", "rsi", "ri0c", "kb"], w=["xi0", "ri0", "sP"])
-    task("y", [dma(T.pr[16:128, :], T.pay[0:112, :]), dma(T.pr[0:16, :], T.pay[112:128, :])], w=["pr"], dma=True)
-    MMs, TTs = ["MM%d" % j for j in range(8)], ["TT%d" % j for j in range(8)]
-
-    def spread(bank, n, R, t, name, j):
-        task("t", [mm(bank[:, kk:512:8], T.sD[0:66, kk, :], R[0:66, t, 64 * j:64 * j + 64]) for kk in range(8)],
-             r=["sD", name], w=[n], b=[n])
-
-    def prep(t, j):
-        n = "Y%d" % (j % 2)
-        spread(YB[j % 2], n, T.ro, t, "ro%d" % t, j)
-        task("s", act(T.GP[:, ch(j)], T.pr[:, 0:W_].indirect(T.xo[:, t, oc(j)])), r=["pr", "xo%d" % t], w=["GP%d" % j])
-        task("s", act(T.WW[:, ch(j)], YB[j % 2][:], F.Exp, scale=-0.125), r=[n], w=["WW%d" % j], b=[n])
-
-    def horner(j):
-        task("v", [scan(T.U0[:, ch(j)], T.WW[:, ch(j)], T.GP[:, ch(j)], A.mult, A.add),
-                   scan(T.U1[:, ch(j)], T.WW[:, ch(j)], T.GP[:, ch(j)], A.mult, A.max)],
-             r=["WW%d" % j, "GP%d" % j], w=["SO%d" % j, "U0%d" % j, "U1%d" % j])
-    SOs = ["SO%d" % j for j in range(6)]
+            c, two = slice(512 * j - 512, 512 * j + 512), (j - 1, j)
+            load("y", [dma(T.TT[0:128:2, W_ + c.start:W_ + c.stop], T.TT[1:128:2, c])], 256, r=["TT%d" % i for i in two], w=["TU%d" % i for i in two])
+            load("y", [dma(T.TT[1:128:2, c], T.U1[0:128:2, c])], 256, r=["U1%d" % i for i in two], w=["TT%d" % i for i in two])
+    load("s", [dma(T.pr[16:128, :], T.pay[0:112, :]), dma(T.pr[0:16, :], T.pay[112:128, :])], 1024, r=["ar7"], w=["pr"])
+    MMs, TTs = ["MM%d" % j for j in range(8)], ["T%s%d" % (h, j) for j in range(8) for h in "TU"]
     sent = [0]
 
     def send(out, src, sem, to, r):
-        dst = T.cores[to]
+        dst = T.cores[to % N]
         rid, pid, _ = topo.addr(dst)
-        task("g", lambda q: q.remote_dma(out, src, T.sem[sem], T.sem.gone, pid, rid, topo.mask(core, dst)), r=r)
         sent[0] += len(topo.engines(core, dst))
+        return task("g", lambda q: q.remote_dma(out, src, T.sem[sem], T.sem.gone, pid, rid, topo.mask(core, dst)), 300, r=r)
 
-    def compact(t, a, b):
-        task("s", [act(T.XO[:, t, h * L_ + 64 * a:h * L_ + 64 * b], (T.U0, T.U1)[h][:, 512 * a + 7:512 * b:8]) for h in range(2)],
-             r=SOs[a:b], w=["XO%d%d" % (t, a)])
+    def lands(sem, frm, w, like): arrival(sem, len(topo.engines(T.cores[frm % N], core)), w, like)
 
-    def hand_back(t):
-        compact(t, EARLY, 6)
-        if t: send(T.XL[:, t - 1, :], T.XO[:, t, :], "x%d" % t, (rank - t) % N, ["XO%d0" % t, "XO%d%d" % (t, EARLY)])
-
-    def gather_parts(t, first, last):
-        if t: arrival("x%d" % t, len(topo.engines(T.cores[(rank + t) % N], core)), ["XL%d" % t])
-        so = (T.XO, 0) if t == 0 else (T.XL, t - 1)
-        task("t", [mm(XB[h][:, 0:L_], T.PM[:, t, :], so[0][:, so[1], h * L_:h * L_ + L_], first, last) for h in range(2)],
-             r=["PM"] + (["XO00", "XO0%d" % EARLY] if t == 0 else ["XL%d" % t]), w=["X0", "X1"], b=["X0", "X1"])
-
-    ALL, REV = slice(None), slice(None, None, -1)
-
-    def side(mem, pp, dims, fix, rev=()):
-        ix = [0] * (3 - len(dims)) + [fix[d] if d in fix else REV if d in rev else ALL for d in dims]
-        return (T.Z2 if mem == 0 else T.SB)[(ALL, pp, slice(0, 24)) + tuple(ix)]
-
-    def layer(pp, allbits, s, flip, nxt, only_min=False):
-        din = [d for d in allbits if d != s]
-        dout = [d for d in allbits if d != nxt and not (only_min and d == s)]
-        low = [d for d in din if d < s] if flip else []
-        f = []
-        for mx in range(1 if only_min else 2):
-            for v in range(2):
-                o = 1 - v if nxt in low else v
-                a = side(0, pp, din, {nxt: o if mx else v}, low if mx else ())
-                b = side(1, pp, din, {nxt: v if mx else o}, () if mx else low)
-                f.append(tt(side(v, 1 - pp, dout, {s: mx}), a, b, A.max if mx else A.min))
-        task("v", f, r=["so%d" % pp], w=["so%d" % (1 - pp)], b=["Z2"])
+    def spread(n, R, t, name, j):
+        task("t", [mm(T[n][:, k:512:8], T.sD[0:66, k, :], R[0:66, t, 64 * j:64 * j + 64]) for k in range(8)], 512,
+             r=["sD", "sDc", "roc", name], w=[n], b=[n])
 
     B4, B3 = [3, 2, 1, 0], [2, 1, 0]
-
-    def network(steps):
-        pp = 0
-        for n in range(len(steps) - 1):
-            layer(pp, B4, steps[n][0], steps[n][1], steps[n + 1][0]); pp = 1 - pp
-        return pp
     EIGHT = [(0, 0), (1, 1), (0, 0), (2, 1), (1, 0), (0, 0), (3, 1)]
     UP = 128.5 + 2.0 ** -13
+    SINK = 2 * (16 * 132 - 800) + 2047.0 / 4096
 
-    def visit(t):
-        xi, ri = "xi%d" % t, "ri%d" % t
-        late = list(range(EARLY, 6)) if t >= 2 else []
-        for j in late[:AHEAD]: horner(j)
-        late = late[AHEAD:]
-        if t:
-            n = len(topo.engines(T.cores[(rank - 1) % N], core))
-            arrival("m%d" % t, n, [xi]); arrival("n%d" % t, n, [ri])
-        for j in range(6 - OWN, 6):
-            task("v", ts(T.G[:, ch(j)], T.MM[:, 0:W_].indirect(T.xi[:, t, oc(j)]), 2.0 ** -12, A.mult, UP, A.add),
-                 r=MMs + [xi], w=["G%d" % j])
-        for i in range(4): spread(PB[i][1], PB[i][0], T.ri, t, ri, i)
-        for j in range(6):
-            n, P = PB[j % 4]
-            if j < 6 - OWN:
-                task("s", act(T.G[:, ch(j)], T.MM[:, 0:W_].indirect(T.xi[:, t, oc(j)]), bias=UP, scale=2.0 ** -12),
-                     r=MMs + [xi], w=["G%d" % j])
-            if j == 1: task("v", cp(T.stf[:], T.xi[:, t, :]), r=[xi], w=["stf"])
-            if j == 2 and late: horner(late.pop(0))
-            task("v", scan(T.GS[:, ch(j)], P[:], T.G[:, ch(j)], A.add, A.min), r=[n, "G%d" % j], w=["GS%d" % j], b=[n])
-            if j < 2: spread(P, n, T.ri, t, ri, j + 4)
-            if j == 4 and t >= 1:
-                for i in range(EARLY): prep(t - 1, i)
-            if j % 2:
-                c = j // 2
-                task("t", [mm(T.Z3[:, 136 * c:136 * c + 136], T.ri[0:66, t, 128 * c:128 * c + 128], T.sL[0:66, :, :], True, False),
-                           mm(T.Z3[:, 136 * c:136 * c + 136], T.GS[:, 1024 * c + 7:1024 * c + 1024:8], T.I17[:], False, True)],
-                     r=[ri, "sL", "I17", "GS%d" % j, "GS%d" % (j - 1)], w=["Z3%d" % c] + (["Z3"] if c == 0 else []), b=["Z3"])
-        for j in late: horner(j)
-        task("t", [mm(T.Z1[:, 8 * c:8 * c + 8, :], T.ri[0:66, t, 128 * c:128 * c + 128], T.sP[0:66, :]) for c in range(3)],
-             r=[ri, "sP"], w=["Z1"], b=["Z1"])
-        task("v", tt(T.sc[:], T.Z3[:, 0:408], T.acT[:], A.add), r=["Z3", "Z30", "Z31", "Z32", "acT"], w=["sc"], b=["Z3"])
-        task("t", mm(T.Z3[:, 0:192], T.If[:], T.stf[:], True, False), r=["If", "stf"], w=["Z3"], b=["Z3"])
-        task("v", scan(T.X0[:, 0:408], T.p17[:], T.sc[:], A.add, A.min), r=["sc", "p17"], w=["X0"], b=["X0"])
-        task("v", tt(T.nf[:, 1:408], T.X0[:, 0:407], T.sc[:, 1:408], A.is_le), r=["sc", "X0"], w=["nf"], b=["X0"])
-        task("v", [scan(T.s2[:, 1, :], T.nf[:], T.pS[:, 1, :], A.mult, A.add), scan(T.s2[:, 0, :], T.nf[:], T.pS[:, 0, :], A.mult, A.add)],
-             r=["nf", "pS"], w=["s2"])
-        task("v", [cp(T.d4[:, 8:392:16], T.s2[:, 1, 16:408:17]), ts(T.d3[:, 0:L_:16], T.s2[:, 0, 16:408:17], 1.0, A.add)], r=["s2"], w=["d3", "d4"])
-        task("v", scan(T.zb[:], T.p4[:], T.d4[:], A.mult, A.add), r=["d4", "p4"], w=["zb"])
-        task("v", scan(T.H[:], T.p3[:], T.d3[:], A.mult, A.add), r=["d3", "p3"], w=["H"])
-        task("v", ts(T.H[:], T.H[:], 9.0, A.is_equal), w=["H"])
+    def visit(t, x):
+        c0, c1 = BATCHES[x]
+        lead[0] = LEAD * (1 - x)
+        nc = c1 - c0
+        cg, lg, lanes, cols = slice(8 * c0, 8 * c1), slice(0, 128 * nc), slice(128 * c0, 128 * c1), slice(64 * c0, 64 * c1)
+        K, M, Kn, Mn = T["K%d" % x], T["M%d" % x], "K%d" % x, "M%d" % x
+        def nm(s): return "%s%d" % (s, x)
+        xi, ri, xo, ro = ["%s%d%d" % (s, t, x) for s in ("xi", "ri", "xo", "ro")]
+        def wide(n): return max(64, n * nc)
+        def lc(c): return slice(128 * c, 128 * c + 128)
+        def gc(c, a=0, step=1): return slice(128 * (c - c0) + a, 128 * (c - c0) + 128, step)
+        chunks, pieces = range(c0, c1), range(2 * c0, 2 * c1)
 
-        def mask(j):
-            n = "X%d" % (j % 2)
-            task("t", mm(XB[j % 2][:], T.H[:, 128 * (j // 2):128 * (j // 2) + 128], T.EE[:, ch(j % 2)]), r=["H", "EE"], w=[n], b=[n])
-        task("t", [mm(T.Z3[:, 64 * c:64 * c + 64], T.zb[:, 128 * c + 8 - 8 * b:128 * c + 136 - 8 * b], T.Db[:, b, :], False, c == 2 and b == 1)
-                   for c in range(3) for b in range(2)], r=["zb", "Db"], w=["Z3"], b=["Z3"])
-        mask(0); mask(1)
-        task("v", cp(T.ix2[:], T.Z3[:, 0:192]), r=["Z3"], w=["ix2"], b=["Z3"])
-        early = list(range(EARLY)) if t >= 1 else []
-        for j in range(6 - OWN, 6):
-            task("v", cp(T.GA[:, ch(j)], T.TT[:, 0:2 * W_].indirect(T.ix2[:, oc(j)])), r=TTs + ["ix2"], w=["GA%d" % j])
-        for j in range(6):
-            n = "X%d" % (j % 2)
-            if j < 6 - OWN:
-                task("s", act(T.GA[:, ch(j)], T.TT[:, 0:2 * W_].indirect(T.ix2[:, oc(j)])), r=TTs + ["ix2"], w=["GA%d" % j])
-            if early and j == FILLC: horner(early.pop(0))
-            task("v", tt(T.GA[:, ch(j)], XB[j % 2][:], T.GA[:, ch(j)], A.mult), r=[n], w=["GA%d" % j], b=[n])
-            if j < 4: mask(j + 2)
-            if j % 2:
-                c = j // 2
-                task("t", [mm(T.Z0[:, 8 * c:8 * c + 8, 7 - kk:16:8] if c < 2 else T.Z3[:, 7 - kk:128:8],
-                              T.GA[:, 1024 * c + kk:1024 * c + 1024:8], T.sC[:]) for kk in range(8)],
-                     r=["sC", "GA%d" % j, "GA%d" % (j - 1)], w=[["Z00", "Z0"], ["Z01"], ["Z3"]][c], b=["Z0" if c < 2 else "Z3"])
-        task("s", act(T.kb[:], T.Z0[:, 0:16, :], bias=UP, scale=2.0 ** -12), r=["Z0", "Z00", "Z01"], w=["kb"], b=["Z0"])
-        task("s", act(T.kb[:], T.kb[:], bias=-129.0), w=["kb"])
-        task("s", act(T.k1[:, 0:16, :], T.kb[:], scale=4096.0 - 2.0 ** -7), r=["kb"], w=["k1", "k1Z0"])
-        for j in early: horner(j)
-        if t >= 2: hand_back(t - 2)
-        if t >= 1:
-            compact(t - 1, 0, EARLY)
-            for j in range(EARLY, EARLY + PRE): prep(t - 1, j)
-        if t == V_ - 1:
-            for s in range(3): gather_parts(s, s == 0, False)
-        Z0, Z1, zz = T.Z0[:, 0:24, :], T.Z1[:, 0:24, :], ["Z0", "Z00", "Z01", "Z02"]
-        big = 1.5 * 2.0 ** 35
-        k3, P3 = T.k1[:, 16:24, :], T.Z3[:, 0:128]
-        task("v", ts(k3, P3, -2047.5, A.add, big, A.add), r=["Z3"], w=["k1Z3"], b=["Z3"])
-        task("v", ts(k3, k3, big, A.subtract, 1.0 - 2.0 ** -19, A.mult), w=["k1Z3"])
-        task("v", tt(k3, P3, k3, A.subtract), r=["Z3"], w=["k1Z3"], b=["Z3"])
-        task("v", tt(T.k1[:, 0:16, :], T.Z0[:, 0:16, :], T.k1[:, 0:16, :], A.subtract), r=zz, w=["k1Z0"], b=["Z0"])
-        task("v", [tt(side(v, 0, [3, 2, 1], {}), T.Z1[:, 0:24, v:16:2], T.k1[:, :, v:16:2], A.add) for v in range(2)],
-             r=["k1Z0", "k1Z3", "Z1"], w=["so0"], b=["Z1", "Z2"])
-        pp = network(EIGHT + [(2, 0), (1, 0), (0, 0)])
-        task("v", [tt(T.k1[:, :, mx:16:2], side(0, pp, [3, 2, 1], {}), side(1, pp, [3, 2, 1], {}), A.max if mx else A.min) for mx in range(2)],
-             r=["so%d" % pp], w=["k1", "k1Z0", "k1Z3"], b=["Z2"])
-        task("v", ts(Z0, T.k1[:], 8388608.0, A.add, 8388607.5, A.subtract), r=["k1"], w=zz, b=["Z0"])
-        task("s", act(T.k2[:], T.k1[:], bias=8388608.0), r=["k1"], w=["k2"])
-        task("s", act(T.k2[:], T.k2[:], bias=-4096.0 * 2.0 ** -23, scale=2.0 ** -23), w=["k2"])
-        task("v", [tt(Z1, T.k1[:], Z0, A.subtract), tt(T.dup[:, :, 1:16], T.k1[:, :, 1:16], T.Z0[:, 0:24, 0:15], A.is_lt)],
-             r=zz + ["k1"], w=["Z1", "dup"], b=["Z0", "Z1"])
-        task("v", tt(Z0, Z1, T.k2[:], A.add), r=["Z1", "k2"], w=zz, b=["Z0", "Z1"])
-        task("v", [tt(side(v, 0, [3, 2, 1], {}), T.Z0[:, 0:24, v:16:2], T.dup[:, :, v:16:2], A.max) for v in range(2)],
-             r=zz + ["dup"], w=["so0"], b=["Z0", "Z2"])
-        if t >= 1:
-            for j in range(EARLY + PRE, 6): prep(t - 1, j)
+        task("v", ts(T.sth[:, cols], T.xi[:, t, cols], -2048.0, A.add), 64, r=[xi], w=[nm("sth")])
+        for j in pieces:
+            n = (Mn, "D0" if x == 0 else Kn)[j % 2]
+            spread(n, T.ri, t, ri, j)
+            task("s", act(T.G[:, ch(j)], T.MM[:, 0:W_].indirect(T.xi[:, t, 32 * j:32 * j + 32]), bias=UP, scale=2.0 ** -12), 80 + 512 * GATHER,
+                 r=MMs + [xi] + ["GA3"] * (x and t < STAG), w=["G%d" % j])
+            bk = back(512 * j, 512 * j + 512)
+            task("v", scan(T.GS[:, bk], T[n][:, REV], T.G[:, bk], A.add, A.min), 512, r=[n, "G%d" % j], w=["GS%d" % j], b=[n])
+        GSs = ["GS%d" % j for j in pieces]
+        for c in chunks:
+            task("t", [mm(K[:, gc(c)], T.ri[0:66, t, lc(c)], T.sL[0:66], True, False),
+                       mm(K[:, gc(c)], T.GS[:, 1024 * c:1024 * c + 1024:8], T.Ib[:, 0, :], False, True)], 256,
+                 r=[ri, "sL", "sLc", "Ib", "GS%d" % (2 * c), "GS%d" % (2 * c + 1)], w=[Kn], b=[Kn])
+        task("v", tt(T.sc[:, lanes], K[:, lg], T.acT[:, lanes], A.add), wide(128), r=[Kn, "acT"], w=[nm("sc")], b=[Kn])
+        task("v", scan(M[:, lg], T.p16[:, lg], T.sc[:, lanes], A.add, A.min), wide(128), r=[nm("sc"), "p16"], w=[Mn], b=[Mn])
+        task("v", tt(T.nf[:, 128 * c0 + 1:128 * c1], M[:, 0:128 * nc - 1], T.sc[:, 128 * c0 + 1:128 * c1], A.is_gt), wide(128), r=[nm("sc"), Mn], w=[nm("nf")], b=[Mn])
+        bk = back(128 * c0, 128 * c1)
+        task("v", scan(T.UU[:, bk], T.pU[:, back(0, 128 * nc)], T.nf[:, bk], A.add, A.max), wide(64), r=[nm("nf"), "pU"], w=[nm("UU")])
+        task("t", [mm(K[:, gc(c)], T.UU[:, lc(c)], T.Ib[:, 0, :]) for c in chunks], 128 * nc, r=[nm("UU"), "Ib"], w=[Kn], b=[Kn])
+        task("s", act(T.UT[:, lanes], K[:, lg]), wide(128), r=[Kn], w=[nm("UT")], b=[Kn])
+        half = slice(0, 64 * nc)
+        task("t", [mm(K[:, half], T.Ih[:, 0, :], T.sth[:, cols], True, False)]
+             + [mm(K[:, half], T.Lp[:, b], T.UT[:, 128 * c0 + b:128 * c1:2], False, b == 1) for b in range(2)], 192 * nc,
+             r=[nm("UT"), nm("sth"), "Lp", "Ih"], w=[Kn], b=[Kn])
+        task("v", cp(T.ix2[:, cols], K[:, half]), wide(64), r=[Kn], w=[nm("ix2")], b=[Kn])
+        one = slice(256, 256 + 128 * nc)
+        task("t", [mm(M[:, lg], T.Lm[:], T.UT[:, lanes]), mm(M[:, one], T.Lh[:], T.UT[:, lanes])], 256 * nc, r=[nm("UT"), "Lm", "Lh"], w=[Mn], b=[Mn])
+        task("v", tt(T.MH[:, lanes], M[:, one], T.GS[:, 1024 * c0:1024 * c1:8], A.mult), wide(128), r=[Mn] + GSs, w=[nm("MH")], b=[Mn])
+        for j in pieces:
+            task("s", act(T.GA[:, ch(j)], T.TT[:, 0:2 * W_].indirect(T.ix2[:, 32 * j:32 * j + 32])), 80 + 512 * GATHER, r=TTs + [nm("ix2")], w=["GA%d" % j])
+        for c in chunks:
+            n = Kn if c == c0 else "D0"
+            for h in range(2):
+                ks = range(4 * h, 4 * h + 4)
+                ga = [T.GA[:, 1024 * c + k:1024 * c + 1024:8] for k in range(8)]
+                task("v", [tt(ga[k], M[:, gc(c)], ga[k], A.mult) for k in ks], 512, r=[Mn, "GA%d" % (2 * c), "GA%d" % (2 * c + 1)], w=["GB%d%d" % (c, h)], b=[Mn])
+                task("t", [mm(T[n][:, 256 + k:384:8], ga[k], T.sC[:]) for k in ks], 1024,
+                     r=["sC", "GB%d%d" % (c, h), "GA%d" % (2 * c), "GA%d" % (2 * c + 1)], w=[n], b=[n])
+            task("s", [act(T.kb[:, lc(c)], T[n][:, 256:384], bias=UP, scale=2.0 ** -12), act(T.pen[:, lc(c)], T[n][:, 256:384], bias=129 * 4096.0 - 2048)], 256,
+                 r=[n], w=["kb%d" % c, nm("pen")], b=[n])
+            task("t", [mm(K[:, gc(c)], I1, T.pen[:, lc(c)], True, False)] + [mm(K[:, gc(c)], T.Ib[:, i, :], T.kb[:, lc(c)], False, False) for i in (1, 2)]
+                 + [mm(K[:, gc(c)], T.ri[0:66, t, lc(c)], T.sP[0:66], False, False), mm(K[:, gc(c)], T.MH[:, lc(c)], T.sM[:], False, True)], 1024,
+                 r=["kb%d" % c, nm("pen"), nm("MH"), ri, "sP", "sPc", "sC", "Ib", "I2"], w=[Kn], b=[Kn])
+        task("s", act(T.SB[:, cg, 0], K[:, 1:128 * nc:2]), wide(64), r=[Kn], w=[nm("so0")], b=[Kn])
+
+        def side(mem, pp, dims, fix, rev=()):
+            ix = [0] * (3 - len(dims)) + [fix[d] if d in fix else REV if d in rev else ALL for d in dims]
+            return (T.S if mem == 0 else T.SB)[(ALL, cg, pp) + tuple(ix)]
+
+        def layer(pp, allbits, s, flip, nxt, only_min=False, first=False):
+            din = [d for d in allbits if d != s]
+            dout = [d for d in allbits if d != nxt and not (only_min and d == s)]
+            low = [d for d in din if d < s] if flip else []
+            f = []
+            for mx in range(1 if only_min else 2):
+                for v in range(2):
+                    o = 1 - v if nxt in low else v
+                    a = K[:, 2 * v:128 * nc:4] if first else side(0, pp, din, {nxt: o if mx else v}, low if mx else ())
+                    b = side(1, pp, din, {nxt: v if mx else o}, () if mx else low)
+                    f.append(tt(side(v, 1 - pp, dout, {s: mx}), a, b, A.max if mx else A.min))
+            task("v", f, len(f) * wide(2 ** (len(allbits) + 1)), r=[nm("so%d" % pp)] + [Kn] * first, w=[nm("so%d" % (1 - pp))], b=["S"] + [Kn] * first)
+
+        def network(steps, first=False):
+            pp = 0
+            for n in range(len(steps) - 1):
+                layer(pp, B4, steps[n][0], steps[n][1], steps[n + 1][0], first=first and n == 0); pp = 1 - pp
+            return pp
+        pp = network(EIGHT + [(2, 0), (1, 0), (0, 0)], True)
+        task("v", [tt(T.k1[:, 128 * c0 + mx:128 * c1:2], side(0, pp, [3, 2, 1], {}), side(1, pp, [3, 2, 1], {}), A.max if mx else A.min) for mx in range(2)], 2 * wide(64),
+             r=[nm("so%d" % pp)], w=[nm("k1")], b=["S"])
+        task("v", ts(T.DD[:, cg, 1:17], T.k1[:, lanes], 1.5 * 2 ** 23, A.add, 1.5 * 2 ** 23, A.subtract), wide(128), r=[nm("k1")], w=[nm("DD")])
+        task("t", mm(M[:, lg], T.If4[:], T.k1[:, lanes], True, False), 512 * nc, r=[nm("k1"), "Ib"], w=[Mn], b=[Mn])
+        task("t", [mm(K[:, lg], T.Ih[:, 0, :], T.DD[:, cg, 0:16], True, False), mm(K[:, lg], T.Ih[:, 1, :], T.DD[:, cg, 1:17], False, True)], 256 * nc,
+             r=[nm("DD"), "Ih"], w=[Kn], b=[Kn])
+        task("t", [mm(M[:, lg], T.Ih[:, n, :], T.DD[:, cg, 1:17], False, n == 3) for n in (2, 3)], 256 * nc, r=[nm("DD"), "Ih"], w=[Mn], b=[Mn])
+        task("s", act(T.pen[:, lanes], K[:, lg], bias=SINK, scale=8192.0), wide(128), r=[Kn], w=[nm("pen")], b=[Kn])
+        task("v", [tt(side(v, 0, [3, 2, 1], {}), M[:, v:128 * nc:2], T.pen[:, 128 * c0 + v:128 * c1:2], A.max) for v in range(2)], 2 * wide(64),
+             r=[Mn, nm("pen")], w=[nm("so0")], b=[Mn, "S"])
         pp = network(EIGHT)
         layer(pp, B4, 3, 1, 2, only_min=True); pp = 1 - pp
         layer(pp, B3, 2, 0, 1); pp = 1 - pp
         layer(pp, B3, 1, 0, 0); pp = 1 - pp
-        task("v", [tt(T.KS[:, :, 1 - mx:8:2], side(0, pp, [2, 1], {}, [2, 1]), side(1, pp, [2, 1], {}, [2, 1]), A.max if mx else A.min) for mx in range(2)],
-             r=["so%d" % pp], w=["KS"], b=["Z2"])
-        task("v", ts(T.yy[:], T.KS[:], 2047.5 * 2.0 ** -23, A.add, 4096.0, A.add), r=["KS"], w=["yy"])
-        task("v", [ts(T.Z0[:, 0:24, 0:8], T.yy[:], 4096.0, A.subtract),
-                   ts(T.cb[:], T.yy[:], 4096.0 - (115 - 0.46875) / 128, A.subtract, 128.0, A.mult)], r=["yy"], w=zz + ["cb"], b=["Z0"])
-        task("v", tt(T.zd[:, 1:49:2, :], T.KS[:], T.Z0[:, 0:24, 0:8], A.subtract), r=zz + ["KS"], w=["zd"], b=["Z0"])
-        task("t", [mm(T.Z3[:, 64 * c:64 * c + 64], T.zd[:, 16 * c + 1 - b:16 * c + 17 - b, :], T.Df[:, b, :], b == 0, b == 1)
-                   for c in range(3) for b in range(2)], r=["zd", "Df"], w=["Z3"], b=["Z3"])
-        task("v", [scan(T.Y0[:, 191::-1], T.p8[:, ::-1], T.cb[:, ::-1], A.add, A.min), ts(T.ng[:], T.cb[:], 242.5, A.is_lt)],
-             r=["cb", "p8"], w=["Y0", "ng"], b=["Y0"])
-        task("v", tt(T.Y0[:, 192:384], T.Y0[:, 0:192], T.cb[:], A.subtract), r=["cb"], w=["Y0"], b=["Y0"])
-        task("v", tt(T.tn[:], T.Y0[:, 192:384], T.ng[:], A.mult), r=["ng", "Y0"], w=["tn"], b=["Y0"])
-        task("v", ts(T.xo[:, t, :], T.Z3[:, 0:192], 4095.0, A.add), r=["Z3"], w=["xo%d" % t], b=["Z3"])
-        if t < V_ - 1: send(T.xi[:, t + 1, :], T.xo[:, t, :], "m%d" % (t + 1), (rank + 1) % N, ["xo%d" % t])
-        f = []
-        for c in range(3):
-            f += [mm(T.Z1[0:64, 8 * c:8 * c + 8, :], T.ng[:, 64 * c:64 * c + 64], T.In[:], True, False),
-                  mm(T.Z1[0:64, 8 * c:8 * c + 8, :], T.tn[:, 64 * c:64 * c + 64], T.Ib[:], False, True)]
-        task("t", f, r=["ng", "tn", "In", "Ib"], w=["Z1"], b=["Z1"])
-        task("s", act(T.ro[0:64, t, :], T.Z1[0:64, 0:24, :], bias=64.0, scale=-1.0), r=["Z1"], w=["ro%d" % t], b=["Z1"])
-        if t < V_ - 1: send(T.ri[:, t + 1, :], T.ro[:, t, :], "n%d" % (t + 1), (rank + 1) % N, ["ro%d" % t])
+        task("v", [tt(T.KS[:, cg, mx:8:2], side(0, pp, [2, 1], {}), side(1, pp, [2, 1], {}), A.max if mx else A.min) for mx in range(2)], 2 * wide(32),
+             r=[nm("so%d" % pp)], w=[nm("KS")], b=["S"])
+        task("v", ts(T.S[:, cg, 1 - pp], T.KS[:, cg], 1.5 * 2 ** 24, A.add, 1.5 * 2 ** 24, A.subtract), wide(64), r=[nm("KS")], w=[nm("so%d" % (1 - pp))], b=["S"])
+        task("v", tt(T.zd[:, 16 * c0 + 1:16 * c1 + 1:2, :], T.KS[:, cg], T.S[:, cg, 1 - pp], A.subtract), wide(64),
+             r=[nm("KS"), nm("so%d" % (1 - pp))], w=[nm("zd")], b=["S"])
+        task("s", act(T.cb[:, cg], T.KS[:, cg], bias=180 - 15.0 / 32, scale=1.0 / 32), wide(64), r=[nm("KS")], w=[nm("cb")])
+        task("t", [mm(K[:, 64 * (c - c0):64 * (c - c0) + 64], T.zd[:, 16 * c + 1 - b:16 * c + 17 - b, :], T.Dh[:, b, :], b == 0, b == 1)
+                   for c in chunks for b in range(2)], 128 * nc, r=[nm("zd"), "Dh"], w=[Kn], b=[Kn])
+        task("v", ts(T.xo[:, t, cols], K[:, half], 2048.0, A.add), wide(64), r=[Kn], w=[xo], b=[Kn])
+        task("t", [mm(M[0:64, gc(c)], T.cb[:, 8 * c:8 * c + 8, :], T.Ib[:, 0, :]) for c in chunks], 128 * nc, r=[nm("cb"), "Ib"], w=[Mn], b=[Mn])
+        task("s", act(T.ro[0:64, t, lanes], M[0:64, lg], F.Abs, bias=-228.0), wide(128), r=[Mn], w=[ro], b=[Mn])
+        if t < V_ - 1:
+            sem = "%d%d" % (t + 1, x)
+            lands("m" + sem, rank - 1, ["xi" + sem], send(T.xi[:, t + 1, cols], T.xo[:, t, cols], "m" + sem, rank + 1, [xo]))
+            lands("n" + sem, rank - 1, ["ri" + sem], send(T.ri[:, t + 1, lanes], T.ro[:, t, lanes], "n" + sem, rank + 1, [ro, "roc"]))
 
-    for t in range(V_): visit(t)
+        lead[0] = 0
+        for j in pieces:
+            spread("D1", T.ro, t, ro, j)
+            task("s", act(T.GP[:, ch(j)], T.pr[:, 0:W_].indirect(T.xo[:, t, 32 * j:32 * j + 32])), 80 + 512 * GATHER, r=["pr", xo], w=["GP%d" % j])
+            task("s", act(T.WW[:, ch(j)], T.D1[:], F.Exp, scale=-0.125), 512, r=["D1", "roc"], w=["WW%d" % j], b=["D1"])
+            bk = back(512 * j, 512 * j + 512)
+            for S, op, n in ((T.U1, A.add, "U1"), (T.S1, A.max, "S1")):
+                task("v", scan(S[:, bk], T.WW[:, bk], T.GP[:, bk], A.mult, op), 512, r=["WW%d" % j, "GP%d" % j], w=["%s%d" % (n, j)])
+        Ss = ["%s%d" % (h, j) for j in pieces for h in ("U1", "S1")]
+        part = [slice(256 * c0 + 128 * nc * h, 256 * c0 + 128 * nc * (h + 1)) for h in range(2)]
+        both = slice(256 * c0, 256 * c1)
+        last = [(T.U1, T.S1)[h][:, 1024 * c0:1024 * c1:8] for h in range(2)]
+        acc, accn = (T.AC, "AC") if x == 0 else (T.K0, "K0")
 
-    t = V_ - 1
-    for j in range(EARLY): prep(t, j)
-    for j in range(EARLY, 6): horner(j)
-    prep(t, EARLY)
-    hand_back(t - 1)
-    for j in range(6):
-        if j > EARLY: prep(t, j)
-        horner(j)
-    gather_parts(t - 1, False, True)
-    task("v", tt(T.YO[:, 0:L_], T.X0[:, 0:L_], T.U0[:, 7:3072:8], A.add), r=SOs + ["X0"], w=["YO0"], b=["X0"])
-    task("v", tt(T.YO[:, L_:768], T.X1[:, 0:L_], T.U1[:, 7:3072:8], A.add), r=SOs + ["X1"], w=["YO1"], b=["X1"])
-    cut = 16 * (V_ % 8)
-    task("y", [dma(T.ys[0:128 - cut, :], T.YO[cut:128, 0:L_]), dma(T.ys[128 - cut:128, :], T.YO[0:cut, 0:L_])], r=["YO0"], w=["ys"], dma=True)
-    task("s", [dma(T.ym[0:128 - cut, :], T.YO[cut:128, L_:768]), dma(T.ym[128 - cut:128, :], T.YO[0:cut, L_:768])], r=["YO1"], w=["ym"], dma=True)
-    task("y", [], r=["ys", "ym"])
-    emit(g, T, tasks)
+        def gather_part(s):
+            src, name = (T.XO[:, 0], "XO0%d" % x) if s == 0 else (T.XL[:, s - 1], "XL%d%d" % (s, x))
+            src = T.XO if s == 0 else T.XL
+            turn = 128 - 16 * (V_ - 1 - s)
+            if s == 0: task("t", mm(acc[:, 0:256 * nc], T.Z[:, 0:128], T.Z[:, 0:256 * nc], True, False), 256 * nc, r=["Z"], w=[accn], b=[accn])
+            for i in range(4 * nc):
+                task("t", mm(acc[:, 64 * i:64 * i + 64], T.I2[:, turn:turn + 128], src[:, max(s - 1, 0), 256 * c0 + 64 * i:256 * c0 + 64 * i + 64], False,
+                             s == V_ - 2 and i == 4 * nc - 1), 256, r=["I2", name], w=[accn], b=[accn])
+        if t < V_ - 1:
+            task("s", [act(T.XO[:, t, part[h]], last[h]) for h in range(2)], 2 * wide(128), r=Ss, w=["XO%d%d" % (t, x)])
+            if t:
+                sem = "x%d%d" % (t, x)
+                lands(sem, rank + t, ["XL%d%d" % (t, x)], send(T.XL[:, t - 1, both], T.XO[:, t, both], sem, rank - t, ["XO%d%d" % (t, x)]))
+            if x == 0: gather_part(t)
+        else:
+            if x:
+                for s in range(V_ - 1): gather_part(s)
+            task("v", [tt(T.YO[:, part[h]], acc[:, 128 * nc * h:128 * nc * (h + 1)], last[h], A.add) for h in range(2)], 2 * wide(128),
+                 r=Ss + [accn], w=[nm("YO")], b=[accn])
+            cut = 16 * (V_ % 8)
+            for e, y, h in (("y", T.ys, 0), ("s", T.ym, 1)):
+                load(e, [dma(y[0:128 - cut, lanes], T.YO[cut:128, part[h]]), dma(y[128 - cut:128, lanes], T.YO[0:cut, part[h]])], 64 * nc,
+                     r=[nm("YO")], w=["out%d%d" % (x, h)])
+
+    for t in range(V_):
+        for x in range(len(BATCHES)): visit(t, x)
+    task("y", [], 0, r=["out%d%d" % (x, h) for x in range(len(BATCHES)) for h in range(2)])
+    emit(g, T, arrange(tasks))
     g.wait_ge(T.sem.gone, sent[0])

@@ -1,10 +1,11 @@
+from concourse.bass import DstId, RemoteDMATransfer
 from concourse.mybir import AluOpType, ActivationFunctionType, AxisListType
 
 A = AluOpType
 F = ActivationFunctionType
 V_, L_, W_ = 5, 384, 4096
 f32, bf, f16, i32, u16 = "float32", "bfloat16", "float16", "int32", "uint16"
-BATCHES = ((0, 2), (2, 3))
+BATCHES = ((0, 1), (1, 2), (2, 3))
 SCRATCH = {
     "ar": ("sbuf", [128, W_], i32), "a0": ("sbuf", [128, W_], i32), "a1": ("sbuf", [128, 2, 512], i32),
     "U1": ("sbuf", [128, W_], f32), "TT": ("sbuf", [128, 2 * W_], f32), "MM": ("sbuf", [128, W_], f32), "pr": ("sbuf", [128, W_], bf),
@@ -14,14 +15,14 @@ SCRATCH = {
     "GP": ("sbuf", [128, 3072], bf), "WW": ("sbuf", [128, 3072], f32), "S1": ("sbuf", [128, 3072], f32),
     "sc": ("sbuf", [128, L_], f32), "nf": ("sbuf", [128, L_], bf), "UU": ("sbuf", [128, L_], bf), "UT": ("sbuf", [128, L_], bf),
     "MH": ("sbuf", [128, L_], bf), "sth": ("sbuf", [128, 192], f16), "ix2": ("sbuf", [128, 192], u16), "kb": ("sbuf", [128, L_], bf),
-    "k1": ("sbuf", [128, L_], f32), "DD": ("sbuf", [128, 24, 17], f16), "pen": ("sbuf", [128, L_], f32),
-    "SB": ("sbuf", [128, 24, 2, 2, 2, 2], f32), "KS": ("sbuf", [128, 24, 8], f32), "cb": ("sbuf", [128, 24, 8], bf), "zd": ("sbuf", [128, 49, 8], f16),
-    "Z": ("sbuf", [128, 1024], bf), "Zf": ("sbuf", [128, 256], f32), "I2": ("sbuf", [128, 256], f32), "If4": ("sbuf", [128, 128], f32),
-    "Ib": ("sbuf", [128, 3, 128], bf), "Ih": ("sbuf", [128, 4, 128], f16), "Db": ("sbuf", [128, 2, 64], bf), "Dh": ("sbuf", [128, 2, 64], f16),
+    "FF": ("sbuf", [128, L_], f16), "DD": ("sbuf", [128, 24, 17], f16), "pen": ("sbuf", [128, L_], f32), "AF": ("sbuf", [128, L_], f32),
+    "SB0": ("sbuf", [128, 24, 2, 2, 2, 2], f32), "SB1": ("sbuf", [128, 24, 2, 2, 2, 2], f32), "KS": ("sbuf", [128, 24, 8], f32), "cb": ("sbuf", [128, 24, 8], bf), "zd": ("sbuf", [128, 49, 8], f16),
+    "Z": ("sbuf", [128, 1024], bf), "Zf": ("sbuf", [128, 256], f32), "I2": ("sbuf", [128, 256], f32),
+    "Ib": ("sbuf", [128, 2, 128], bf), "Ih": ("sbuf", [128, 4, 128], f16), "Db": ("sbuf", [128, 2, 64], bf), "Dh": ("sbuf", [128, 2, 64], f16),
     "sD": ("sbuf", [128, 8, 128], bf), "sL": ("sbuf", [128, 8, 16], bf), "sP": ("sbuf", [128, 8, 2, 8], bf),
     "Bk": ("sbuf", [128, 9, 16], bf), "sM": ("sbuf", [128, 8, 16], bf), "sC": ("sbuf", [128, 8, 2], f32), "col": ("sbuf", [128, 8], f32),
     "Lh": ("sbuf", [128, 8, 16], bf), "Lm": ("sbuf", [128, 8, 8, 2], bf), "Lp": ("sbuf", [128, 2, 8, 2, 8], bf),
-    "p16": ("sbuf", [128, 256], f32), "pU": ("sbuf", [128, 256], bf),
+    "p16": ("sbuf", [128, 128], f32), "pU": ("sbuf", [128, 128], bf),
     "xi": ("sbuf", [128, V_, 192], u16), "xo": ("sbuf", [128, V_, 192], u16),
     "ri": ("sbuf", [128, V_, L_], bf), "ro": ("sbuf", [128, V_, L_], bf),
     "XO": ("sbuf", [128, 4, 768], f32), "XL": ("sbuf", [128, 3, 768], f32), "YO": ("sbuf", [128, 768], f32),
@@ -29,13 +30,57 @@ SCRATCH = {
     "D0": ("psum", [128, 512], f32), "D1": ("psum", [128, 512], f32), "AC": ("psum", [128, 512], f32),
     "S": ("psum", [128, 32, 2, 2, 2, 2], f32),
 }
-POOL = {"v": 30, "s": 28, "t": 28, "g": 21, "d": 20}
+POOL = {"v": 30, "s": 26, "t": 26, "g": 16, "d": 18}
 SEMAPHORES = (["%s%d" % (e, i) for e in POOL for i in range(POOL[e])] + ["gone"]
-              + ["%s%d%d" % (n, t, b) for n, k in (("m", 5), ("n", 5), ("x", 4)) for t in range(1, k) for b in range(2)])
+              + ["%s%d%d" % (n, t, b) for n, k in (("m", 5), ("n", 5), ("x", 4)) for t in range(1, k) for b in range(len(BATCHES))])
 LEAD = 0
-SLACK = 300
-STAG = 5
-HOP, LOCAL, REMOTE, GATHER = 110, 2600, 3200, 1.56
+SLACK = 0
+STAG = 0
+PASSES = 0
+CUT = 512
+FUSE = 0
+TLEAD = 1000
+HOP = 110
+REMOTE = 5500
+LOCAL, GATHER = 2600, 1.56
+
+
+ALL, REV = slice(None), slice(None, None, -1)
+
+
+def box(addrs, bits):
+    f = len(addrs).bit_length() - 1
+    free = [b for b in range(bits - 1, -1, -1) if any((a ^ addrs[0]) >> b & 1 for a in addrs)]
+    if len(free) != f: return None
+    for i, a in enumerate(addrs):
+        if a ^ addrs[0] != sum((i >> (f - 1 - n) & 1) << b for n, b in enumerate(free)): return None
+    return tuple((REV if addrs[0] >> b & 1 else ALL) if b in free else addrs[0] >> b & 1 for b in range(bits - 1, -1, -1))
+
+
+def network(steps, at):
+    if not steps: return []
+    (mask, kind), bits = steps[0], (3, 4)
+    pairs = [(w, w ^ mask) for w in at if w < w ^ mask]
+    f = len(pairs).bit_length() - 1
+    for fix in range(4):
+        side = [sorted(p, key=lambda w: (at[w][0], at[w][1] >> fix & 1)) for p in pairs]
+        order = sorted(range(len(pairs)), key=(lambda n: pairs[n][0]) if kind == "e" else (lambda n: at[side[n][0]][1]))
+        for key in range(f if kind == "s" else 1):
+            for pos in range(f + 1 if kind == "u" else f if kind == "s" else 1):
+                calls, new = [], {}
+                for mx in range(1 if kind == "m" else 2):
+                    for v in range(2 if kind == "s" else 1):
+                        part = [n for i, n in enumerate(order) if kind != "s" or i >> key & 1 == v]
+                        mem = {"b": 1 if mx else 0, "s": v}.get(kind, 1)
+                        out = [(i >> pos << pos + 1 | mx << pos | i & (1 << pos) - 1) if kind in "us" else i for i in range(len(part))]
+                        new.update((pairs[n][mx], (mem, o)) for n, o in zip(part, out))
+                        a, b = [(at[side[part[0]][h]][0], box([at[side[n][h]][1] for n in part], bits[at[side[part[0]][h]][0]])) for h in range(2)]
+                        ok = all(at[side[n][h]][0] == (a, b)[h][0] for n in part for h in range(2)) and a[0] + b[0] > 0
+                        calls.append((mx, (mem, box(out, bits[mem])), a, b, len(part)) if ok and a[1] and b[1] else None)
+                if None in calls: continue
+                rest = network(steps[1:], new)
+                if rest is not None: return [calls] + rest
+    return None
 
 
 def needs(tasks):
@@ -75,6 +120,42 @@ def arrange(tasks):
             ready[u] = max(ready[u], end + k["lat"] + HOP); left[u] -= 1
             if not left[u]: open_.append(u)
     return done
+
+
+def arrange2(tasks):
+    dep = needs(tasks)
+    for n, k in enumerate(tasks): dep[n].update(k["after"])
+    users = [set() for _ in tasks]
+    for n, d in enumerate(dep):
+        for m in d: users[m].add(n)
+
+    def place(order, before, forward):
+        busy, start = {}, {}
+        for n in order:
+            k = tasks[n]
+            t = max([start[m] + tasks[m]["c"] + tasks[m if forward else n]["lat"] + (0 if k["e"] == "t" == tasks[m]["e"] else HOP) for m in before[n]] + [0])
+            lines = [(k["e"], 0)] * (k["e"] != "x") + [(b, HOP) for b in k["b"]]
+            moved = True
+            while moved:
+                moved = False
+                for line, gap in lines:
+                    for a, b, e in busy.get(line, ()):
+                        if (not gap or e != k["e"]) and a - gap < t + k["c"] and t < b + gap:
+                            t, moved = b + gap, True
+            start[n] = t
+            for line, gap in lines: busy.setdefault(line, []).append((t, t + k["c"], k["e"]))
+        return start
+    way = {}
+    for n in range(len(tasks) - 1, -1, -1):
+        way[n] = tasks[n]["c"] + tasks[n]["lat"] + max([HOP + way[u] for u in users[n]] + [0])
+    order, best = sorted(way, key=lambda n: (-way[n] - tasks[n]["lead"], n)), None
+    for _ in range(PASSES):
+        start = place(order, dep, True)
+        end = max(start[n] + tasks[n]["c"] + tasks[n]["lat"] for n in start)
+        if best is None or end < best[0]: best = (end, start)
+        late = place(sorted(start, key=lambda n: (-start[n] - tasks[n]["c"] - tasks[n]["lat"], -n)), users, False)
+        order = sorted(late, key=lambda n: (-late[n] - tasks[n]["c"], n))
+    return [tasks[n] for n in sorted(best[1], key=lambda n: (best[1][n], n))]
 
 
 def emit(g, T, tasks):
@@ -149,7 +230,6 @@ def rank_program(g, core, T, topo):
     def paint(name, ap, n, pat, val, base, cm, src=None, op=A.not_equal):
         task("g", lambda q: q.affine_select(ap, ap if src is None else src, pat, op, val, base, cm), 200 + 2 * n, r=[name, "Z"], w=[name])
     def ch(j): return slice(512 * j, 512 * j + 512)
-    ALL, REV = slice(None), slice(None, None, -1)
     def back(a, b): return slice(b - 1, a - 1 if a else None, -1)
 
     for a, b in ((0, 1), (1, 2), (2, 4), (4, 6), (6, 8)):
@@ -165,10 +245,10 @@ def rank_program(g, core, T, topo):
     task("v", [ms(T.sD[64:66, 0:7, :], 0.0), ms(T.sD[64:66, 7, :], 512.0), ms(T.sD[0:64, 7, :], 0.0), ms(T.sL[64:66], -15.5),
                ms(T.ri[64:128, 0, :], 1.0), ms(T.Bk[:], 1.0), ms(T.sP[0:64], 0.0), ms(T.Lp[:], 0.0),
                ms(T.p16[:], 0.0), ms(T.pU[:], 0.0), ms(T.nf[:, 0:L_:128], 0.0)],
-         1700, w=["sDc", "sLc", "ri0c", "Bk", "sP", "sK0", "Lp", "p16", "pU", "nf0", "nf1"])
-    task("v", [ms(T.p16[:, 0:256:16], 1000.0), ms(T.pU[:, 15:256:16], -4.0), ms(T.pU[:, 0:256:16], 1.0)], 192, w=["p16", "pU"])
+         1700, w=["sDc", "sLc", "ri0c", "Bk", "sP", "sK0", "Lp", "p16", "pU", "nf"])
+    task("v", [ms(T.p16[:, 0:128:16], 1000.0), ms(T.pU[:, 15:128:16], -4.0), ms(T.pU[:, 0:128:16], 1.0)], 192, w=["p16", "pU"])
     task("v", [ms(T.sP[64:66], -25.0 / 64), cp(T.zd[:], T.Z[:, 0:392]), ts(T.DD[:, :, 0], T.Z[:, 0:24], -4096.0, A.add)],
-         450, r=["Z"], w=["sPc", "sK", "zd0", "zd1", "DD0", "DD1"])
+         450, r=["Z"], w=["sPc", "sK", "zd0", "zd1", "zd2", "DD0", "DD1", "DD2"])
     paint("I2", T.I2[:], 256, [[0, 2], [-1, 128]], 1.0, 0, 1, T.Zf[:])
     paint("sD", T.sD[0:64, 0:7, :], 896, [[-1, 7], [-8, 8], [0, 16]], 1.0, 0, 1, T.Z[0:64, 0:896])
     paint("sD", T.sD[0:64, 0:7, :], 896, [[-1, 7], [-8, 8], [0, 16]], -1.0, -1, 1)
@@ -188,8 +268,8 @@ def rank_program(g, core, T, topo):
     task("g", lambda q: q.iota(T.kb[:, 0:128], [[0, 8], [1, 16]], 0, 0, allow_small_or_imprecise_dtypes=True), 400, w=["kb0"])
     paint("Db", T.Db[:], 128, [[-1, 2], [-2, 64]], 4096.0, 0, 1, T.Z[:, 0:128])
     I1 = T.I2[:, 0:128]
-    task("s", [act(T.Ib[:, n, :], I1, scale=s) for n, s in enumerate((1.0, -4096.0, 2.0 ** -7))] + [act(T.If4[:], I1, scale=4096.0)], 512, r=["I2"], w=["Ib"])
-    task("v", [ts(T.Ih[:, n, :], I1, s, A.mult) for n, s in enumerate((1.0, -1.0, -4096.0, 2.0 ** -12))]
+    task("s", [act(T.Ib[:, n, :], I1, scale=s) for n, s in enumerate((1.0, 2.0 ** -7))], 256, r=["I2"], w=["Ib"])
+    task("v", [ts(T.Ih[:, n, :], I1, s, A.mult) for n, s in enumerate((1.0, -1.0, 4096.0, 2.0 ** -12))]
          + [red(T.col[:, u:u + 1], T.I2[:, u:128:2]) for u in range(2)] + [red(T.col[:, 2 + u:3 + u], T.I2[:, u:128:16]) for u in range(2)], 800, r=["I2"], w=["Ih", "col"])
     task("v", [ts(T.col[:, 4:5], T.col[:, 1:2], 8192.0, A.mult, -4096.0, A.add), ts(T.col[:, 6:7], T.col[:, 2:3], 6144.0, A.mult),
                ts(T.col[:, 7:8], T.col[:, 3:4], -2048.0, A.mult)], 192, r=["col"], w=["col4"])
@@ -198,33 +278,42 @@ def rank_program(g, core, T, topo):
     task("s", [act(T.sC[:, :, u], T.Bk[:, 0:8, 0], scale=T.col[:, u:u + 1]) for u in range(2)] + [act(T.sM[:], T.Bk[:, 0:8, :], scale=-1.0 / 128)]
          + [act(T.Lp[:, b, :, b, :], T.Bk[:, 1:9, 0:8], scale=T.col[:, 5:6]) for b in range(2)], 400, r=["Bk", "col", "col5", "Lp"], w=["sC", "Lp"])
     task("s", [act(T.ro[64:128, t, :], T.Z[64:128, 0:L_], bias=1.0) for t in range(V_)], V_ * L_, r=["Z"], w=["roc"])
-    task("t", [lambda q, c=c: q.transpose(T.AC[:, 128 * c:128 * c + 128], T.acs[:, 128 * c:128 * c + 128], I1) for c in range(3)], 1536,
-         r=["acs", "I2"], w=["AC"], b=["AC"])
-    task("s", act(T.acT[:], T.AC[:, 0:L_]), 384, r=["AC"], w=["acT"], b=["AC"])
     task("v", [cp(T.xi[:, 0, q2:192:8], T.sti[:, q2, :]) for q2 in range(8)] + [ts(T.ri[0:64, 0, :], T.rsi[0:64, :], -1.0, A.mult, 98.0, A.add)], 900,
-         r=["sti", "rsi", "ri0c"], w=["xi00", "xi01", "ri00", "ri01"])
+         r=["sti", "rsi", "ri0c"], w=["xi00", "xi01", "xi02", "ri00", "ri01", "ri02"])
 
     for j in range(8):
         n = ("D0", "D1", "M0", "M1")[j % 4]
+        lead[0] = TLEAD * (8 - j)
         task("v", [ts(T.a0[:, ch(j)], T.ar[:, ch(j)], 32767, A.bitwise_and), ts(T.a1[:, j % 2, :], T.ar[:, ch(j)], 15, A.logical_shift_right)], 1024,
              r=["ar%d" % j], w=["a0%d" % j, "a1%d" % (j % 2)])
         task("v", cp(T[n][:], T.a1[:, j % 2, :]), 512, r=["a1%d" % (j % 2)], w=[n], b=[n])
         task("v", tt(T.MM[:, ch(j)], T.a0[:, ch(j)], T[n][:], A.min), 512, r=[n, "a0%d" % j], w=["MM%d" % j], b=[n])
         task("s", [act(T.U1[:, ch(j)], T[n][:]), act(T.TT[:, ch(8 + j)], T[n][:])], 1024, r=[n], w=["U1%d" % j, "TU%d" % j], b=[n])
         task("v", cp(T.TT[:, ch(j)], T.a0[:, ch(j)]), 512, r=["a0%d" % j], w=["TT%d" % j])
+        U0, un = (T.WW, "WW") if j < 6 else (T.GA, "GA")
+        task("s", act(U0[:, ch(j % 6)], T.TT[:, ch(j)]), 512, r=["TT%d" % j], w=["%s%d" % (un, j % 6)])
         if j % 2:
             c, two = slice(512 * j - 512, 512 * j + 512), (j - 1, j)
-            load("y", [dma(T.TT[0:128:2, W_ + c.start:W_ + c.stop], T.TT[1:128:2, c])], 256, r=["TT%d" % i for i in two], w=["TU%d" % i for i in two])
-            load("y", [dma(T.TT[1:128:2, c], T.U1[0:128:2, c])], 256, r=["U1%d" % i for i in two], w=["TT%d" % i for i in two])
-    load("s", [dma(T.pr[16:128, :], T.pay[0:112, :]), dma(T.pr[0:16, :], T.pay[112:128, :])], 1024, r=["ar7"], w=["pr"])
+            load("y", [dma(T.TT[0:128:2, W_ + c.start:W_ + c.stop], U0[1:128:2, 512 * (j % 6) - 512:512 * (j % 6) + 512]), dma(T.TT[1:128:2, c], T.U1[0:128:2, c])], 512,
+                 r=["%s%d" % (un, i % 6) for i in two] + ["U1%d" % i for i in two], w=["T%s%d" % (h, i) for i in two for h in "TU"])
+    lead[0] = 0
+    task("t", [lambda q, c=c: q.transpose(T.AC[:, 128 * c:128 * c + 128], T.acs[:, 128 * c:128 * c + 128], I1) for c in range(3)], 1536,
+         r=["acs", "I2", "a05"], w=["AC"], b=["AC"])
+    task("s", act(T.acT[:], T.AC[:, 0:L_]), 384, r=["AC"], w=["acT"], b=["AC"])
+    load("y", [dma(T.pr[16:128, :], T.pay[0:112, :]), dma(T.pr[0:16, :], T.pay[112:128, :])], 1024, r=["TU7"], w=["pr"])
     MMs, TTs = ["MM%d" % j for j in range(8)], ["T%s%d" % (h, j) for j in range(8) for h in "TU"]
     sent = [0]
 
-    def send(out, src, sem, to, r):
+    def send(pairs, sem, to, r):
         dst = T.cores[to % N]
         rid, pid, _ = topo.addr(dst)
-        sent[0] += len(topo.engines(core, dst))
-        return task("g", lambda q: q.remote_dma(out, src, T.sem[sem], T.sem.gone, pid, rid, topo.mask(core, dst)), 300, r=r)
+        rest, moves = topo.engines(core, dst), []
+        sent[0] += len(rest)
+        for n, (out, src) in enumerate(pairs):
+            k = len(rest) if n == len(pairs) - 1 else len(rest) // 2
+            moves.append(RemoteDMATransfer(dst_ids=[DstId(rid=rid, pnc=pid)], dma_engine_mask=sum(1 << e for e in rest[:k]), remote_sem=T.sem[sem], src=src, dst=out))
+            rest = rest[k:]
+        return task("g", lambda q: q.remote_dma_fused(moves, local_sem=T.sem.gone), 300, r=r)
 
     def lands(sem, frm, w, like): arrival(sem, len(topo.engines(T.cores[frm % N], core)), w, like)
 
@@ -232,8 +321,7 @@ def rank_program(g, core, T, topo):
         task("t", [mm(T[n][:, k:512:8], T.sD[0:66, k, :], R[0:66, t, 64 * j:64 * j + 64]) for k in range(8)], 512,
              r=["sD", "sDc", "roc", name], w=[n], b=[n])
 
-    B4, B3 = [3, 2, 1, 0], [2, 1, 0]
-    EIGHT = [(0, 0), (1, 1), (0, 0), (2, 1), (1, 0), (0, 0), (3, 1)]
+    ALL16, BEST8 = [network(list(zip((1, 3, 1, 7, 2, 1, 15, 4, 2, 1), kinds)), {i: (i & 1, i >> 1) for i in range(16)}) for kinds in ("bubusbusue", "bubusbmuue")]
     UP = 128.5 + 2.0 ** -13
     SINK = 2 * (16 * 132 - 800) + 2047.0 / 4096
 
@@ -242,7 +330,8 @@ def rank_program(g, core, T, topo):
         lead[0] = LEAD * (1 - x)
         nc = c1 - c0
         cg, lg, lanes, cols = slice(8 * c0, 8 * c1), slice(0, 128 * nc), slice(128 * c0, 128 * c1), slice(64 * c0, 64 * c1)
-        K, M, Kn, Mn = T["K%d" % x], T["M%d" % x], "K%d" % x, "M%d" % x
+        Kn, Mn = ("K0", "K1", "D0")[x], ("M0", "M1", "AC")[x]
+        K, M = T[Kn], T[Mn]
         def nm(s): return "%s%d" % (s, x)
         xi, ri, xo, ro = ["%s%d%d" % (s, t, x) for s in ("xi", "ri", "xo", "ro")]
         def wide(n): return max(64, n * nc)
@@ -252,91 +341,74 @@ def rank_program(g, core, T, topo):
 
         task("v", ts(T.sth[:, cols], T.xi[:, t, cols], -2048.0, A.add), 64, r=[xi], w=[nm("sth")])
         for j in pieces:
-            n = (Mn, "D0" if x == 0 else Kn)[j % 2]
+            n = (Mn, "D0" if nc > 1 else Kn)[j % 2]
             spread(n, T.ri, t, ri, j)
             task("s", act(T.G[:, ch(j)], T.MM[:, 0:W_].indirect(T.xi[:, t, 32 * j:32 * j + 32]), bias=UP, scale=2.0 ** -12), 80 + 512 * GATHER,
-                 r=MMs + [xi] + ["GA3"] * (x and t < STAG), w=["G%d" % j])
+                 r=MMs + [xi] + ["GA%d" % (2 * c0 - 1)] * (x > 0 and t < STAG), w=["G%d" % j])
             bk = back(512 * j, 512 * j + 512)
-            task("v", scan(T.GS[:, bk], T[n][:, REV], T.G[:, bk], A.add, A.min), 512, r=[n, "G%d" % j], w=["GS%d" % j], b=[n])
-        GSs = ["GS%d" % j for j in pieces]
-        for c in chunks:
-            task("t", [mm(K[:, gc(c)], T.ri[0:66, t, lc(c)], T.sL[0:66], True, False),
-                       mm(K[:, gc(c)], T.GS[:, 1024 * c:1024 * c + 1024:8], T.Ib[:, 0, :], False, True)], 256,
-                 r=[ri, "sL", "sLc", "Ib", "GS%d" % (2 * c), "GS%d" % (2 * c + 1)], w=[Kn], b=[Kn])
-        task("v", tt(T.sc[:, lanes], K[:, lg], T.acT[:, lanes], A.add), wide(128), r=[Kn, "acT"], w=[nm("sc")], b=[Kn])
-        task("v", scan(M[:, lg], T.p16[:, lg], T.sc[:, lanes], A.add, A.min), wide(128), r=[nm("sc"), "p16"], w=[Mn], b=[Mn])
-        task("v", tt(T.nf[:, 128 * c0 + 1:128 * c1], M[:, 0:128 * nc - 1], T.sc[:, 128 * c0 + 1:128 * c1], A.is_gt), wide(128), r=[nm("sc"), Mn], w=[nm("nf")], b=[Mn])
-        bk = back(128 * c0, 128 * c1)
-        task("v", scan(T.UU[:, bk], T.pU[:, back(0, 128 * nc)], T.nf[:, bk], A.add, A.max), wide(64), r=[nm("nf"), "pU"], w=[nm("UU")])
-        task("t", [mm(K[:, gc(c)], T.UU[:, lc(c)], T.Ib[:, 0, :]) for c in chunks], 128 * nc, r=[nm("UU"), "Ib"], w=[Kn], b=[Kn])
-        task("s", act(T.UT[:, lanes], K[:, lg]), wide(128), r=[Kn], w=[nm("UT")], b=[Kn])
+            task("v", scan(T.GS[:, bk], T[n][:, REV], T.G[:, bk], A.add, A.min), 512, r=["G%d" % j], w=[n, "GS%d" % j], b=[n])
         half = slice(0, 64 * nc)
-        task("t", [mm(K[:, half], T.Ih[:, 0, :], T.sth[:, cols], True, False)]
-             + [mm(K[:, half], T.Lp[:, b], T.UT[:, 128 * c0 + b:128 * c1:2], False, b == 1) for b in range(2)], 192 * nc,
-             r=[nm("UT"), nm("sth"), "Lp", "Ih"], w=[Kn], b=[Kn])
-        task("v", cp(T.ix2[:, cols], K[:, half]), wide(64), r=[Kn], w=[nm("ix2")], b=[Kn])
-        one = slice(256, 256 + 128 * nc)
-        task("t", [mm(M[:, lg], T.Lm[:], T.UT[:, lanes]), mm(M[:, one], T.Lh[:], T.UT[:, lanes])], 256 * nc, r=[nm("UT"), "Lm", "Lh"], w=[Mn], b=[Mn])
-        task("v", tt(T.MH[:, lanes], M[:, one], T.GS[:, 1024 * c0:1024 * c1:8], A.mult), wide(128), r=[Mn] + GSs, w=[nm("MH")], b=[Mn])
-        for j in pieces:
-            task("s", act(T.GA[:, ch(j)], T.TT[:, 0:2 * W_].indirect(T.ix2[:, 32 * j:32 * j + 32])), 80 + 512 * GATHER, r=TTs + [nm("ix2")], w=["GA%d" % j])
         for c in chunks:
-            n = Kn if c == c0 else "D0"
+            d = c - c0
+            n = (Kn, "D0")[d]
+            B, Kc, Mc, GSs, GAs = T[n], "%sc%d" % (Kn, d), "%sc%d" % (Mn, d), ["GS%d" % (2 * c), "GS%d" % (2 * c + 1)], ["GA%d" % (2 * c), "GA%d" % (2 * c + 1)]
+            Bc, Bl, an = n + "c0", n + "l", n + "a"
+            def cn(s): return "%sc%d" % (s, c)
+            task("t", [mm(B[:, 0:128], T.ri[0:66, t, lc(c)], T.sL[0:66], True, False),
+                       mm(B[:, 0:128], T.GS[:, 1024 * c:1024 * c + 1024:8], T.Ib[:, 0, :], False, True)], 256, r=[ri, "sL", "sLc", "Ib", n] + GSs, w=[Bc], b=[n])
+            task("v", tt(B[:, 0:128], B[:, 0:128], T.acT[:, lc(c)], A.add), 128, r=[n, "acT"], w=[Bc], b=[n])
+            task("v", scan(T.sc[:, lc(c)], T.p16[:], B[:, 0:128], A.add, A.min), 128, r=[n, Bc, "p16"], w=[cn("sc")], b=[n])
+            task("v", tt(T.nf[:, 128 * c + 1:128 * c + 128], T.sc[:, 128 * c:128 * c + 127], B[:, 1:128], A.is_gt), 128, r=[n, Bc, cn("sc"), "nf"], w=[cn("nf")], b=[n])
+            bk = back(128 * c, 128 * c + 128)
+            task("v", scan(T.UU[:, bk], T.pU[:, REV], T.nf[:, bk], A.add, A.max), 64, r=[cn("nf"), "pU"], w=[cn("UU")])
+            task("t", mm(B[:, 0:128], T.UU[:, lc(c)], T.Ib[:, 0, :]), 128, r=[n, cn("UU"), "Ib"], w=[Bc], b=[n])
+            task("s", act(T.UT[:, lc(c)], B[:, 0:128]), 128, r=[n, Bc], w=[cn("UT")], b=[n])
+            li, one = slice(256, 320), slice(256 + 128 * d, 384 + 128 * d)
+            task("t", [mm(B[:, li], T.Ih[:, 0, :], T.sth[:, 64 * c:64 * c + 64], True, False)]
+                 + [mm(B[:, li], T.Lp[:, b], T.UT[:, 128 * c + b:128 * c + 128:2], False, b == 1) for b in range(2)], 192,
+                 r=[n, cn("UT"), nm("sth"), "Lp", "Ih"], w=[Bl], b=[n])
+            task("v", cp(T.ix2[:, 64 * c:64 * c + 64], B[:, li]), 64, r=[n, Bl], w=[cn("ix2")], b=[n])
+            task("t", [mm(M[:, gc(c)], T.Lm[:], T.UT[:, lc(c)]), mm(M[:, one], T.Lh[:], T.UT[:, lc(c)])], 256, r=[Mn, cn("UT"), "Lm", "Lh"], w=[Mc], b=[Mn])
+            task("v", tt(T.MH[:, lc(c)], M[:, one], T.GS[:, 1024 * c:1024 * c + 1024:8], A.mult), 128, r=[Mn, Mc] + GSs, w=[cn("MH")], b=[Mn])
+            for j in (2 * c, 2 * c + 1):
+                task("s", act(T.GA[:, ch(j)], T.TT[:, 0:2 * W_].indirect(T.ix2[:, 32 * j:32 * j + 32])), 80 + 512 * GATHER, r=TTs + [cn("ix2")], w=["GA%d" % j])
             for h in range(2):
                 ks = range(4 * h, 4 * h + 4)
                 ga = [T.GA[:, 1024 * c + k:1024 * c + 1024:8] for k in range(8)]
-                task("v", [tt(ga[k], M[:, gc(c)], ga[k], A.mult) for k in ks], 512, r=[Mn, "GA%d" % (2 * c), "GA%d" % (2 * c + 1)], w=["GB%d%d" % (c, h)], b=[Mn])
-                task("t", [mm(T[n][:, 256 + k:384:8], ga[k], T.sC[:]) for k in ks], 1024,
-                     r=["sC", "GB%d%d" % (c, h), "GA%d" % (2 * c), "GA%d" % (2 * c + 1)], w=[n], b=[n])
-            task("s", [act(T.kb[:, lc(c)], T[n][:, 256:384], bias=UP, scale=2.0 ** -12), act(T.pen[:, lc(c)], T[n][:, 256:384], bias=129 * 4096.0 - 2048)], 256,
-                 r=[n], w=["kb%d" % c, nm("pen")], b=[n])
-            task("t", [mm(K[:, gc(c)], I1, T.pen[:, lc(c)], True, False)] + [mm(K[:, gc(c)], T.Ib[:, i, :], T.kb[:, lc(c)], False, False) for i in (1, 2)]
-                 + [mm(K[:, gc(c)], T.ri[0:66, t, lc(c)], T.sP[0:66], False, False), mm(K[:, gc(c)], T.MH[:, lc(c)], T.sM[:], False, True)], 1024,
-                 r=["kb%d" % c, nm("pen"), nm("MH"), ri, "sP", "sPc", "sC", "Ib", "I2"], w=[Kn], b=[Kn])
-        task("s", act(T.SB[:, cg, 0], K[:, 1:128 * nc:2]), wide(64), r=[Kn], w=[nm("so0")], b=[Kn])
+                task("v", [tt(ga[k], M[:, gc(c)], ga[k], A.mult) for k in ks], 512, r=[Mn, Mc] + GAs, w=["GB%d%d" % (c, h)], b=[Mn])
+                task("t", [mm(T[n][:, 384 + k:512:8], ga[k], T.sC[:]) for k in ks], 1024, r=[n, "sC", "GB%d%d" % (c, h)] + GAs, w=[an], b=[n])
+            task("s", act(T.kb[:, lc(c)], B[:, 384:512], bias=UP, scale=2.0 ** -12), 128, r=[n, an], w=["kb%d" % c], b=[n])
+            task("s", act(T.AF[:, lc(c)], T.kb[:, lc(c)], bias=2048 - 129 * 4096.0, scale=4096.0), 128, r=["kb%d" % c], w=[cn("AF")])
+            task("v", tt(T.FF[:, lc(c)], B[:, 384:512], T.AF[:, lc(c)], A.subtract), 128, r=[n, an, cn("AF")], w=[cn("FF")], b=[n])
+            task("t", [mm(K[:, gc(c)], T.ri[0:66, t, lc(c)], T.sP[0:66], True, False), mm(K[:, gc(c)], T.MH[:, lc(c)], T.sM[:], False, False),
+                       mm(K[:, gc(c)], T.Ib[:, 1, :], T.kb[:, lc(c)], False, False), mm(K[:, gc(c)], T.Ih[:, 0, :], T.FF[:, lc(c)], False, True)], 512,
+                 r=[Kn, "kb%d" % c, cn("FF"), cn("MH"), ri, "sP", "sPc", "sC", "Ib", "Ih"], w=[Kc], b=[Kn])
+        task("s", act(T.SB0[:, cg, 0], K[:, 1:128 * nc:2]), wide(64), r=["%sc%d" % (Kn, d) for d in range(nc)], w=[nm("so0"), Kn], b=[Kn])
 
-        def side(mem, pp, dims, fix, rev=()):
-            ix = [0] * (3 - len(dims)) + [fix[d] if d in fix else REV if d in rev else ALL for d in dims]
-            return (T.S if mem == 0 else T.SB)[(ALL, cg, pp) + tuple(ix)]
+        def view(pp, place): return T.S[(ALL, cg, pp) + place[1]] if place[0] == 0 else (T.SB0, T.SB1)[pp][(ALL, cg) + place[1]]
 
-        def layer(pp, allbits, s, flip, nxt, only_min=False, first=False):
-            din = [d for d in allbits if d != s]
-            dout = [d for d in allbits if d != nxt and not (only_min and d == s)]
-            low = [d for d in din if d < s] if flip else []
-            f = []
-            for mx in range(1 if only_min else 2):
-                for v in range(2):
-                    o = 1 - v if nxt in low else v
-                    a = K[:, 2 * v:128 * nc:4] if first else side(0, pp, din, {nxt: o if mx else v}, low if mx else ())
-                    b = side(1, pp, din, {nxt: v if mx else o}, () if mx else low)
-                    f.append(tt(side(v, 1 - pp, dout, {s: mx}), a, b, A.max if mx else A.min))
-            task("v", f, len(f) * wide(2 ** (len(allbits) + 1)), r=[nm("so%d" % pp)] + [Kn] * first, w=[nm("so%d" % (1 - pp))], b=["S"] + [Kn] * first)
-
-        def network(steps, first=False):
-            pp = 0
-            for n in range(len(steps) - 1):
-                layer(pp, B4, steps[n][0], steps[n][1], steps[n + 1][0], first=first and n == 0); pp = 1 - pp
-            return pp
-        pp = network(EIGHT + [(2, 0), (1, 0), (0, 0)], True)
-        task("v", [tt(T.k1[:, 128 * c0 + mx:128 * c1:2], side(0, pp, [3, 2, 1], {}), side(1, pp, [3, 2, 1], {}), A.max if mx else A.min) for mx in range(2)], 2 * wide(64),
-             r=[nm("so%d" % pp)], w=[nm("k1")], b=["S"])
-        task("v", ts(T.DD[:, cg, 1:17], T.k1[:, lanes], 1.5 * 2 ** 23, A.add, 1.5 * 2 ** 23, A.subtract), wide(128), r=[nm("k1")], w=[nm("DD")])
-        task("t", mm(M[:, lg], T.If4[:], T.k1[:, lanes], True, False), 512 * nc, r=[nm("k1"), "Ib"], w=[Mn], b=[Mn])
+        def sort(steps, first, last, w, b):
+            for n, calls in enumerate(steps):
+                pp, head, end = n % 2, n == 0 and first is not None, n == len(steps) - 1
+                task("v", [tt(last(mx) if end else view(1 - pp, o), first if head else view(pp, i0), view(pp, i1), A.max if mx else A.min) for mx, o, i0, i1, _ in calls],
+                     sum(max(64, 8 * nc * k * (i0[0] + i1[0])) for _, _, i0, i1, k in calls), r=[nm("so%d" % pp)] + [Kn] * head,
+                     w=w if end else [nm("so%d" % (1 - pp))], b=["S"] + [Kn] * head + b * end)
+        FFs = ["FFc%d" % c for c in chunks]
+        sort(ALL16, K[:, 0:128 * nc:2], lambda mx: M[:, 256 + mx:256 + 128 * nc:2], [Mn], [Mn])
+        k1 = M[:, 256:256 + 128 * nc]
+        task("v", ts(T.DD[:, cg, 1:17], k1, 1.5 * 2 ** 23, A.add, 1.5 * 2 ** 23, A.subtract), wide(128), r=[Mn], w=[nm("DD")], b=[Mn])
+        task("v", tt(T.FF[:, lanes], k1, T.DD[:, cg, 1:17], A.subtract), wide(128), r=[Mn, nm("DD")], w=FFs, b=[Mn])
         task("t", [mm(K[:, lg], T.Ih[:, 0, :], T.DD[:, cg, 0:16], True, False), mm(K[:, lg], T.Ih[:, 1, :], T.DD[:, cg, 1:17], False, True)], 256 * nc,
              r=[nm("DD"), "Ih"], w=[Kn], b=[Kn])
-        task("t", [mm(M[:, lg], T.Ih[:, n, :], T.DD[:, cg, 1:17], False, n == 3) for n in (2, 3)], 256 * nc, r=[nm("DD"), "Ih"], w=[Mn], b=[Mn])
+        task("t", [mm(M[:, lg], T.Ih[:, 3, :], T.DD[:, cg, 1:17], True, False), mm(M[:, lg], T.Ih[:, 2, :], T.FF[:, lanes], False, True)], 256 * nc,
+             r=[nm("DD"), "Ih"] + FFs, w=[Mn], b=[Mn])
         task("s", act(T.pen[:, lanes], K[:, lg], bias=SINK, scale=8192.0), wide(128), r=[Kn], w=[nm("pen")], b=[Kn])
-        task("v", [tt(side(v, 0, [3, 2, 1], {}), M[:, v:128 * nc:2], T.pen[:, 128 * c0 + v:128 * c1:2], A.max) for v in range(2)], 2 * wide(64),
+        task("v", [tt((T.S, T.SB0)[v][:, cg, 0], M[:, v:128 * nc:2], T.pen[:, 128 * c0 + v:128 * c1:2], A.max) for v in range(2)], 2 * wide(64),
              r=[Mn, nm("pen")], w=[nm("so0")], b=[Mn, "S"])
-        pp = network(EIGHT)
-        layer(pp, B4, 3, 1, 2, only_min=True); pp = 1 - pp
-        layer(pp, B3, 2, 0, 1); pp = 1 - pp
-        layer(pp, B3, 1, 0, 0); pp = 1 - pp
-        task("v", [tt(T.KS[:, cg, mx:8:2], side(0, pp, [2, 1], {}), side(1, pp, [2, 1], {}), A.max if mx else A.min) for mx in range(2)], 2 * wide(32),
-             r=[nm("so%d" % pp)], w=[nm("KS")], b=["S"])
-        task("v", ts(T.S[:, cg, 1 - pp], T.KS[:, cg], 1.5 * 2 ** 24, A.add, 1.5 * 2 ** 24, A.subtract), wide(64), r=[nm("KS")], w=[nm("so%d" % (1 - pp))], b=["S"])
-        task("v", tt(T.zd[:, 16 * c0 + 1:16 * c1 + 1:2, :], T.KS[:, cg], T.S[:, cg, 1 - pp], A.subtract), wide(64),
-             r=[nm("KS"), nm("so%d" % (1 - pp))], w=[nm("zd")], b=["S"])
+        sort(BEST8, None, lambda mx: T.KS[:, cg, mx:8:2], [nm("KS")], [])
+        task("v", ts(T.S[:, cg, 0], T.KS[:, cg], 1.5 * 2 ** 24, A.add, 1.5 * 2 ** 24, A.subtract), wide(64), r=[nm("KS")], w=[nm("so0")], b=["S"])
+        task("v", tt(T.zd[:, 16 * c0 + 1:16 * c1 + 1:2, :], T.KS[:, cg], T.S[:, cg, 0], A.subtract), wide(64),
+             r=[nm("KS"), nm("so0")], w=[nm("zd")], b=["S"])
         task("s", act(T.cb[:, cg], T.KS[:, cg], bias=180 - 15.0 / 32, scale=1.0 / 32), wide(64), r=[nm("KS")], w=[nm("cb")])
         task("t", [mm(K[:, 64 * (c - c0):64 * (c - c0) + 64], T.zd[:, 16 * c + 1 - b:16 * c + 17 - b, :], T.Dh[:, b, :], b == 0, b == 1)
                    for c in chunks for b in range(2)], 128 * nc, r=[nm("zd"), "Dh"], w=[Kn], b=[Kn])
@@ -345,8 +417,13 @@ def rank_program(g, core, T, topo):
         task("s", act(T.ro[0:64, t, lanes], M[0:64, lg], F.Abs, bias=-228.0), wide(128), r=[Mn], w=[ro], b=[Mn])
         if t < V_ - 1:
             sem = "%d%d" % (t + 1, x)
-            lands("m" + sem, rank - 1, ["xi" + sem], send(T.xi[:, t + 1, cols], T.xo[:, t, cols], "m" + sem, rank + 1, [xo]))
-            lands("n" + sem, rank - 1, ["ri" + sem], send(T.ri[:, t + 1, lanes], T.ro[:, t, lanes], "n" + sem, rank + 1, [ro, "roc"]))
+            mid = 64 * (c0 + c1)
+            pairs = [(T.xi[:, t + 1, cols], T.xo[:, t, cols])] + [(T.ri[:, t + 1, a:b], T.ro[:, t, a:b]) for a, b in ((128 * c0, mid), (mid, 128 * c1))]
+            if FUSE:
+                lands("m" + sem, rank - 1, ["xi" + sem, "ri" + sem], send(pairs, "m" + sem, rank + 1, [xo, ro, "roc"]))
+            else:
+                lands("m" + sem, rank - 1, ["xi" + sem], send(pairs[:1], "m" + sem, rank + 1, [xo]))
+                lands("n" + sem, rank - 1, ["ri" + sem], send([(T.ri[:, t + 1, lanes], T.ro[:, t, lanes])], "n" + sem, rank + 1, [ro, "roc"]))
 
         lead[0] = 0
         for j in pieces:
@@ -355,32 +432,31 @@ def rank_program(g, core, T, topo):
             task("s", act(T.WW[:, ch(j)], T.D1[:], F.Exp, scale=-0.125), 512, r=["D1", "roc"], w=["WW%d" % j], b=["D1"])
             bk = back(512 * j, 512 * j + 512)
             for S, op, n in ((T.U1, A.add, "U1"), (T.S1, A.max, "S1")):
-                task("v", scan(S[:, bk], T.WW[:, bk], T.GP[:, bk], A.mult, op), 512, r=["WW%d" % j, "GP%d" % j], w=["%s%d" % (n, j)])
+                task("v", [scan(S[:, b2], T.WW[:, b2], T.GP[:, b2], A.mult, op) for b2 in [back(512 * j + i, 512 * j + i + CUT) for i in range(0, 512, CUT)]], 512,
+                     r=["WW%d" % j, "GP%d" % j], w=["%s%d" % (n, j)])
         Ss = ["%s%d" % (h, j) for j in pieces for h in ("U1", "S1")]
         part = [slice(256 * c0 + 128 * nc * h, 256 * c0 + 128 * nc * (h + 1)) for h in range(2)]
         both = slice(256 * c0, 256 * c1)
         last = [(T.U1, T.S1)[h][:, 1024 * c0:1024 * c1:8] for h in range(2)]
-        acc, accn = (T.AC, "AC") if x == 0 else (T.K0, "K0")
+        def turned(s): return T.I2[:, 128 - 16 * (V_ - 1 - s):256 - 16 * (V_ - 1 - s)]
 
-        def gather_part(s):
-            src, name = (T.XO[:, 0], "XO0%d" % x) if s == 0 else (T.XL[:, s - 1], "XL%d%d" % (s, x))
-            src = T.XO if s == 0 else T.XL
-            turn = 128 - 16 * (V_ - 1 - s)
-            if s == 0: task("t", mm(acc[:, 0:256 * nc], T.Z[:, 0:128], T.Z[:, 0:256 * nc], True, False), 256 * nc, r=["Z"], w=[accn], b=[accn])
-            for i in range(4 * nc):
-                task("t", mm(acc[:, 64 * i:64 * i + 64], T.I2[:, turn:turn + 128], src[:, max(s - 1, 0), 256 * c0 + 64 * i:256 * c0 + 64 * i + 64], False,
-                             s == V_ - 2 and i == 4 * nc - 1), 256, r=["I2", name], w=[accn], b=[accn])
+        def add_part(s, n):
+            for i in range(2):
+                cs = slice(256 * c0 + 128 * i, 256 * c0 + 128 * i + 128)
+                task("t", [mm(T[n][:, 128 * i:128 * i + 128], turned(0 if s == 1 else V_ - 1), T.XO[:, 0, cs], True, False),
+                           mm(T[n][:, 128 * i:128 * i + 128], turned(s), T.XL[:, s - 1, cs], False, True)], 1024,
+                     r=["I2", "XO0%d" % x, "XL%d%d" % (s, x)], w=[n], b=[n])
         if t < V_ - 1:
             task("s", [act(T.XO[:, t, part[h]], last[h]) for h in range(2)], 2 * wide(128), r=Ss, w=["XO%d%d" % (t, x)])
             if t:
                 sem = "x%d%d" % (t, x)
-                lands(sem, rank + t, ["XL%d%d" % (t, x)], send(T.XL[:, t - 1, both], T.XO[:, t, both], sem, rank - t, ["XO%d%d" % (t, x)]))
-            if x == 0: gather_part(t)
-        else:
-            if x:
-                for s in range(V_ - 1): gather_part(s)
-            task("v", [tt(T.YO[:, part[h]], acc[:, 128 * nc * h:128 * nc * (h + 1)], last[h], A.add) for h in range(2)], 2 * wide(128),
-                 r=Ss + [accn], w=[nm("YO")], b=[accn])
+                lands(sem, rank + t, ["XL%d%d" % (t, x)], send([(T.XL[:, t - 1, both], T.XO[:, t, both])], sem, rank - t, ["XO%d%d" % (t, x)]))
+        if 2 <= t < V_ - 1:
+            add_part(t - 1, "D1")
+            task("s", act(T.XO[:, 0, both], T.D1[:, 0:256]), 256, r=["D1"], w=["XO0%d" % x], b=["D1"])
+        if t == V_ - 1:
+            add_part(t - 1, Kn)
+            task("v", [tt(T.YO[:, part[h]], K[:, 128 * h:128 * h + 128], last[h], A.add) for h in range(2)], 256, r=Ss + [Kn], w=[nm("YO")], b=[Kn])
             cut = 16 * (V_ % 8)
             for e, y, h in (("y", T.ys, 0), ("s", T.ym, 1)):
                 load(e, [dma(y[0:128 - cut, lanes], T.YO[cut:128, part[h]]), dma(y[128 - cut:128, lanes], T.YO[0:cut, part[h]])], 64 * nc,
@@ -389,5 +465,5 @@ def rank_program(g, core, T, topo):
     for t in range(V_):
         for x in range(len(BATCHES)): visit(t, x)
     task("y", [], 0, r=["out%d%d" % (x, h) for x in range(len(BATCHES)) for h in range(2)])
-    emit(g, T, arrange(tasks))
+    emit(g, T, (arrange2 if PASSES else arrange)(tasks))
     g.wait_ge(T.sem.gone, sent[0])

@@ -3,9 +3,8 @@ from concourse.mybir import AluOpType, ActivationFunctionType, AxisListType
 
 A = AluOpType
 F = ActivationFunctionType
-V_, L_, W_ = 5, 384, 4096
+V_, L_, W_, NB = 5, 384, 4096, 3
 f32, bf, f16, i32, u16 = "float32", "bfloat16", "float16", "int32", "uint16"
-BATCHES = ((0, 1), (1, 2), (2, 3))
 SCRATCH = {
     "ar": ("sbuf", [128, W_], i32), "a0": ("sbuf", [128, W_], i32), "a1": ("sbuf", [128, 2, 512], i32),
     "U1": ("sbuf", [128, W_], f32), "TT": ("sbuf", [128, 2 * W_], f32), "MM": ("sbuf", [128, W_], f32), "pr": ("sbuf", [128, W_], bf),
@@ -13,38 +12,38 @@ SCRATCH = {
     "rsi": ("sbuf", [128, L_], i32), "sti": ("sbuf", [128, 8, 24], i32), "std": ("dram", [8, 8, 2, 8, 24], i32),
     "G": ("sbuf", [128, 3072], bf), "GS": ("sbuf", [128, 3072], bf), "GA": ("sbuf", [128, 3072], f32),
     "GP": ("sbuf", [128, 3072], bf), "WW": ("sbuf", [128, 3072], f32), "S1": ("sbuf", [128, 3072], f32),
-    "sc": ("sbuf", [128, L_], f32), "nf": ("sbuf", [128, L_], bf), "UU": ("sbuf", [128, L_], bf), "UT": ("sbuf", [128, L_], bf),
+    "sc": ("sbuf", [128, L_], f32), "UU": ("sbuf", [128, L_], bf), "UT": ("sbuf", [128, L_], bf),
     "MH": ("sbuf", [128, L_], bf), "sth": ("sbuf", [128, 192], f16), "ix2": ("sbuf", [128, 192], u16), "kb": ("sbuf", [128, L_], bf),
-    "FF": ("sbuf", [128, L_], f16), "DD": ("sbuf", [128, 24, 17], f16), "pen": ("sbuf", [128, L_], f32), "AF": ("sbuf", [128, L_], f32),
-    "SB0": ("sbuf", [128, 24, 2, 2, 2, 2], f32), "SB1": ("sbuf", [128, 24, 2, 2, 2, 2], f32), "KS": ("sbuf", [128, 24, 8], f32), "cb": ("sbuf", [128, 24, 8], bf), "zd": ("sbuf", [128, 49, 8], f16),
-    "Z": ("sbuf", [128, 1024], bf), "Zf": ("sbuf", [128, 256], f32), "I2": ("sbuf", [128, 256], f32),
-    "Ib": ("sbuf", [128, 2, 128], bf), "Ih": ("sbuf", [128, 4, 128], f16), "Db": ("sbuf", [128, 2, 64], bf), "Dh": ("sbuf", [128, 2, 64], f16),
+    "k1": ("sbuf", [128, L_], f32), "DD": ("sbuf", [128, 24, 17], f16), "pen": ("sbuf", [128, L_], f32), "AF": ("sbuf", [128, L_], f32),
+    "SB0": ("sbuf", [128, 24, 2, 2, 2, 2], f32), "SB1": ("sbuf", [128, 24, 2, 2, 2, 2], f32),
+    "kz": ("sbuf", [128, 49, 8], f32), "tz": ("sbuf", [128, 49, 8], f32), "cb": ("sbuf", [128, 24, 8], bf),
+    "Z": ("sbuf", [128, 896], bf), "Zf": ("sbuf", [128, 256], f32), "I2": ("sbuf", [128, 256], f32), "I4": ("sbuf", [128, 128], f32),
+    "Ib": ("sbuf", [128, 3, 128], bf), "Ih": ("sbuf", [128, 4, 128], f16), "Df": ("sbuf", [128, 2, 2, 64], f32),
     "sD": ("sbuf", [128, 8, 128], bf), "sL": ("sbuf", [128, 8, 16], bf), "sP": ("sbuf", [128, 8, 2, 8], bf),
     "Bk": ("sbuf", [128, 9, 16], bf), "sM": ("sbuf", [128, 8, 16], bf), "sC": ("sbuf", [128, 8, 2], f32), "col": ("sbuf", [128, 8], f32),
-    "Lh": ("sbuf", [128, 8, 16], bf), "Lm": ("sbuf", [128, 8, 8, 2], bf), "Lp": ("sbuf", [128, 2, 8, 2, 8], bf),
-    "p16": ("sbuf", [128, 128], f32), "pU": ("sbuf", [128, 128], bf),
+    "Lh": ("sbuf", [128, 8, 16], bf), "Lm": ("sbuf", [128, 8, 8, 2], bf), "Lp": ("sbuf", [128, 2, 8, 2, 8], bf), "p16": ("sbuf", [128, 128], f32),
     "xi": ("sbuf", [128, V_, 192], u16), "xo": ("sbuf", [128, V_, 192], u16),
     "ri": ("sbuf", [128, V_, L_], bf), "ro": ("sbuf", [128, V_, L_], bf),
     "XO": ("sbuf", [128, 4, 768], f32), "XL": ("sbuf", [128, 3, 768], f32), "YO": ("sbuf", [128, 768], f32),
     "K0": ("psum", [128, 512], f32), "M0": ("psum", [128, 512], f32), "K1": ("psum", [128, 512], f32), "M1": ("psum", [128, 512], f32),
-    "D0": ("psum", [128, 512], f32), "D1": ("psum", [128, 512], f32), "AC": ("psum", [128, 512], f32),
+    "K2": ("psum", [128, 512], f32), "M2": ("psum", [128, 512], f32), "D": ("psum", [128, 512], f32),
     "S": ("psum", [128, 32, 2, 2, 2, 2], f32),
 }
 POOL = {"v": 30, "s": 26, "t": 26, "g": 16, "d": 18}
 SEMAPHORES = (["%s%d" % (e, i) for e in POOL for i in range(POOL[e])] + ["gone"]
-              + ["%s%d%d" % (n, t, b) for n, k in (("m", 5), ("n", 5), ("x", 4)) for t in range(1, k) for b in range(len(BATCHES))])
-LEAD = 0
+              + ["%s%d%d" % (n, t, b) for n, k in (("m", 5), ("n", 5), ("x", 4)) for t in range(1, k) for b in range(NB)])
 SLACK = 0
-STAG = 0
-PASSES = 0
-CUT = 512
-FUSE = 0
+GATE = ("kb2", "kb2", "kb2")
+DEFER = 4
+LATE = (0, 0, 0)
+LEND = 3
 TLEAD = 1000
-HOP = 110
-REMOTE = 5500
+CUT = 256
+HOP = 230
+REMOTE = 2500
+ISSUE = 300
+PEF = 0.5
 LOCAL, GATHER = 2600, 1.56
-
-
 ALL, REV = slice(None), slice(None, None, -1)
 
 
@@ -99,9 +98,10 @@ def arrange(tasks):
     dep = needs(tasks)
     for n, k in enumerate(tasks): dep[n].update(k["after"])
     n_ = len(tasks)
+    def hop(a, b): return 0 if tasks[a]["e"] == tasks[b]["e"] == "t" or tasks[b]["e"] == "x" else HOP
     way, users = [0] * n_, [[] for _ in tasks]
     for n in range(n_ - 1, -1, -1):
-        way[n] = tasks[n]["c"] + tasks[n]["lat"] + max([HOP + way[u] for u in users[n]] + [0])
+        way[n] = tasks[n]["c"] + tasks[n]["lat"] + max([hop(n, u) + way[u] for u in users[n]] + [0])
         for m in dep[n]: users[m].append(n)
     left, ready, done = [len(d) for d in dep], [0] * n_, []
     free, bank, open_ = {}, {}, [n for n in range(n_) if not dep[n]]
@@ -117,45 +117,9 @@ def arrange(tasks):
         for b in k["b"]: bank.setdefault(b, {})[k["e"]] = end
         open_.remove(n); done.append(k)
         for u in users[n]:
-            ready[u] = max(ready[u], end + k["lat"] + HOP); left[u] -= 1
+            ready[u] = max(ready[u], end + k["lat"] + hop(n, u)); left[u] -= 1
             if not left[u]: open_.append(u)
     return done
-
-
-def arrange2(tasks):
-    dep = needs(tasks)
-    for n, k in enumerate(tasks): dep[n].update(k["after"])
-    users = [set() for _ in tasks]
-    for n, d in enumerate(dep):
-        for m in d: users[m].add(n)
-
-    def place(order, before, forward):
-        busy, start = {}, {}
-        for n in order:
-            k = tasks[n]
-            t = max([start[m] + tasks[m]["c"] + tasks[m if forward else n]["lat"] + (0 if k["e"] == "t" == tasks[m]["e"] else HOP) for m in before[n]] + [0])
-            lines = [(k["e"], 0)] * (k["e"] != "x") + [(b, HOP) for b in k["b"]]
-            moved = True
-            while moved:
-                moved = False
-                for line, gap in lines:
-                    for a, b, e in busy.get(line, ()):
-                        if (not gap or e != k["e"]) and a - gap < t + k["c"] and t < b + gap:
-                            t, moved = b + gap, True
-            start[n] = t
-            for line, gap in lines: busy.setdefault(line, []).append((t, t + k["c"], k["e"]))
-        return start
-    way = {}
-    for n in range(len(tasks) - 1, -1, -1):
-        way[n] = tasks[n]["c"] + tasks[n]["lat"] + max([HOP + way[u] for u in users[n]] + [0])
-    order, best = sorted(way, key=lambda n: (-way[n] - tasks[n]["lead"], n)), None
-    for _ in range(PASSES):
-        start = place(order, dep, True)
-        end = max(start[n] + tasks[n]["c"] + tasks[n]["lat"] for n in start)
-        if best is None or end < best[0]: best = (end, start)
-        late = place(sorted(start, key=lambda n: (-start[n] - tasks[n]["c"] - tasks[n]["lat"], -n)), users, False)
-        order = sorted(late, key=lambda n: (-late[n] - tasks[n]["c"], n))
-    return [tasks[n] for n in sorted(best[1], key=lambda n: (best[1][n], n))]
 
 
 def emit(g, T, tasks):
@@ -209,7 +173,7 @@ def rank_program(g, core, T, topo):
 
     def task(e, f, c, r=(), w=(), b=(), dma=0):
         f = f if isinstance(f, list) else [f]
-        tasks.append({"e": e, "f": f, "r": list(r), "w": list(w), "b": list(b), "dma": dma > 0, "c": c, "lat": dma, "after": [], "lead": lead[0]})
+        tasks.append({"e": e, "f": f, "r": list(r), "w": list(w), "b": list(b), "dma": dma > 0, "c": c * PEF if e == "t" else c, "lat": dma, "after": [], "lead": lead[0]})
         return len(tasks) - 1
 
     def arrival(sem, val, w, like):
@@ -231,6 +195,7 @@ def rank_program(g, core, T, topo):
         task("g", lambda q: q.affine_select(ap, ap if src is None else src, pat, op, val, base, cm), 200 + 2 * n, r=[name, "Z"], w=[name])
     def ch(j): return slice(512 * j, 512 * j + 512)
     def back(a, b): return slice(b - 1, a - 1 if a else None, -1)
+    def each(s): return ["%s%d" % (s, x) for x in range(NB)]
 
     for a, b in ((0, 1), (1, 2), (2, 4), (4, 6), (6, 8)):
         lead[0] = 10 ** 6 * (8 - a)
@@ -241,14 +206,12 @@ def rank_program(g, core, T, topo):
     load("s", [dma(T.acs[:, :], T.ac[:, :])], 200, w=["acs"])
     load("y", [dma(T.sti[:, q2, :], T.std[:, q2, :, :, :]) for q2 in range(8)], 300, r=["std"], w=["sti"])
 
-    task("v", [ms(T.Z[:], 0.0), ms(T.Zf[:], 0.0)], 768, w=["Z"])
+    task("v", [ms(T.Z[:], 0.0), ms(T.Zf[:], 0.0)], 704, w=["Z"])
     task("v", [ms(T.sD[64:66, 0:7, :], 0.0), ms(T.sD[64:66, 7, :], 512.0), ms(T.sD[0:64, 7, :], 0.0), ms(T.sL[64:66], -15.5),
-               ms(T.ri[64:128, 0, :], 1.0), ms(T.Bk[:], 1.0), ms(T.sP[0:64], 0.0), ms(T.Lp[:], 0.0),
-               ms(T.p16[:], 0.0), ms(T.pU[:], 0.0), ms(T.nf[:, 0:L_:128], 0.0)],
-         1700, w=["sDc", "sLc", "ri0c", "Bk", "sP", "sK0", "Lp", "p16", "pU", "nf"])
-    task("v", [ms(T.p16[:, 0:128:16], 1000.0), ms(T.pU[:, 15:128:16], -4.0), ms(T.pU[:, 0:128:16], 1.0)], 192, w=["p16", "pU"])
-    task("v", [ms(T.sP[64:66], -25.0 / 64), cp(T.zd[:], T.Z[:, 0:392]), ts(T.DD[:, :, 0], T.Z[:, 0:24], -4096.0, A.add)],
-         450, r=["Z"], w=["sPc", "sK", "zd0", "zd1", "zd2", "DD0", "DD1", "DD2"])
+               ms(T.ri[64:128, 0, :], 1.0), ms(T.Bk[:], 1.0), ms(T.sP[0:64], 0.0), ms(T.Lp[:], 0.0), ms(T.p16[:], 0.0), ms(T.UU[:, 0:L_:128], 0.0),
+               ms(T.sP[64:66], -25.0 / 64), ms(T.kz[:, 0:49:2, :], 0.0), ms(T.tz[:, 0:49:2, :], 0.0)],
+         1900, w=["sDc", "sLc", "ri0c", "Bk", "sP", "Lp", "p16", "sPc", "zeros"] + each("UU"))
+    task("v", [ms(T.p16[:, 0:128:16], 1000.0), ts(T.DD[:, :, 0], T.Z[:, 0:24], -4096.0, A.add)], 128, r=["Z"], w=["p16"] + each("DD"))
     paint("I2", T.I2[:], 256, [[0, 2], [-1, 128]], 1.0, 0, 1, T.Zf[:])
     paint("sD", T.sD[0:64, 0:7, :], 896, [[-1, 7], [-8, 8], [0, 16]], 1.0, 0, 1, T.Z[0:64, 0:896])
     paint("sD", T.sD[0:64, 0:7, :], 896, [[-1, 7], [-8, 8], [0, 16]], -1.0, -1, 1)
@@ -260,29 +223,28 @@ def rank_program(g, core, T, topo):
     paint("Lh", T.Lh[:, :, 0:15], 120, [[-16, 8], [-1, 15]], -1.0, -1, 1)
     paint("Lm", T.Lm[:], 128, [[-2, 64], [0, 2]], 1.0, 0, 1, T.Z[:, 0:128])
     paint("Lm", T.Lm[:, :, 0:7, :], 112, [[-16, 8], [-2, 7], [0, 2]], -1.0, -2, 1)
-    paint("Lh", T.Lh[:, :, 0], 8, [[-16, 8]], -2.0, -1, 1)
-    paint("Lm", T.Lm[:, :, 0, :], 16, [[-16, 8], [0, 2]], -1.0, -1, 1)
     for a, b, base in ((1, 8, 0), (0, 1, -56)):
         paint("sP", T.sP[0:64, a:b, :, 1:8], 98, [[-8, b - a], [0, 14]], 1.0 / 128, base, 1)
         paint("sP", T.sP[0:64, a:b, :, 1:8], 98, [[-8, b - a], [0, 2], [-1, 7]], -1.0 / 128, base - 1, 1)
     task("g", lambda q: q.iota(T.kb[:, 0:128], [[0, 8], [1, 16]], 0, 0, allow_small_or_imprecise_dtypes=True), 400, w=["kb0"])
-    paint("Db", T.Db[:], 128, [[-1, 2], [-2, 64]], 4096.0, 0, 1, T.Z[:, 0:128])
+    paint("Df", T.Df[:, 0], 128, [[-1, 2], [-2, 64]], 4096.0, 0, 1, T.Zf[:, 0:128])
     I1 = T.I2[:, 0:128]
-    task("s", [act(T.Ib[:, n, :], I1, scale=s) for n, s in enumerate((1.0, 2.0 ** -7))], 256, r=["I2"], w=["Ib"])
-    task("v", [ts(T.Ih[:, n, :], I1, s, A.mult) for n, s in enumerate((1.0, -1.0, 4096.0, 2.0 ** -12))]
-         + [red(T.col[:, u:u + 1], T.I2[:, u:128:2]) for u in range(2)] + [red(T.col[:, 2 + u:3 + u], T.I2[:, u:128:16]) for u in range(2)], 800, r=["I2"], w=["Ih", "col"])
+    task("s", [act(T.Ib[:, n, :], I1, scale=s) for n, s in enumerate((1.0, -4096.0, 2.0 ** -7))] + [act(T.I4[:], I1, scale=4096.0)], 512, r=["I2"], w=["Ib"])
+    task("s", act(T.Df[:, 1], T.Df[:, 0], scale=-1.0), 128, r=["Df"], w=["Dn"])
+    task("v", [ts(T.Ih[:, n, :], I1, s, A.mult) for n, s in enumerate((1.0, -1.0, -4096.0, 2.0 ** -12))]
+         + [red(T.col[:, u:u + 1], T.I2[:, u:128:2]) for u in range(2)] + [red(T.col[:, 2:3], T.I2[:, 0:128:16])], 700, r=["I2"], w=["Ih", "col"])
     task("v", [ts(T.col[:, 4:5], T.col[:, 1:2], 8192.0, A.mult, -4096.0, A.add), ts(T.col[:, 6:7], T.col[:, 2:3], 6144.0, A.mult),
-               ts(T.col[:, 7:8], T.col[:, 3:4], -2048.0, A.mult)], 192, r=["col"], w=["col4"])
-    task("v", ts(T.col[:, 5:6], T.col[:, 4:5], T.col[:, 6:7], A.add, T.col[:, 7:8], A.add), 64, r=["col4"], w=["col5"])
-    task("v", [cp(T.Dh[:], T.Db[:]), ts(T.sP[64:65], T.kb[64:65, 0:128], 1.0 / 2048, A.mult)], 128, r=["Db", "kb0", "sPc"], w=["Dh", "sPc"])
+               ts(T.col[:, 3:4], T.col[:, 2:3], -1.0, A.mult, 1.0, A.add), ts(T.sP[64:65], T.kb[64:65, 0:128], 1.0 / 2048, A.mult)], 256,
+         r=["col", "kb0"], w=["col4", "sPc"])
+    task("v", ts(T.col[:, 5:6], T.col[:, 4:5], T.col[:, 6:7], A.add), 64, r=["col4"], w=["col5"])
     task("s", [act(T.sC[:, :, u], T.Bk[:, 0:8, 0], scale=T.col[:, u:u + 1]) for u in range(2)] + [act(T.sM[:], T.Bk[:, 0:8, :], scale=-1.0 / 128)]
          + [act(T.Lp[:, b, :, b, :], T.Bk[:, 1:9, 0:8], scale=T.col[:, 5:6]) for b in range(2)], 400, r=["Bk", "col", "col5", "Lp"], w=["sC", "Lp"])
     task("s", [act(T.ro[64:128, t, :], T.Z[64:128, 0:L_], bias=1.0) for t in range(V_)], V_ * L_, r=["Z"], w=["roc"])
     task("v", [cp(T.xi[:, 0, q2:192:8], T.sti[:, q2, :]) for q2 in range(8)] + [ts(T.ri[0:64, 0, :], T.rsi[0:64, :], -1.0, A.mult, 98.0, A.add)], 900,
-         r=["sti", "rsi", "ri0c"], w=["xi00", "xi01", "xi02", "ri00", "ri01", "ri02"])
+         r=["sti", "rsi", "ri0c"], w=each("xi0") + each("ri0"))
 
     for j in range(8):
-        n = ("D0", "D1", "M0", "M1")[j % 4]
+        n = ("K2", "D", "M0", "M1")[j % 4]
         lead[0] = TLEAD * (8 - j)
         task("v", [ts(T.a0[:, ch(j)], T.ar[:, ch(j)], 32767, A.bitwise_and), ts(T.a1[:, j % 2, :], T.ar[:, ch(j)], 15, A.logical_shift_right)], 1024,
              r=["ar%d" % j], w=["a0%d" % j, "a1%d" % (j % 2)])
@@ -297,25 +259,19 @@ def rank_program(g, core, T, topo):
             load("y", [dma(T.TT[0:128:2, W_ + c.start:W_ + c.stop], U0[1:128:2, 512 * (j % 6) - 512:512 * (j % 6) + 512]), dma(T.TT[1:128:2, c], T.U1[0:128:2, c])], 512,
                  r=["%s%d" % (un, i % 6) for i in two] + ["U1%d" % i for i in two], w=["T%s%d" % (h, i) for i in two for h in "TU"])
     lead[0] = 0
-    task("t", [lambda q, c=c: q.transpose(T.AC[:, 128 * c:128 * c + 128], T.acs[:, 128 * c:128 * c + 128], I1) for c in range(3)], 1536,
-         r=["acs", "I2", "a05"], w=["AC"], b=["AC"])
-    task("s", act(T.acT[:], T.AC[:, 0:L_]), 384, r=["AC"], w=["acT"], b=["AC"])
+    task("t", [lambda q, c=c: q.transpose(T.M2[:, 128 * c:128 * c + 128], T.acs[:, 128 * c:128 * c + 128], I1) for c in range(3)], 1536,
+         r=["acs", "I2", "a05"], w=["M2"], b=["M2"])
+    task("s", act(T.acT[:], T.M2[:, 0:L_]), 384, r=["M2"], w=["acT"], b=["M2"])
     load("y", [dma(T.pr[16:128, :], T.pay[0:112, :]), dma(T.pr[0:16, :], T.pay[112:128, :])], 1024, r=["TU7"], w=["pr"])
     MMs, TTs = ["MM%d" % j for j in range(8)], ["T%s%d" % (h, j) for j in range(8) for h in "TU"]
     sent = [0]
 
-    def send(pairs, sem, to, r):
-        dst = T.cores[to % N]
+    def send(out, src, sem, step, r, w):
+        dst = T.cores[(rank + step) % N]
         rid, pid, _ = topo.addr(dst)
-        rest, moves = topo.engines(core, dst), []
-        sent[0] += len(rest)
-        for n, (out, src) in enumerate(pairs):
-            k = len(rest) if n == len(pairs) - 1 else len(rest) // 2
-            moves.append(RemoteDMATransfer(dst_ids=[DstId(rid=rid, pnc=pid)], dma_engine_mask=sum(1 << e for e in rest[:k]), remote_sem=T.sem[sem], src=src, dst=out))
-            rest = rest[k:]
-        return task("g", lambda q: q.remote_dma_fused(moves, local_sem=T.sem.gone), 300, r=r)
-
-    def lands(sem, frm, w, like): arrival(sem, len(topo.engines(T.cores[frm % N], core)), w, like)
+        sent[0] += len(topo.engines(core, dst))
+        n = task("g", lambda q: q.remote_dma(out, src, T.sem[sem], T.sem.gone, pid, rid, topo.mask(core, dst)), ISSUE, r=r)
+        arrival(sem, len(topo.engines(T.cores[(rank - step) % N], core)), w, n)
 
     def spread(n, R, t, name, j):
         task("t", [mm(T[n][:, k:512:8], T.sD[0:66, k, :], R[0:66, t, 64 * j:64 * j + 64]) for k in range(8)], 512,
@@ -326,144 +282,123 @@ def rank_program(g, core, T, topo):
     SINK = 2 * (16 * 132 - 800) + 2047.0 / 4096
 
     def visit(t, x):
-        c0, c1 = BATCHES[x]
-        lead[0] = LEAD * (1 - x)
-        nc = c1 - c0
-        cg, lg, lanes, cols = slice(8 * c0, 8 * c1), slice(0, 128 * nc), slice(128 * c0, 128 * c1), slice(64 * c0, 64 * c1)
-        Kn, Mn = ("K0", "K1", "D0")[x], ("M0", "M1", "AC")[x]
+        cg, lanes, cols, odd = slice(8 * x, 8 * x + 8), slice(128 * x, 128 * x + 128), slice(64 * x, 64 * x + 64), slice(16 * x + 1, 16 * x + 17, 2)
+        Kn, Mn = "K%d" % x, "M%d" % x
         K, M = T[Kn], T[Mn]
         def nm(s): return "%s%d" % (s, x)
         xi, ri, xo, ro = ["%s%d%d" % (s, t, x) for s in ("xi", "ri", "xo", "ro")]
-        def wide(n): return max(64, n * nc)
-        def lc(c): return slice(128 * c, 128 * c + 128)
-        def gc(c, a=0, step=1): return slice(128 * (c - c0) + a, 128 * (c - c0) + 128, step)
-        chunks, pieces = range(c0, c1), range(2 * c0, 2 * c1)
+        pieces = (2 * x, 2 * x + 1)
+        GSs, GAs, GS0 = ["GS%d" % j for j in pieces], ["GA%d" % j for j in pieces], T.GS[:, 1024 * x:1024 * x + 1024:8]
 
         task("v", ts(T.sth[:, cols], T.xi[:, t, cols], -2048.0, A.add), 64, r=[xi], w=[nm("sth")])
         for j in pieces:
-            n = (Mn, "D0" if nc > 1 else Kn)[j % 2]
+            n = (Mn, Kn)[j % 2]
             spread(n, T.ri, t, ri, j)
             task("s", act(T.G[:, ch(j)], T.MM[:, 0:W_].indirect(T.xi[:, t, 32 * j:32 * j + 32]), bias=UP, scale=2.0 ** -12), 80 + 512 * GATHER,
-                 r=MMs + [xi] + ["GA%d" % (2 * c0 - 1)] * (x > 0 and t < STAG), w=["G%d" % j])
+                 r=MMs + [xi], w=["G%d" % j])
             bk = back(512 * j, 512 * j + 512)
             task("v", scan(T.GS[:, bk], T[n][:, REV], T.G[:, bk], A.add, A.min), 512, r=["G%d" % j], w=[n, "GS%d" % j], b=[n])
-        half = slice(0, 64 * nc)
-        for c in chunks:
-            d = c - c0
-            n = (Kn, "D0")[d]
-            B, Kc, Mc, GSs, GAs = T[n], "%sc%d" % (Kn, d), "%sc%d" % (Mn, d), ["GS%d" % (2 * c), "GS%d" % (2 * c + 1)], ["GA%d" % (2 * c), "GA%d" % (2 * c + 1)]
-            Bc, Bl, an = n + "c0", n + "l", n + "a"
-            def cn(s): return "%sc%d" % (s, c)
-            task("t", [mm(B[:, 0:128], T.ri[0:66, t, lc(c)], T.sL[0:66], True, False),
-                       mm(B[:, 0:128], T.GS[:, 1024 * c:1024 * c + 1024:8], T.Ib[:, 0, :], False, True)], 256, r=[ri, "sL", "sLc", "Ib", n] + GSs, w=[Bc], b=[n])
-            task("v", tt(B[:, 0:128], B[:, 0:128], T.acT[:, lc(c)], A.add), 128, r=[n, "acT"], w=[Bc], b=[n])
-            task("v", scan(T.sc[:, lc(c)], T.p16[:], B[:, 0:128], A.add, A.min), 128, r=[n, Bc, "p16"], w=[cn("sc")], b=[n])
-            task("v", tt(T.nf[:, 128 * c + 1:128 * c + 128], T.sc[:, 128 * c:128 * c + 127], B[:, 1:128], A.is_gt), 128, r=[n, Bc, cn("sc"), "nf"], w=[cn("nf")], b=[n])
-            bk = back(128 * c, 128 * c + 128)
-            task("v", scan(T.UU[:, bk], T.pU[:, REV], T.nf[:, bk], A.add, A.max), 64, r=[cn("nf"), "pU"], w=[cn("UU")])
-            task("t", mm(B[:, 0:128], T.UU[:, lc(c)], T.Ib[:, 0, :]), 128, r=[n, cn("UU"), "Ib"], w=[Bc], b=[n])
-            task("s", act(T.UT[:, lc(c)], B[:, 0:128]), 128, r=[n, Bc], w=[cn("UT")], b=[n])
-            li, one = slice(256, 320), slice(256 + 128 * d, 384 + 128 * d)
-            task("t", [mm(B[:, li], T.Ih[:, 0, :], T.sth[:, 64 * c:64 * c + 64], True, False)]
-                 + [mm(B[:, li], T.Lp[:, b], T.UT[:, 128 * c + b:128 * c + 128:2], False, b == 1) for b in range(2)], 192,
-                 r=[n, cn("UT"), nm("sth"), "Lp", "Ih"], w=[Bl], b=[n])
-            task("v", cp(T.ix2[:, 64 * c:64 * c + 64], B[:, li]), 64, r=[n, Bl], w=[cn("ix2")], b=[n])
-            task("t", [mm(M[:, gc(c)], T.Lm[:], T.UT[:, lc(c)]), mm(M[:, one], T.Lh[:], T.UT[:, lc(c)])], 256, r=[Mn, cn("UT"), "Lm", "Lh"], w=[Mc], b=[Mn])
-            task("v", tt(T.MH[:, lc(c)], M[:, one], T.GS[:, 1024 * c:1024 * c + 1024:8], A.mult), 128, r=[Mn, Mc] + GSs, w=[cn("MH")], b=[Mn])
-            for j in (2 * c, 2 * c + 1):
-                task("s", act(T.GA[:, ch(j)], T.TT[:, 0:2 * W_].indirect(T.ix2[:, 32 * j:32 * j + 32])), 80 + 512 * GATHER, r=TTs + [cn("ix2")], w=["GA%d" % j])
-            for h in range(2):
-                ks = range(4 * h, 4 * h + 4)
-                ga = [T.GA[:, 1024 * c + k:1024 * c + 1024:8] for k in range(8)]
-                task("v", [tt(ga[k], M[:, gc(c)], ga[k], A.mult) for k in ks], 512, r=[Mn, Mc] + GAs, w=["GB%d%d" % (c, h)], b=[Mn])
-                task("t", [mm(T[n][:, 384 + k:512:8], ga[k], T.sC[:]) for k in ks], 1024, r=[n, "sC", "GB%d%d" % (c, h)] + GAs, w=[an], b=[n])
-            task("s", act(T.kb[:, lc(c)], B[:, 384:512], bias=UP, scale=2.0 ** -12), 128, r=[n, an], w=["kb%d" % c], b=[n])
-            task("s", act(T.AF[:, lc(c)], T.kb[:, lc(c)], bias=2048 - 129 * 4096.0, scale=4096.0), 128, r=["kb%d" % c], w=[cn("AF")])
-            task("v", tt(T.FF[:, lc(c)], B[:, 384:512], T.AF[:, lc(c)], A.subtract), 128, r=[n, an, cn("AF")], w=[cn("FF")], b=[n])
-            task("t", [mm(K[:, gc(c)], T.ri[0:66, t, lc(c)], T.sP[0:66], True, False), mm(K[:, gc(c)], T.MH[:, lc(c)], T.sM[:], False, False),
-                       mm(K[:, gc(c)], T.Ib[:, 1, :], T.kb[:, lc(c)], False, False), mm(K[:, gc(c)], T.Ih[:, 0, :], T.FF[:, lc(c)], False, True)], 512,
-                 r=[Kn, "kb%d" % c, cn("FF"), cn("MH"), ri, "sP", "sPc", "sC", "Ib", "Ih"], w=[Kc], b=[Kn])
-        task("s", act(T.SB0[:, cg, 0], K[:, 1:128 * nc:2]), wide(64), r=["%sc%d" % (Kn, d) for d in range(nc)], w=[nm("so0"), Kn], b=[Kn])
+        task("t", [mm(K[:, 0:128], T.ri[0:66, t, lanes], T.sL[0:66], True, False), mm(K[:, 0:128], GS0, T.Ib[:, 0, :], False, True)], 256,
+             r=[ri, "sL", "sLc", "Ib"] + GSs, w=[Kn], b=[Kn])
+        task("v", tt(K[:, 0:128], K[:, 0:128], T.acT[:, lanes], A.add), 128, r=["acT"], w=[Kn], b=[Kn])
+        task("v", [scan(T.sc[:, lanes], T.p16[:], K[:, 0:128], A.add, A.min), scan(K[:, 255:127:-1], T.p16[:], K[:, 127::-1], A.add, A.min)], 256,
+             r=["p16"], w=[nm("sc"), Kn], b=[Kn])
+        task("v", tt(T.UU[:, 128 * x + 1:128 * x + 128], K[:, 129:256], T.sc[:, 128 * x:128 * x + 127], A.is_lt), 128, r=[Kn, nm("sc")], w=[nm("UU")], b=[Kn])
+        task("t", mm(K[:, 0:128], T.UU[:, lanes], T.Ib[:, 0, :]), 128, r=[nm("UU"), "Ib"], w=[Kn], b=[Kn])
+        task("s", act(T.UT[:, lanes], K[:, 0:128], bias=T.col[:, 2:3], scale=T.col[:, 3:4]), 128, r=[Kn, "col4"], w=[nm("UT")], b=[Kn])
+        task("t", [mm(K[:, 256:320], T.Ih[:, 0, :], T.sth[:, cols], True, False)]
+             + [mm(K[:, 256:320], T.Lp[:, b], T.UT[:, 128 * x + b:128 * x + 128:2], False, b == 1) for b in range(2)], 192,
+             r=[nm("UT"), nm("sth"), "Lp", "Ih"], w=[Kn], b=[Kn])
+        task("v", cp(T.ix2[:, cols], K[:, 256:320]), 64, r=[Kn], w=[nm("ix2")], b=[Kn])
+        task("t", [mm(M[:, 0:128], T.Lm[:], T.UT[:, lanes]), mm(M[:, 256:384], T.Lh[:], T.UT[:, lanes])], 256, r=[nm("UT"), "Lm", "Lh"], w=[Mn], b=[Mn])
+        task("v", tt(T.MH[:, lanes], M[:, 256:384], GS0, A.mult), 128, r=[Mn] + GSs, w=[nm("MH")], b=[Mn])
+        for j in pieces:
+            task("s", act(T.GA[:, ch(j)], T.TT[:, 0:2 * W_].indirect(T.ix2[:, 32 * j:32 * j + 32])), 80 + 512 * GATHER, r=TTs + [nm("ix2")], w=["GA%d" % j])
+        ga = [T.GA[:, 1024 * x + k:1024 * x + 1024:8] for k in range(8)]
+        for h in range(2):
+            ks = range(4 * h, 4 * h + 4)
+            task("v", [tt(ga[k], M[:, 0:128], ga[k], A.mult) for k in ks], 512, r=[Mn] + GAs, w=["GB%d%d" % (x, h)], b=[Mn])
+            task("t", [mm(K[:, 384 + k:512:8], ga[k], T.sC[:]) for k in ks], 1024, r=["sC", "GB%d%d" % (x, h)] + GAs, w=[Kn], b=[Kn])
+        task("s", [act(T.kb[:, lanes], K[:, 384:512], bias=UP, scale=2.0 ** -12), act(T.AF[:, lanes], K[:, 384:512], bias=129 * 4096.0 - 2048)], 256,
+             r=[Kn], w=[nm("kb")], b=[Kn])
+        task("t", [mm(K[:, 0:128], I1, T.AF[:, lanes], True, False)] + [mm(K[:, 0:128], T.Ib[:, i, :], T.kb[:, lanes], False, False) for i in (1, 2)]
+             + [mm(K[:, 0:128], T.ri[0:66, t, lanes], T.sP[0:66], False, False), mm(K[:, 0:128], T.MH[:, lanes], T.sM[:], False, True)], 1024,
+             r=[nm("kb"), nm("MH"), ri, "sP", "sPc", "sC", "Ib", "I2"], w=[Kn], b=[Kn])
+        task("s", act(T.SB0[:, cg, 0], K[:, 1:128:2]), 64, r=[Kn], w=[nm("so0")], b=[Kn])
 
         def view(pp, place): return T.S[(ALL, cg, pp) + place[1]] if place[0] == 0 else (T.SB0, T.SB1)[pp][(ALL, cg) + place[1]]
 
-        def sort(steps, first, last, w, b):
+        def sort(steps, first, last, w):
             for n, calls in enumerate(steps):
                 pp, head, end = n % 2, n == 0 and first is not None, n == len(steps) - 1
                 task("v", [tt(last(mx) if end else view(1 - pp, o), first if head else view(pp, i0), view(pp, i1), A.max if mx else A.min) for mx, o, i0, i1, _ in calls],
-                     sum(max(64, 8 * nc * k * (i0[0] + i1[0])) for _, _, i0, i1, k in calls), r=[nm("so%d" % pp)] + [Kn] * head,
-                     w=w if end else [nm("so%d" % (1 - pp))], b=["S"] + [Kn] * head + b * end)
-        FFs = ["FFc%d" % c for c in chunks]
-        sort(ALL16, K[:, 0:128 * nc:2], lambda mx: M[:, 256 + mx:256 + 128 * nc:2], [Mn], [Mn])
-        k1 = M[:, 256:256 + 128 * nc]
-        task("v", ts(T.DD[:, cg, 1:17], k1, 1.5 * 2 ** 23, A.add, 1.5 * 2 ** 23, A.subtract), wide(128), r=[Mn], w=[nm("DD")], b=[Mn])
-        task("v", tt(T.FF[:, lanes], k1, T.DD[:, cg, 1:17], A.subtract), wide(128), r=[Mn, nm("DD")], w=FFs, b=[Mn])
-        task("t", [mm(K[:, lg], T.Ih[:, 0, :], T.DD[:, cg, 0:16], True, False), mm(K[:, lg], T.Ih[:, 1, :], T.DD[:, cg, 1:17], False, True)], 256 * nc,
+                     sum(max(64, 8 * k * (i0[0] + i1[0])) for _, _, i0, i1, k in calls), r=[nm("so%d" % pp)] + [Kn] * head,
+                     w=[w if end else nm("so%d" % (1 - pp))], b=["S"] + [Kn] * head)
+        sort(ALL16, K[:, 0:128:2], lambda mx: T.k1[:, 128 * x + mx:128 * x + 128:2], nm("k1"))
+        task("v", ts(T.DD[:, cg, 1:17], T.k1[:, lanes], 1.5 * 2 ** 23, A.add, 1.5 * 2 ** 23, A.subtract), 128, r=[nm("k1")], w=[nm("DD")])
+        task("t", mm(M[:, 0:128], T.I4[:], T.k1[:, lanes], True, False), 512, r=[nm("k1"), "Ib"], w=[Mn], b=[Mn])
+        task("t", [mm(K[:, 0:128], T.Ih[:, 0, :], T.DD[:, cg, 0:16], True, False), mm(K[:, 0:128], T.Ih[:, 1, :], T.DD[:, cg, 1:17], False, True)], 256,
              r=[nm("DD"), "Ih"], w=[Kn], b=[Kn])
-        task("t", [mm(M[:, lg], T.Ih[:, 3, :], T.DD[:, cg, 1:17], True, False), mm(M[:, lg], T.Ih[:, 2, :], T.FF[:, lanes], False, True)], 256 * nc,
-             r=[nm("DD"), "Ih"] + FFs, w=[Mn], b=[Mn])
-        task("s", act(T.pen[:, lanes], K[:, lg], bias=SINK, scale=8192.0), wide(128), r=[Kn], w=[nm("pen")], b=[Kn])
-        task("v", [tt((T.S, T.SB0)[v][:, cg, 0], M[:, v:128 * nc:2], T.pen[:, 128 * c0 + v:128 * c1:2], A.max) for v in range(2)], 2 * wide(64),
+        task("t", [mm(M[:, 0:128], T.Ih[:, n, :], T.DD[:, cg, 1:17], False, n == 3) for n in (2, 3)], 256, r=[nm("DD"), "Ih"], w=[Mn], b=[Mn])
+        task("s", act(T.pen[:, lanes], K[:, 0:128], bias=SINK, scale=8192.0), 128, r=[Kn], w=[nm("pen")], b=[Kn])
+        task("v", [tt((T.S, T.SB0)[v][:, cg, 0], M[:, v:128:2], T.pen[:, 128 * x + v:128 * x + 128:2], A.max) for v in range(2)], 128,
              r=[Mn, nm("pen")], w=[nm("so0")], b=[Mn, "S"])
-        sort(BEST8, None, lambda mx: T.KS[:, cg, mx:8:2], [nm("KS")], [])
-        task("v", ts(T.S[:, cg, 0], T.KS[:, cg], 1.5 * 2 ** 24, A.add, 1.5 * 2 ** 24, A.subtract), wide(64), r=[nm("KS")], w=[nm("so0")], b=["S"])
-        task("v", tt(T.zd[:, 16 * c0 + 1:16 * c1 + 1:2, :], T.KS[:, cg], T.S[:, cg, 0], A.subtract), wide(64),
-             r=[nm("KS"), nm("so0")], w=[nm("zd")], b=["S"])
-        task("s", act(T.cb[:, cg], T.KS[:, cg], bias=180 - 15.0 / 32, scale=1.0 / 32), wide(64), r=[nm("KS")], w=[nm("cb")])
-        task("t", [mm(K[:, 64 * (c - c0):64 * (c - c0) + 64], T.zd[:, 16 * c + 1 - b:16 * c + 17 - b, :], T.Dh[:, b, :], b == 0, b == 1)
-                   for c in chunks for b in range(2)], 128 * nc, r=[nm("zd"), "Dh"], w=[Kn], b=[Kn])
-        task("v", ts(T.xo[:, t, cols], K[:, half], 2048.0, A.add), wide(64), r=[Kn], w=[xo], b=[Kn])
-        task("t", [mm(M[0:64, gc(c)], T.cb[:, 8 * c:8 * c + 8, :], T.Ib[:, 0, :]) for c in chunks], 128 * nc, r=[nm("cb"), "Ib"], w=[Mn], b=[Mn])
-        task("s", act(T.ro[0:64, t, lanes], M[0:64, lg], F.Abs, bias=-228.0), wide(128), r=[Mn], w=[ro], b=[Mn])
+        sort(BEST8, None, lambda mx: T.kz[:, odd, mx:8:2], nm("kz"))
+        task("v", ts(T.tz[:, odd, :], T.kz[:, odd, :], 1.5 * 2 ** 24, A.add, 1.5 * 2 ** 24, A.subtract), 64, r=[nm("kz")], w=[nm("tz")])
+        task("s", act(T.cb[:, cg], T.kz[:, odd, :], bias=180 - 15.0 / 32, scale=1.0 / 32), 64, r=[nm("kz")], w=[nm("cb")])
+        for s, z in enumerate(("kz", "tz")):
+            task("t", [mm(K[:, 0:64], T[z][:, 16 * x + 1 - b:16 * x + 17 - b, :], T.Df[:, s, b, :], s + b == 0, s + b == 2) for b in range(2)], 512,
+                 r=[nm(z), "Df", "Dn", "zeros"], w=[Kn], b=[Kn])
+        task("v", ts(T.xo[:, t, cols], K[:, 0:64], 2048.0, A.add), 64, r=[Kn], w=[xo], b=[Kn])
+        task("t", mm(M[0:64, 0:128], T.cb[:, cg], T.Ib[:, 0, :]), 128, r=[nm("cb"), "Ib"], w=[Mn], b=[Mn])
+        task("s", act(T.ro[0:64, t, lanes], M[0:64, 0:128], F.Abs, bias=-228.0), 128, r=[Mn], w=[ro], b=[Mn])
         if t < V_ - 1:
             sem = "%d%d" % (t + 1, x)
-            mid = 64 * (c0 + c1)
-            pairs = [(T.xi[:, t + 1, cols], T.xo[:, t, cols])] + [(T.ri[:, t + 1, a:b], T.ro[:, t, a:b]) for a, b in ((128 * c0, mid), (mid, 128 * c1))]
-            if FUSE:
-                lands("m" + sem, rank - 1, ["xi" + sem, "ri" + sem], send(pairs, "m" + sem, rank + 1, [xo, ro, "roc"]))
-            else:
-                lands("m" + sem, rank - 1, ["xi" + sem], send(pairs[:1], "m" + sem, rank + 1, [xo]))
-                lands("n" + sem, rank - 1, ["ri" + sem], send([(T.ri[:, t + 1, lanes], T.ro[:, t, lanes])], "n" + sem, rank + 1, [ro, "roc"]))
+            send(T.xi[:, t + 1, cols], T.xo[:, t, cols], "m" + sem, 1, [xo], ["xi" + sem])
+            send(T.ri[:, t + 1, lanes], T.ro[:, t, lanes], "n" + sem, 1, [ro, "roc"], ["ri" + sem])
 
-        lead[0] = 0
+    def payload(t, x, gate):
+        lanes, pieces, Kn, Mn = slice(128 * x, 128 * x + 128), (2 * x, 2 * x + 1), "K%d" % x, "M%d" % x
+        K = T[Kn]
+        def nm(s): return "%s%d" % (s, x)
+        xo, ro = ["%s%d%d" % (s, t, x) for s in ("xo", "ro")]
+        Ss, late = [], ["xo%d%d" % (t + 1, LATE[x])] if gate and LATE[x] >= 0 and t < LEND else []
         for j in pieces:
-            spread("D1", T.ro, t, ro, j)
-            task("s", act(T.GP[:, ch(j)], T.pr[:, 0:W_].indirect(T.xo[:, t, 32 * j:32 * j + 32])), 80 + 512 * GATHER, r=["pr", xo], w=["GP%d" % j])
-            task("s", act(T.WW[:, ch(j)], T.D1[:], F.Exp, scale=-0.125), 512, r=["D1", "roc"], w=["WW%d" % j], b=["D1"])
-            bk = back(512 * j, 512 * j + 512)
-            for S, op, n in ((T.U1, A.add, "U1"), (T.S1, A.max, "S1")):
-                task("v", [scan(S[:, b2], T.WW[:, b2], T.GP[:, b2], A.mult, op) for b2 in [back(512 * j + i, 512 * j + i + CUT) for i in range(0, 512, CUT)]], 512,
-                     r=["WW%d" % j, "GP%d" % j], w=["%s%d" % (n, j)])
-        Ss = ["%s%d" % (h, j) for j in pieces for h in ("U1", "S1")]
-        part = [slice(256 * c0 + 128 * nc * h, 256 * c0 + 128 * nc * (h + 1)) for h in range(2)]
-        both = slice(256 * c0, 256 * c1)
-        last = [(T.U1, T.S1)[h][:, 1024 * c0:1024 * c1:8] for h in range(2)]
+            d = Mn if t == V_ - 1 and j % 2 else "D"
+            spread(d, T.ro, t, ro, j)
+            task("s", act(T.GP[:, ch(j)], T.pr[:, 0:W_].indirect(T.xo[:, t, 32 * j:32 * j + 32])), 80 + 512 * GATHER, r=["pr", xo] + gate, w=["GP%d" % j])
+            task("s", act(T.WW[:, ch(j)], T[d][:], F.Exp, scale=-0.125), 512, r=[d] + gate, w=["WW%d" % j], b=[d])
+            for i in range(0, 512, CUT):
+                bk = back(512 * j + i, 512 * j + i + CUT)
+                for S, op, n in ((T.U1, A.add, "U1"), (T.S1, A.max, "S1")):
+                    Ss.append("%s%d.%d" % (n, j, i))
+                    task("v", scan(S[:, bk], T.WW[:, bk], T.GP[:, bk], A.mult, op), CUT, r=["WW%d" % j, "GP%d" % j, "TU7"] + late, w=Ss[-1:])
+        part, both = [slice(256 * x + 128 * h, 256 * x + 128 * h + 128) for h in range(2)], slice(256 * x, 256 * x + 256)
+        last = [(T.U1, T.S1)[h][:, 1024 * x:1024 * x + 1024:8] for h in range(2)]
         def turned(s): return T.I2[:, 128 - 16 * (V_ - 1 - s):256 - 16 * (V_ - 1 - s)]
 
         def add_part(s, n):
-            for i in range(2):
-                cs = slice(256 * c0 + 128 * i, 256 * c0 + 128 * i + 128)
-                task("t", [mm(T[n][:, 128 * i:128 * i + 128], turned(0 if s == 1 else V_ - 1), T.XO[:, 0, cs], True, False),
-                           mm(T[n][:, 128 * i:128 * i + 128], turned(s), T.XL[:, s - 1, cs], False, True)], 1024,
+            for h in range(2):
+                task("t", [mm(T[n][:, 128 * h:128 * h + 128], turned(0 if s == 1 else V_ - 1), T.XO[:, 0, part[h]], True, False),
+                           mm(T[n][:, 128 * h:128 * h + 128], turned(s), T.XL[:, s - 1, part[h]], False, True)], 1024,
                      r=["I2", "XO0%d" % x, "XL%d%d" % (s, x)], w=[n], b=[n])
         if t < V_ - 1:
-            task("s", [act(T.XO[:, t, part[h]], last[h]) for h in range(2)], 2 * wide(128), r=Ss, w=["XO%d%d" % (t, x)])
-            if t:
-                sem = "x%d%d" % (t, x)
-                lands(sem, rank + t, ["XL%d%d" % (t, x)], send([(T.XL[:, t - 1, both], T.XO[:, t, both])], sem, rank - t, ["XO%d%d" % (t, x)]))
+            task("s", [act(T.XO[:, t, part[h]], last[h]) for h in range(2)], 256, r=Ss, w=["XO%d%d" % (t, x)])
+            if t: send(T.XL[:, t - 1, both], T.XO[:, t, both], "x%d%d" % (t, x), -t, ["XO%d%d" % (t, x)], ["XL%d%d" % (t, x)])
         if 2 <= t < V_ - 1:
-            add_part(t - 1, "D1")
-            task("s", act(T.XO[:, 0, both], T.D1[:, 0:256]), 256, r=["D1"], w=["XO0%d" % x], b=["D1"])
+            add_part(t - 1, "D")
+            task("s", act(T.XO[:, 0, both], T.D[:, 0:256]), 256, r=["D"], w=["XO0%d" % x], b=["D"])
         if t == V_ - 1:
             add_part(t - 1, Kn)
             task("v", [tt(T.YO[:, part[h]], K[:, 128 * h:128 * h + 128], last[h], A.add) for h in range(2)], 256, r=Ss + [Kn], w=[nm("YO")], b=[Kn])
             cut = 16 * (V_ % 8)
             for e, y, h in (("y", T.ys, 0), ("s", T.ym, 1)):
-                load(e, [dma(y[0:128 - cut, lanes], T.YO[cut:128, part[h]]), dma(y[128 - cut:128, lanes], T.YO[0:cut, part[h]])], 64 * nc,
+                load(e, [dma(y[0:128 - cut, lanes], T.YO[cut:128, part[h]]), dma(y[128 - cut:128, lanes], T.YO[0:cut, part[h]])], 64,
                      r=[nm("YO")], w=["out%d%d" % (x, h)])
 
-    for t in range(V_):
-        for x in range(len(BATCHES)): visit(t, x)
-    task("y", [], 0, r=["out%d%d" % (x, h) for x in range(len(BATCHES)) for h in range(2)])
-    emit(g, T, (arrange2 if PASSES else arrange)(tasks))
+    for t in range(V_ + 1):
+        for x in range(NB if t < V_ else 0): visit(t, x)
+        for x in range(NB if t else 0): payload(t - 1, x, [GATE[x]] if t <= DEFER and GATE[x] else [])
+    task("y", [], 0, r=["out%d%d" % (x, h) for x in range(NB) for h in range(2)])
+    emit(g, T, arrange(tasks))
     g.wait_ge(T.sem.gone, sent[0])

@@ -6,10 +6,10 @@ F = ActivationFunctionType
 V_, L_, W_, NB = 5, 384, 4096, 3
 f32, bf, f16, i32, u16 = "float32", "bfloat16", "float16", "int32", "uint16"
 SCRATCH = {
-    "ar": ("sbuf", [128, W_], i32), "a0": ("sbuf", [128, W_], i32), "a1": ("sbuf", [128, 2, 512], i32),
+    "ar": ("sbuf", [128, W_], i32), "a0": ("sbuf", [128, W_], i32), "a1": ("sbuf", [128, 3, 512], i32),
     "U1": ("sbuf", [128, W_], f32), "TT": ("sbuf", [128, 2 * W_], f32), "MM": ("sbuf", [128, W_], f32), "pr": ("sbuf", [128, W_], bf),
     "acs": ("sbuf", [128, L_], f32), "acT": ("sbuf", [128, L_], f32),
-    "rsi": ("sbuf", [128, L_], i32), "sti": ("sbuf", [128, 8, 24], i32), "std": ("dram", [8, 8, 2, 8, 24], i32),
+    "rsi": ("sbuf", [128, L_], i32), "sti": ("sbuf", [128, 192], i32), "sS": ("sbuf", [128, 8, 136], f32),
     "G": ("sbuf", [128, 3072], bf), "GS": ("sbuf", [128, 3072], bf), "GA": ("sbuf", [128, 3072], f32),
     "GP": ("sbuf", [128, 3072], bf), "WW": ("sbuf", [128, 3072], f32), "S1": ("sbuf", [128, 3072], f32),
     "sc": ("sbuf", [128, L_], f32), "UU": ("sbuf", [128, L_], bf), "UT": ("sbuf", [128, L_], bf),
@@ -33,11 +33,29 @@ POOL = {"v": 30, "s": 26, "t": 26, "g": 16, "d": 18}
 SEMAPHORES = (["%s%d" % (e, i) for e in POOL for i in range(POOL[e])] + ["gone"]
               + ["%s%d%d" % (n, t, b) for n, k in (("m", 5), ("n", 5), ("x", 4)) for t in range(1, k) for b in range(NB)])
 SLACK = 0
-GATE = ("kb2", "kb2", "kb2")
-DEFER = 4
-LATE = (0, 0, 0)
-LEND = 3
-TLEAD = 1000
+GATE = "kb1"
+LAST = None
+LEAD = 1000
+LEAD4 = 1500
+GATE4 = "kb2"
+SHORT = {"s": 2000, "v": 500, "t": 2000, "g": 0, "y": 0}
+CHAIN = 20000
+T0LEAD = 0
+NA = 3
+SETUP = 30000
+PLEAD = 3000
+PARTS = ((0, 1), (1, 2), (2, 4), (4, 6), (6, 8))
+T0S = (0, 1, 2)
+U0G = (0, 1, 2, 3, 4, 5, 6)
+U0V = ()
+OWN1 = (1,)
+OWN2 = (5,)
+STAG = 0
+SEND = 5
+MCUT = 512
+KCUT = 4
+LATE = ((1, "xo%d0"),) * 6
+TLEAD = 2000
 CUT = 256
 HOP = 230
 REMOTE = 2500
@@ -173,7 +191,7 @@ def rank_program(g, core, T, topo):
 
     def task(e, f, c, r=(), w=(), b=(), dma=0):
         f = f if isinstance(f, list) else [f]
-        tasks.append({"e": e, "f": f, "r": list(r), "w": list(w), "b": list(b), "dma": dma > 0, "c": c * PEF if e == "t" else c, "lat": dma, "after": [], "lead": lead[0]})
+        tasks.append({"e": e, "f": f, "r": list(r), "w": list(w), "b": list(b), "dma": dma > 0, "c": c * PEF if e == "t" else c, "lat": dma, "after": [], "lead": lead[0] + (SHORT[e] if c <= 256 and lead[0] else 0) + SETUP * (len(lead) == 1)})
         return len(tasks) - 1
 
     def arrival(sem, val, w, like):
@@ -197,14 +215,13 @@ def rank_program(g, core, T, topo):
     def back(a, b): return slice(b - 1, a - 1 if a else None, -1)
     def each(s): return ["%s%d" % (s, x) for x in range(NB)]
 
-    for a, b in ((0, 1), (1, 2), (2, 4), (4, 6), (6, 8)):
+    for a, b in PARTS:
         lead[0] = 10 ** 6 * (8 - a)
         load("y", [dma(T.ar[:, 512 * a:512 * b], T.arcs[:, 512 * a:512 * b])], 256 * b, w=["ar%d" % j for j in range(a, b)])
+    lead[0] = 10 ** 5
+    load("s", [dma(T.sti[:, :], T.st0[:, :])], 300, w=["sti"])
+    load("y", [dma(T.rsi[0:64, :], T.rs0[:, :]), dma(T.acs[:, :], T.ac[:, :])], 2500, w=["rsi", "acs"])
     lead[0] = 0
-    load("s", [dma(T.std[:, :, :, k, :], T.st0[:, k * 24:k * 24 + 24]) for k in range(8)], 300, w=["std"])
-    load("s", [dma(T.rsi[0:64, :], T.rs0[:, :])], 100, w=["rsi"])
-    load("s", [dma(T.acs[:, :], T.ac[:, :])], 200, w=["acs"])
-    load("y", [dma(T.sti[:, q2, :], T.std[:, q2, :, :, :]) for q2 in range(8)], 300, r=["std"], w=["sti"])
 
     task("v", [ms(T.Z[:], 0.0), ms(T.Zf[:], 0.0)], 704, w=["Z"])
     task("v", [ms(T.sD[64:66, 0:7, :], 0.0), ms(T.sD[64:66, 7, :], 512.0), ms(T.sD[0:64, 7, :], 0.0), ms(T.sL[64:66], -15.5),
@@ -240,20 +257,35 @@ def rank_program(g, core, T, topo):
     task("s", [act(T.sC[:, :, u], T.Bk[:, 0:8, 0], scale=T.col[:, u:u + 1]) for u in range(2)] + [act(T.sM[:], T.Bk[:, 0:8, :], scale=-1.0 / 128)]
          + [act(T.Lp[:, b, :, b, :], T.Bk[:, 1:9, 0:8], scale=T.col[:, 5:6]) for b in range(2)], 400, r=["Bk", "col", "col5", "Lp"], w=["sC", "Lp"])
     task("s", [act(T.ro[64:128, t, :], T.Z[64:128, 0:L_], bias=1.0) for t in range(V_)], V_ * L_, r=["Z"], w=["roc"])
-    task("v", [cp(T.xi[:, 0, q2:192:8], T.sti[:, q2, :]) for q2 in range(8)] + [ts(T.ri[0:64, 0, :], T.rsi[0:64, :], -1.0, A.mult, 98.0, A.add)], 900,
-         r=["sti", "rsi", "ri0c"], w=each("xi0") + each("ri0"))
+    task("s", [act(T.sS[:, a:a + 4], T.Z[:, 0:544]) for a in (0, 4)], 1088, r=["Z"], w=["sS"])
+    paint("sS", T.sS[:, :, 7:135:8], 128, [[-2, 8], [-16, 8], [-1, 2]], 1.0, 0, 1)
+    task("s", act(T.ri[0:64, 0, :], T.rsi[0:64, :], bias=98.0, scale=-1.0), 384, r=["rsi", "ri0c"], w=each("ri0"))
+    lead[0] = 10 ** 5
+    task("s", act(T.AF[:, 0:192], T.sti[:]), 192, r=["sti"], w=["kb1"])
+    lead[0] = 0
+    for q in range(8):
+        task("t", [mm(T.K0[:, q:192:8], T.sS[:, q, 7 - k:135 - k], T.AF[:, 24 * k:24 * k + 24], k == 0, k == 7) for k in range(8)], 2048, r=["sS", "kb1"], w=["K0"], b=["K0"])
+    task("v", cp(T.xi[:, 0, :], T.K0[:, 0:192]), 192, r=["K0"], w=each("xi0"), b=["K0"])
 
     for j in range(8):
         n = ("K2", "D", "M0", "M1")[j % 4]
         lead[0] = TLEAD * (8 - j)
-        task("v", [ts(T.a0[:, ch(j)], T.ar[:, ch(j)], 32767, A.bitwise_and), ts(T.a1[:, j % 2, :], T.ar[:, ch(j)], 15, A.logical_shift_right)], 1024,
-             r=["ar%d" % j], w=["a0%d" % j, "a1%d" % (j % 2)])
-        task("v", cp(T[n][:], T.a1[:, j % 2, :]), 512, r=["a1%d" % (j % 2)], w=[n], b=[n])
+        task("v", [ts(T.a0[:, ch(j)], T.ar[:, ch(j)], 32767, A.bitwise_and), ts(T.a1[:, j % NA, :], T.ar[:, ch(j)], 15, A.logical_shift_right)], 1024,
+             r=["ar%d" % j], w=["a0%d" % j, "a1%d" % (j % NA)])
+        lead[0] += PLEAD
+        task("s", act(T[n][:], T.a1[:, j % NA, :]), 512, r=["a1%d" % (j % NA)], w=[n], b=[n])
         task("v", tt(T.MM[:, ch(j)], T.a0[:, ch(j)], T[n][:], A.min), 512, r=[n, "a0%d" % j], w=["MM%d" % j], b=[n])
-        task("s", [act(T.U1[:, ch(j)], T[n][:]), act(T.TT[:, ch(8 + j)], T[n][:])], 1024, r=[n], w=["U1%d" % j, "TU%d" % j], b=[n])
-        task("v", cp(T.TT[:, ch(j)], T.a0[:, ch(j)]), 512, r=["a0%d" % j], w=["TT%d" % j])
+        lead[0] = TLEAD * (8 - j) - T0LEAD
+        task("s", act(T.U1[:, ch(j)], T.a1[:, j % NA, :]), 512, r=["a1%d" % (j % NA)], w=["U1%d" % j])
+        task("s", act(T.TT[:, ch(8 + j)], T.a1[:, j % NA, :]), 512, r=["a1%d" % (j % NA)], w=["TU%d" % j])
+        e, f = ("s", act) if j in T0S else ("v", cp)
+        task(e, f(T.TT[:, ch(j)], T.a0[:, ch(j)]), 512, r=["a0%d" % j], w=["TT%d" % j])
         U0, un = (T.WW, "WW") if j < 6 else (T.GA, "GA")
-        task("s", act(U0[:, ch(j % 6)], T.TT[:, ch(j)]), 512, r=["TT%d" % j], w=["%s%d" % (un, j % 6)])
+        if j in U0G:
+            task("g", lambda q, o=U0[:, ch(j % 6)], i=T.TT[:, ch(j)]: q.affine_select(o, i, [[0, 512]], A.is_gt, 0.0, 1, 0), 1230, r=["TT%d" % j], w=["%s%d" % (un, j % 6)])
+        else:
+            e, f = ("v", cp) if j in U0V else ("s", act)
+            task(e, f(U0[:, ch(j % 6)], T.a0[:, ch(j)]), 512, r=["a0%d" % j], w=["%s%d" % (un, j % 6)])
         if j % 2:
             c, two = slice(512 * j - 512, 512 * j + 512), (j - 1, j)
             load("y", [dma(T.TT[0:128:2, W_ + c.start:W_ + c.stop], U0[1:128:2, 512 * (j % 6) - 512:512 * (j % 6) + 512]), dma(T.TT[1:128:2, c], T.U1[0:128:2, c])], 512,
@@ -285,19 +317,23 @@ def rank_program(g, core, T, topo):
         cg, lanes, cols, odd = slice(8 * x, 8 * x + 8), slice(128 * x, 128 * x + 128), slice(64 * x, 64 * x + 64), slice(16 * x + 1, 16 * x + 17, 2)
         Kn, Mn = "K%d" % x, "M%d" % x
         K, M = T[Kn], T[Mn]
+        lead[0] = (LEAD if t < V_ - 1 else LEAD4) * (NB - 1 - x) + CHAIN
         def nm(s): return "%s%d" % (s, x)
         xi, ri, xo, ro = ["%s%d%d" % (s, t, x) for s in ("xi", "ri", "xo", "ro")]
         pieces = (2 * x, 2 * x + 1)
-        GSs, GAs, GS0 = ["GS%d" % j for j in pieces], ["GA%d" % j for j in pieces], T.GS[:, 1024 * x:1024 * x + 1024:8]
+        GSs, GAs, GS0 = ["GS%d.%d" % (j, i) for j in pieces for i in range(0, 512, MCUT)], ["GA%d" % j for j in pieces], T.GS[:, 1024 * x:1024 * x + 1024:8]
 
         task("v", ts(T.sth[:, cols], T.xi[:, t, cols], -2048.0, A.add), 64, r=[xi], w=[nm("sth")])
         for j in pieces:
             n = (Mn, Kn)[j % 2]
             spread(n, T.ri, t, ri, j)
-            task("s", act(T.G[:, ch(j)], T.MM[:, 0:W_].indirect(T.xi[:, t, 32 * j:32 * j + 32]), bias=UP, scale=2.0 ** -12), 80 + 512 * GATHER,
-                 r=MMs + [xi], w=["G%d" % j])
-            bk = back(512 * j, 512 * j + 512)
-            task("v", scan(T.GS[:, bk], T[n][:, REV], T.G[:, bk], A.add, A.min), 512, r=["G%d" % j], w=[n, "GS%d" % j], b=[n])
+            win = T.MM[:, 0:W_].indirect(T.xi[:, t, 32 * j:32 * j + 32])
+            if j in OWN1: task("v", ts(T.G[:, ch(j)], win, 2.0 ** -12, A.mult, UP, A.add), 60 + 512 * GATHER, r=MMs + [xi], w=["G%d" % j])
+            else: task("s", act(T.G[:, ch(j)], win, bias=UP, scale=2.0 ** -12), 80 + 512 * GATHER, r=MMs + [xi], w=["G%d" % j])
+            if STAG and (t or x) and t < SEND: tasks[-1]["after"] = [max(n for n, k in enumerate(tasks) if STAG % ((x - 1) % NB) in k["w"])]
+            for i in range(0, 512, MCUT):
+                bk = back(512 * j + i, 512 * j + i + MCUT)
+                task("v", scan(T.GS[:, bk], T[n][:, back(i, i + MCUT)], T.G[:, bk], A.add, A.min), MCUT, r=["G%d" % j, n], w=["GS%d.%d" % (j, i)], b=[n])
         task("t", [mm(K[:, 0:128], T.ri[0:66, t, lanes], T.sL[0:66], True, False), mm(K[:, 0:128], GS0, T.Ib[:, 0, :], False, True)], 256,
              r=[ri, "sL", "sLc", "Ib"] + GSs, w=[Kn], b=[Kn])
         task("v", tt(K[:, 0:128], K[:, 0:128], T.acT[:, lanes], A.add), 128, r=["acT"], w=[Kn], b=[Kn])
@@ -313,12 +349,13 @@ def rank_program(g, core, T, topo):
         task("t", [mm(M[:, 0:128], T.Lm[:], T.UT[:, lanes]), mm(M[:, 256:384], T.Lh[:], T.UT[:, lanes])], 256, r=[nm("UT"), "Lm", "Lh"], w=[Mn], b=[Mn])
         task("v", tt(T.MH[:, lanes], M[:, 256:384], GS0, A.mult), 128, r=[Mn] + GSs, w=[nm("MH")], b=[Mn])
         for j in pieces:
-            task("s", act(T.GA[:, ch(j)], T.TT[:, 0:2 * W_].indirect(T.ix2[:, 32 * j:32 * j + 32])), 80 + 512 * GATHER, r=TTs + [nm("ix2")], w=["GA%d" % j])
+            e, f = ("v", cp) if j in OWN2 else ("s", act)
+            task(e, f(T.GA[:, ch(j)], T.TT[:, 0:2 * W_].indirect(T.ix2[:, 32 * j:32 * j + 32])), 80 + 512 * GATHER, r=TTs + [nm("ix2")], w=["GA%d" % j])
         ga = [T.GA[:, 1024 * x + k:1024 * x + 1024:8] for k in range(8)]
-        for h in range(2):
-            ks = range(4 * h, 4 * h + 4)
-            task("v", [tt(ga[k], M[:, 0:128], ga[k], A.mult) for k in ks], 512, r=[Mn] + GAs, w=["GB%d%d" % (x, h)], b=[Mn])
-            task("t", [mm(K[:, 384 + k:512:8], ga[k], T.sC[:]) for k in ks], 1024, r=["sC", "GB%d%d" % (x, h)] + GAs, w=[Kn], b=[Kn])
+        for h in range(0, 8, KCUT):
+            ks = range(h, h + KCUT)
+            task("v", [tt(ga[k], M[:, 0:128], ga[k], A.mult) for k in ks], 128 * KCUT, r=[Mn] + GAs, w=["GB%d%d" % (x, h)], b=[Mn])
+            task("t", [mm(K[:, 384 + k:512:8], ga[k], T.sC[:]) for k in ks], 256 * KCUT, r=["sC", "GB%d%d" % (x, h)] + GAs, w=[Kn], b=[Kn])
         task("s", [act(T.kb[:, lanes], K[:, 384:512], bias=UP, scale=2.0 ** -12), act(T.AF[:, lanes], K[:, 384:512], bias=129 * 4096.0 - 2048)], 256,
              r=[Kn], w=[nm("kb")], b=[Kn])
         task("t", [mm(K[:, 0:128], I1, T.AF[:, lanes], True, False)] + [mm(K[:, 0:128], T.Ib[:, i, :], T.kb[:, lanes], False, False) for i in (1, 2)]
@@ -357,22 +394,31 @@ def rank_program(g, core, T, topo):
             send(T.xi[:, t + 1, cols], T.xo[:, t, cols], "m" + sem, 1, [xo], ["xi" + sem])
             send(T.ri[:, t + 1, lanes], T.ro[:, t, lanes], "n" + sem, 1, [ro, "roc"], ["ri" + sem])
 
-    def payload(t, x, gate):
-        lanes, pieces, Kn, Mn = slice(128 * x, 128 * x + 128), (2 * x, 2 * x + 1), "K%d" % x, "M%d" % x
+    def behind(name):
+        if name: tasks[-1]["after"] = [max(n for n, k in enumerate(tasks) if name in k["w"])]
+
+    def fetch(t, j, gate):
+        x = j // 2
+        d = "M%d" % x if t == V_ - 1 and j % 2 else "D"
+        spread(d, T.ro, t, "ro%d%d" % (t, x), j)
+        task("s", act(T.GP[:, ch(j)], T.pr[:, 0:W_].indirect(T.xo[:, t, 32 * j:32 * j + 32])), 80 + 512 * GATHER, r=["pr", "xo%d%d" % (t, x)], w=["GP%d" % j])
+        behind(gate)
+        task("s", act(T.WW[:, ch(j)], T[d][:], F.Exp, scale=-0.125), 512, r=[d], w=["WW%d" % j], b=[d])
+        behind(gate)
+
+    def horner(t, j, gate):
+        for i in range(0, 512, CUT):
+            bk = back(512 * j + i, 512 * j + i + CUT)
+            for S, op, n in ((T.U1, A.add, "U1"), (T.S1, A.max, "S1")):
+                task("v", scan(S[:, bk], T.WW[:, bk], T.GP[:, bk], A.mult, op), CUT, r=["WW%d" % j, "GP%d" % j, "TU7"], w=["%s%d.%d" % (n, j, i)])
+                behind(gate)
+        if j % 2: hand_back(t, j // 2)
+
+    def hand_back(t, x):
+        lanes, Kn = slice(128 * x, 128 * x + 128), "K%d" % x
         K = T[Kn]
         def nm(s): return "%s%d" % (s, x)
-        xo, ro = ["%s%d%d" % (s, t, x) for s in ("xo", "ro")]
-        Ss, late = [], ["xo%d%d" % (t + 1, LATE[x])] if gate and LATE[x] >= 0 and t < LEND else []
-        for j in pieces:
-            d = Mn if t == V_ - 1 and j % 2 else "D"
-            spread(d, T.ro, t, ro, j)
-            task("s", act(T.GP[:, ch(j)], T.pr[:, 0:W_].indirect(T.xo[:, t, 32 * j:32 * j + 32])), 80 + 512 * GATHER, r=["pr", xo] + gate, w=["GP%d" % j])
-            task("s", act(T.WW[:, ch(j)], T[d][:], F.Exp, scale=-0.125), 512, r=[d] + gate, w=["WW%d" % j], b=[d])
-            for i in range(0, 512, CUT):
-                bk = back(512 * j + i, 512 * j + i + CUT)
-                for S, op, n in ((T.U1, A.add, "U1"), (T.S1, A.max, "S1")):
-                    Ss.append("%s%d.%d" % (n, j, i))
-                    task("v", scan(S[:, bk], T.WW[:, bk], T.GP[:, bk], A.mult, op), CUT, r=["WW%d" % j, "GP%d" % j, "TU7"] + late, w=Ss[-1:])
+        Ss = ["%s%d.%d" % (n, j, i) for n in ("U1", "S1") for j in (2 * x, 2 * x + 1) for i in range(0, 512, CUT)]
         part, both = [slice(256 * x + 128 * h, 256 * x + 128 * h + 128) for h in range(2)], slice(256 * x, 256 * x + 256)
         last = [(T.U1, T.S1)[h][:, 1024 * x:1024 * x + 1024:8] for h in range(2)]
         def turned(s): return T.I2[:, 128 - 16 * (V_ - 1 - s):256 - 16 * (V_ - 1 - s)]
@@ -396,9 +442,16 @@ def rank_program(g, core, T, topo):
                 load(e, [dma(y[0:128 - cut, lanes], T.YO[cut:128, part[h]]), dma(y[128 - cut:128, lanes], T.YO[0:cut, part[h]])], 64,
                      r=[nm("YO")], w=["out%d%d" % (x, h)])
 
+    lead.append(0)
     for t in range(V_ + 1):
         for x in range(NB if t < V_ else 0): visit(t, x)
-        for x in range(NB if t else 0): payload(t - 1, x, [GATE[x]] if t <= DEFER and GATE[x] else [])
+        lead[0] = 0
+        for j in range(6 if 2 <= t < V_ else 0):
+            if LATE[j][0] == 2: horner(t - 2, j, LATE[j][1])
+        for j in range(6 if t else 0):
+            fetch(t - 1, j, GATE if t < V_ - 1 else GATE4 if t < V_ else None)
+            if t >= V_ - 1: horner(t - 1, j, LAST if t < V_ else None)
+            elif LATE[j][0] == 1: horner(t - 1, j, LATE[j][1] % t)
     task("y", [], 0, r=["out%d%d" % (x, h) for x in range(NB) for h in range(2)])
     emit(g, T, arrange(tasks))
     g.wait_ge(T.sem.gone, sent[0])

@@ -6,12 +6,12 @@ F = ActivationFunctionType
 V_, L_, W_, NB = 5, 384, 4096, 3
 f32, bf, f16, i32, u16 = "float32", "bfloat16", "float16", "int32", "uint16"
 SCRATCH = {
-    "ar": ("sbuf", [128, W_], i32), "a0": ("sbuf", [128, W_], i32), "a1": ("sbuf", [128, 3, 512], i32),
-    "U1": ("sbuf", [128, W_], f32), "TT": ("sbuf", [128, 2 * W_], f32), "MM": ("sbuf", [128, W_], f32), "pr": ("sbuf", [128, W_], bf),
+    "ar": ("sbuf", [128, W_], i32), "a0": ("sbuf", [128, W_], i32), "a1": ("sbuf", [128, 2048], i32),
+    "TT": ("sbuf", [128, 2 * W_], i32), "MM": ("sbuf", [128, W_], f32), "pr": ("sbuf", [128, W_], bf),
     "acs": ("sbuf", [128, L_], f32), "acT": ("sbuf", [128, L_], f32),
     "rsi": ("sbuf", [128, L_], i32), "sti": ("sbuf", [128, 192], i32), "sS": ("sbuf", [128, 8, 136], f32),
     "G": ("sbuf", [128, 3072], bf), "GS": ("sbuf", [128, 3072], bf), "GA": ("sbuf", [128, 3072], f32),
-    "GP": ("sbuf", [128, 3072], bf), "WW": ("sbuf", [128, 3072], f32), "S1": ("sbuf", [128, 3072], f32),
+    "GP": ("sbuf", [128, 3072], bf), "S0": ("sbuf", [128, 3072], f32), "WW": ("sbuf", [128, 3072], f32), "S1": ("sbuf", [128, 3072], f32),
     "sc": ("sbuf", [128, L_], f32), "UU": ("sbuf", [128, L_], bf), "UT": ("sbuf", [128, L_], bf),
     "MH": ("sbuf", [128, L_], bf), "sth": ("sbuf", [128, 192], f16), "ix2": ("sbuf", [128, 192], u16), "kb": ("sbuf", [128, L_], bf),
     "k1": ("sbuf", [128, L_], f32), "DD": ("sbuf", [128, 24, 17], f16), "pen": ("sbuf", [128, L_], f32), "AF": ("sbuf", [128, L_], f32),
@@ -32,18 +32,35 @@ SCRATCH = {
 POOL = {"v": 30, "s": 26, "t": 26, "g": 16, "d": 18}
 SEMAPHORES = (["%s%d" % (e, i) for e in POOL for i in range(POOL[e])] + ["gone"]
               + ["%s%d%d" % (n, t, b) for n, k in (("m", 5), ("n", 5), ("x", 4)) for t in range(1, k) for b in range(NB)])
-SLACK = 0
+SLACK = 80
 GATE = "kb1"
 LAST = None
 LEAD = 1000
-LEAD4 = 1500
+LEAD4 = 3000
 GATE4 = "kb2"
-SHORT = {"s": 2000, "v": 500, "t": 2000, "g": 0, "y": 0}
-CHAIN = 20000
+SHORT = {"s": 5000, "v": 2000, "t": 0, "g": 0, "y": 0}
+CHAIN = 1
 T0LEAD = 0
 NA = 3
+U16 = 1
+U17 = 1
+XG = 1
+STH = 0
+APART = 4
+SMALL = 8
+SLEAD = 0
+OWN5 = (1,)
+OWN6 = (5,)
+BYDMA = 2
+DDA = 0
+FREE = 0
+GROUPS = ((0,), (1,), (2,))
+PASSES = 2
+EARLY = 2
+OWN3 = (1, 5)
+OWN4 = (1, 3, 5)
 SETUP = 30000
-PLEAD = 3000
+PLEAD = 0
 PARTS = ((0, 1), (1, 2), (2, 4), (4, 6), (6, 8))
 T0S = (0, 1, 2)
 U0G = (0, 1, 2, 3, 4, 5, 6)
@@ -52,16 +69,17 @@ OWN1 = (1,)
 OWN2 = (5,)
 STAG = 0
 SEND = 5
-MCUT = 512
-KCUT = 4
+MCUT = 256
+KCUT = 2
 LATE = ((1, "xo%d0"),) * 6
-TLEAD = 2000
+TLEAD = 2500
 CUT = 256
 HOP = 230
-REMOTE = 2500
+REMOTE = 2800
 ISSUE = 300
 PEF = 0.5
-LOCAL, GATHER = 2600, 1.56
+LOCAL = 2600
+GATHER = 1.56
 ALL, REV = slice(None), slice(None, None, -1)
 
 
@@ -82,13 +100,13 @@ def network(steps, at):
     for fix in range(4):
         side = [sorted(p, key=lambda w: (at[w][0], at[w][1] >> fix & 1)) for p in pairs]
         order = sorted(range(len(pairs)), key=(lambda n: pairs[n][0]) if kind == "e" else (lambda n: at[side[n][0]][1]))
-        for key in range(f if kind == "s" else 1):
+        for key in range(f if kind in "sn" else 1):
             for pos in range(f + 1 if kind == "u" else f if kind == "s" else 1):
                 calls, new = [], {}
-                for mx in range(1 if kind == "m" else 2):
-                    for v in range(2 if kind == "s" else 1):
-                        part = [n for i, n in enumerate(order) if kind != "s" or i >> key & 1 == v]
-                        mem = {"b": 1 if mx else 0, "s": v}.get(kind, 1)
+                for mx in range(1 if kind in "mn" else 2):
+                    for v in range(2 if kind in "sn" else 1):
+                        part = [n for i, n in enumerate(order) if kind not in "sn" or i >> key & 1 == v]
+                        mem = {"b": 1 if mx else 0, "s": v, "n": v}.get(kind, 1)
                         out = [(i >> pos << pos + 1 | mx << pos | i & (1 << pos) - 1) if kind in "us" else i for i in range(len(part))]
                         new.update((pairs[n][mx], (mem, o)) for n, o in zip(part, out))
                         a, b = [(at[side[part[0]][h]][0], box([at[side[n][h]][1] for n in part], bits[at[side[part[0]][h]][0]])) for h in range(2)]
@@ -121,23 +139,29 @@ def arrange(tasks):
     for n in range(n_ - 1, -1, -1):
         way[n] = tasks[n]["c"] + tasks[n]["lat"] + max([hop(n, u) + way[u] for u in users[n]] + [0])
         for m in dep[n]: users[m].append(n)
-    left, ready, done = [len(d) for d in dep], [0] * n_, []
-    free, bank, open_ = {}, {}, [n for n in range(n_) if not dep[n]]
-    while open_:
-        def start(n):
+    def run(before, behind, urge, forward):
+        left, ready, done, ends = [len(d) for d in before], [0 if forward else k["lat"] for k in tasks], [], [0] * n_
+        free, bank, open_ = {}, {}, [n for n in range(n_) if not before[n]]
+        while open_:
+            def start(n):
+                k = tasks[n]
+                return max([ready[n], free.get(k["e"], 0)] + [t + HOP for b in k["b"] for e, t in bank.get(b, {}).items() if e != k["e"]])
+            first, n = min((start(n), n) for n in open_)
+            n = max((m for m in open_ if tasks[m]["e"] == tasks[n]["e"] and start(m) <= first + SLACK), key=lambda m: (urge[m], -m))
             k = tasks[n]
-            return max([ready[n], free.get(k["e"], 0)] + [t + HOP for b in k["b"] for e, t in bank.get(b, {}).items() if e != k["e"]])
-        first, n = min((start(n), n) for n in open_)
-        n = max((m for m in open_ if tasks[m]["e"] == tasks[n]["e"] and start(m) <= first + SLACK), key=lambda m: (way[m] + tasks[m]["lead"], -m))
-        k = tasks[n]
-        end = start(n) + k["c"]
-        if k["e"] != "x": free[k["e"]] = end
-        for b in k["b"]: bank.setdefault(b, {})[k["e"]] = end
-        open_.remove(n); done.append(k)
-        for u in users[n]:
-            ready[u] = max(ready[u], end + k["lat"] + hop(n, u)); left[u] -= 1
-            if not left[u]: open_.append(u)
-    return done
+            end = ends[n] = start(n) + k["c"]
+            if k["e"] != "x": free[k["e"]] = end
+            for b in k["b"]: bank.setdefault(b, {})[k["e"]] = end
+            open_.remove(n); done.append(k)
+            for u in behind[n]:
+                ready[u] = max(ready[u], end + (k["lat"] + hop(n, u) if forward else tasks[u]["lat"] + hop(u, n))); left[u] -= 1
+                if not left[u]: open_.append(u)
+        return max(e + k["lat"] for e, k in zip(ends, tasks)), done, ends
+    best = now = run(dep, users, [way[n] + tasks[n]["lead"] for n in range(n_)], True)
+    for _ in range(PASSES):
+        now = run(dep, users, run(users, dep, now[2], False)[2], True)
+        if now[0] < best[0]: best = now
+    return best[1]
 
 
 def emit(g, T, tasks):
@@ -220,7 +244,8 @@ def rank_program(g, core, T, topo):
         load("y", [dma(T.ar[:, 512 * a:512 * b], T.arcs[:, 512 * a:512 * b])], 256 * b, w=["ar%d" % j for j in range(a, b)])
     lead[0] = 10 ** 5
     load("s", [dma(T.sti[:, :], T.st0[:, :])], 300, w=["sti"])
-    load("y", [dma(T.rsi[0:64, :], T.rs0[:, :]), dma(T.acs[:, :], T.ac[:, :])], 2500, w=["rsi", "acs"])
+    lead[0] = 10 ** 6 * (8 - SMALL) + 1
+    load("y", [dma(T.rsi[0:64, :], T.rs0[:, :]), dma(T.acs[:, :], T.ac[:, :])], 256 * SMALL + 400, w=["rsi", "acs"])
     lead[0] = 0
 
     task("v", [ms(T.Z[:], 0.0), ms(T.Zf[:], 0.0)], 704, w=["Z"])
@@ -256,43 +281,38 @@ def rank_program(g, core, T, topo):
     task("v", ts(T.col[:, 5:6], T.col[:, 4:5], T.col[:, 6:7], A.add), 64, r=["col4"], w=["col5"])
     task("s", [act(T.sC[:, :, u], T.Bk[:, 0:8, 0], scale=T.col[:, u:u + 1]) for u in range(2)] + [act(T.sM[:], T.Bk[:, 0:8, :], scale=-1.0 / 128)]
          + [act(T.Lp[:, b, :, b, :], T.Bk[:, 1:9, 0:8], scale=T.col[:, 5:6]) for b in range(2)], 400, r=["Bk", "col", "col5", "Lp"], w=["sC", "Lp"])
-    task("s", [act(T.ro[64:128, t, :], T.Z[64:128, 0:L_], bias=1.0) for t in range(V_)], V_ * L_, r=["Z"], w=["roc"])
+    task("s", [act(T.ro[64:128, t, :], T.Z[64:128, 0:L_], F.Exp) for t in range(V_)], V_ * L_ + 1600, r=["Z"], w=["roc"])
     task("s", [act(T.sS[:, a:a + 4], T.Z[:, 0:544]) for a in (0, 4)], 1088, r=["Z"], w=["sS"])
     paint("sS", T.sS[:, :, 7:135:8], 128, [[-2, 8], [-16, 8], [-1, 2]], 1.0, 0, 1)
-    task("s", act(T.ri[0:64, 0, :], T.rsi[0:64, :], bias=98.0, scale=-1.0), 384, r=["rsi", "ri0c"], w=each("ri0"))
     lead[0] = 10 ** 5
     task("s", act(T.AF[:, 0:192], T.sti[:]), 192, r=["sti"], w=["kb1"])
     lead[0] = 0
     for q in range(8):
         task("t", [mm(T.K0[:, q:192:8], T.sS[:, q, 7 - k:135 - k], T.AF[:, 24 * k:24 * k + 24], k == 0, k == 7) for k in range(8)], 2048, r=["sS", "kb1"], w=["K0"], b=["K0"])
-    task("v", cp(T.xi[:, 0, :], T.K0[:, 0:192]), 192, r=["K0"], w=each("xi0"), b=["K0"])
+    task("s", act(T.xi[:, 0, :], T.K0[:, 0:192]), 192, r=["K0"], w=each("xi0"), b=["K0"])
 
     for j in range(8):
         n = ("K2", "D", "M0", "M1")[j % 4]
         lead[0] = TLEAD * (8 - j)
-        task("v", [ts(T.a0[:, ch(j)], T.ar[:, ch(j)], 32767, A.bitwise_and), ts(T.a1[:, j % NA, :], T.ar[:, ch(j)], 15, A.logical_shift_right)], 1024,
-             r=["ar%d" % j], w=["a0%d" % j, "a1%d" % (j % NA)])
+        a1, h1 = (T.a1, "b") if j < APART else (T.ar, "ar")
+        task("v", ts(T.a0[:, ch(j)], T.ar[:, ch(j)], 32767, A.bitwise_and), 512, r=["ar%d" % j], w=["a%d" % j])
+        task("v", ts(a1[:, ch(j)], T.ar[:, ch(j)], 15, A.logical_shift_right), 512, r=["ar%d" % j], w=[h1 + str(j)])
         lead[0] += PLEAD
-        task("s", act(T[n][:], T.a1[:, j % NA, :]), 512, r=["a1%d" % (j % NA)], w=[n], b=[n])
-        task("v", tt(T.MM[:, ch(j)], T.a0[:, ch(j)], T[n][:], A.min), 512, r=[n, "a0%d" % j], w=["MM%d" % j], b=[n])
-        lead[0] = TLEAD * (8 - j) - T0LEAD
-        task("s", act(T.U1[:, ch(j)], T.a1[:, j % NA, :]), 512, r=["a1%d" % (j % NA)], w=["U1%d" % j])
-        task("s", act(T.TT[:, ch(8 + j)], T.a1[:, j % NA, :]), 512, r=["a1%d" % (j % NA)], w=["TU%d" % j])
-        e, f = ("s", act) if j in T0S else ("v", cp)
-        task(e, f(T.TT[:, ch(j)], T.a0[:, ch(j)]), 512, r=["a0%d" % j], w=["TT%d" % j])
-        U0, un = (T.WW, "WW") if j < 6 else (T.GA, "GA")
-        if j in U0G:
-            task("g", lambda q, o=U0[:, ch(j % 6)], i=T.TT[:, ch(j)]: q.affine_select(o, i, [[0, 512]], A.is_gt, 0.0, 1, 0), 1230, r=["TT%d" % j], w=["%s%d" % (un, j % 6)])
-        else:
-            e, f = ("v", cp) if j in U0V else ("s", act)
-            task(e, f(U0[:, ch(j % 6)], T.a0[:, ch(j)]), 512, r=["a0%d" % j], w=["%s%d" % (un, j % 6)])
+        task("s", act(T[n][:], a1[:, ch(j)]), 512, r=[h1 + str(j)], w=[n], b=[n])
+        task("v", tt(T.MM[:, ch(j)], T.a0[:, ch(j)], T[n][:], A.min), 512, r=[n, "a%d" % j], w=["MM%d" % j], b=[n])
+        lead[0] = TLEAD * (8 - j)
+        if j >= BYDMA:
+            task("s", act(T.TT[:, ch(8 + j)], a1[:, ch(j)]), 512, r=[h1 + str(j)], w=["TU%d" % j])
+            task("s", act(T.TT[:, ch(j)], T.a0[:, ch(j)]), 512, r=["a%d" % j], w=["TT%d" % j])
         if j % 2:
             c, two = slice(512 * j - 512, 512 * j + 512), (j - 1, j)
-            load("y", [dma(T.TT[0:128:2, W_ + c.start:W_ + c.stop], U0[1:128:2, 512 * (j % 6) - 512:512 * (j % 6) + 512]), dma(T.TT[1:128:2, c], T.U1[0:128:2, c])], 512,
-                 r=["%s%d" % (un, i % 6) for i in two] + ["U1%d" % i for i in two], w=["T%s%d" % (h, i) for i in two for h in "TU"])
-    lead[0] = 0
+            load("y", [dma(T.TT[0:128:2, W_ + c.start:W_ + c.stop], T.a0[1:128:2, c]), dma(T.TT[1:128:2, c], a1[0:128:2, c])]
+                 + [dma(T.TT[0:128:2, c], T.a0[0:128:2, c]), dma(T.TT[1:128:2, W_ + c.start:W_ + c.stop], a1[1:128:2, c])] * (j < BYDMA), 512,
+                 r=["%s%d" % (h, i) for i in two for h in ("a", h1)], w=["T%s%d" % (h, i) for i in two for h in "TU"])
+    lead[0] = SLEAD
+    task("s", act(T.ri[0:64, 0, :], T.rsi[0:64, :], bias=98.0, scale=-1.0), 384, r=["rsi", "ri0c"], w=each("ri0"))
     task("t", [lambda q, c=c: q.transpose(T.M2[:, 128 * c:128 * c + 128], T.acs[:, 128 * c:128 * c + 128], I1) for c in range(3)], 1536,
-         r=["acs", "I2", "a05"], w=["M2"], b=["M2"])
+         r=["acs", "I2"], w=["M2"], b=["M2"])
     task("s", act(T.acT[:], T.M2[:, 0:L_]), 384, r=["M2"], w=["acT"], b=["M2"])
     load("y", [dma(T.pr[16:128, :], T.pay[0:112, :]), dma(T.pr[0:16, :], T.pay[112:128, :])], 1024, r=["TU7"], w=["pr"])
     MMs, TTs = ["MM%d" % j for j in range(8)], ["T%s%d" % (h, j) for j in range(8) for h in "TU"]
@@ -309,7 +329,8 @@ def rank_program(g, core, T, topo):
         task("t", [mm(T[n][:, k:512:8], T.sD[0:66, k, :], R[0:66, t, 64 * j:64 * j + 64]) for k in range(8)], 512,
              r=["sD", "sDc", "roc", name], w=[n], b=[n])
 
-    ALL16, BEST8 = [network(list(zip((1, 3, 1, 7, 2, 1, 15, 4, 2, 1), kinds)), {i: (i & 1, i >> 1) for i in range(16)}) for kinds in ("bubusbusue", "bubusbmuue")]
+    NETS = {n: [network(list(zip((1, 3, 1, 7, 2, 1, 15, 4, 2, 1), kinds)), {i: (i & 1, i >> 1) for i in range(16)}) for kinds in both]
+            for n, both in ((1, ("bubusbusue", "bubusbmuue")), (2, ("bsbssbssse", "bsbssbnuse")))}
     UP = 128.5 + 2.0 ** -13
     SINK = 2 * (16 * 132 - 800) + 2047.0 / 4096
 
@@ -317,18 +338,18 @@ def rank_program(g, core, T, topo):
         cg, lanes, cols, odd = slice(8 * x, 8 * x + 8), slice(128 * x, 128 * x + 128), slice(64 * x, 64 * x + 64), slice(16 * x + 1, 16 * x + 17, 2)
         Kn, Mn = "K%d" % x, "M%d" % x
         K, M = T[Kn], T[Mn]
-        lead[0] = (LEAD if t < V_ - 1 else LEAD4) * (NB - 1 - x) + CHAIN
         def nm(s): return "%s%d" % (s, x)
         xi, ri, xo, ro = ["%s%d%d" % (s, t, x) for s in ("xi", "ri", "xo", "ro")]
         pieces = (2 * x, 2 * x + 1)
         GSs, GAs, GS0 = ["GS%d.%d" % (j, i) for j in pieces for i in range(0, 512, MCUT)], ["GA%d" % j for j in pieces], T.GS[:, 1024 * x:1024 * x + 1024:8]
 
-        task("v", ts(T.sth[:, cols], T.xi[:, t, cols], -2048.0, A.add), 64, r=[xi], w=[nm("sth")])
+        if STH: task("s", act(T.sth[:, cols], T.xi[:, t, cols], bias=-2048.0), 64, r=[xi], w=[nm("sth")])
+        else: task("v", ts(T.sth[:, cols], T.xi[:, t, cols], -2048.0, A.add), 64, r=[xi], w=[nm("sth")])
         for j in pieces:
             n = (Mn, Kn)[j % 2]
             spread(n, T.ri, t, ri, j)
             win = T.MM[:, 0:W_].indirect(T.xi[:, t, 32 * j:32 * j + 32])
-            if j in OWN1: task("v", ts(T.G[:, ch(j)], win, 2.0 ** -12, A.mult, UP, A.add), 60 + 512 * GATHER, r=MMs + [xi], w=["G%d" % j])
+            if j in (OWN5 if t == V_ - 1 else OWN1 if t >= EARLY else OWN3): task("v", ts(T.G[:, ch(j)], win, 2.0 ** -12, A.mult, UP, A.add), 60 + 512 * GATHER, r=MMs + [xi], w=["G%d" % j])
             else: task("s", act(T.G[:, ch(j)], win, bias=UP, scale=2.0 ** -12), 80 + 512 * GATHER, r=MMs + [xi], w=["G%d" % j])
             if STAG and (t or x) and t < SEND: tasks[-1]["after"] = [max(n for n, k in enumerate(tasks) if STAG % ((x - 1) % NB) in k["w"])]
             for i in range(0, 512, MCUT):
@@ -345,11 +366,11 @@ def rank_program(g, core, T, topo):
         task("t", [mm(K[:, 256:320], T.Ih[:, 0, :], T.sth[:, cols], True, False)]
              + [mm(K[:, 256:320], T.Lp[:, b], T.UT[:, 128 * x + b:128 * x + 128:2], False, b == 1) for b in range(2)], 192,
              r=[nm("UT"), nm("sth"), "Lp", "Ih"], w=[Kn], b=[Kn])
-        task("v", cp(T.ix2[:, cols], K[:, 256:320]), 64, r=[Kn], w=[nm("ix2")], b=[Kn])
+        task("vs"[U16], (cp, act)[U16](T.ix2[:, cols], K[:, 256:320]), 64, r=[Kn], w=[nm("ix2")], b=[Kn])
         task("t", [mm(M[:, 0:128], T.Lm[:], T.UT[:, lanes]), mm(M[:, 256:384], T.Lh[:], T.UT[:, lanes])], 256, r=[nm("UT"), "Lm", "Lh"], w=[Mn], b=[Mn])
         task("v", tt(T.MH[:, lanes], M[:, 256:384], GS0, A.mult), 128, r=[Mn] + GSs, w=[nm("MH")], b=[Mn])
         for j in pieces:
-            e, f = ("v", cp) if j in OWN2 else ("s", act)
+            e, f = ("v", cp) if j in (OWN6 if t == V_ - 1 else OWN2 if t >= EARLY else OWN4) else ("s", act)
             task(e, f(T.GA[:, ch(j)], T.TT[:, 0:2 * W_].indirect(T.ix2[:, 32 * j:32 * j + 32])), 80 + 512 * GATHER, r=TTs + [nm("ix2")], w=["GA%d" % j])
         ga = [T.GA[:, 1024 * x + k:1024 * x + 1024:8] for k in range(8)]
         for h in range(0, 8, KCUT):
@@ -362,17 +383,11 @@ def rank_program(g, core, T, topo):
              + [mm(K[:, 0:128], T.ri[0:66, t, lanes], T.sP[0:66], False, False), mm(K[:, 0:128], T.MH[:, lanes], T.sM[:], False, True)], 1024,
              r=[nm("kb"), nm("MH"), ri, "sP", "sPc", "sC", "Ib", "I2"], w=[Kn], b=[Kn])
         task("s", act(T.SB0[:, cg, 0], K[:, 1:128:2]), 64, r=[Kn], w=[nm("so0")], b=[Kn])
-
-        def view(pp, place): return T.S[(ALL, cg, pp) + place[1]] if place[0] == 0 else (T.SB0, T.SB1)[pp][(ALL, cg) + place[1]]
-
-        def sort(steps, first, last, w):
-            for n, calls in enumerate(steps):
-                pp, head, end = n % 2, n == 0 and first is not None, n == len(steps) - 1
-                task("v", [tt(last(mx) if end else view(1 - pp, o), first if head else view(pp, i0), view(pp, i1), A.max if mx else A.min) for mx, o, i0, i1, _ in calls],
-                     sum(max(64, 8 * k * (i0[0] + i1[0])) for _, _, i0, i1, k in calls), r=[nm("so%d" % pp)] + [Kn] * head,
-                     w=[w if end else nm("so%d" % (1 - pp))], b=["S"] + [Kn] * head)
-        sort(ALL16, K[:, 0:128:2], lambda mx: T.k1[:, 128 * x + mx:128 * x + 128:2], nm("k1"))
-        task("v", ts(T.DD[:, cg, 1:17], T.k1[:, lanes], 1.5 * 2 ** 23, A.add, 1.5 * 2 ** 23, A.subtract), 128, r=[nm("k1")], w=[nm("DD")])
+        yield
+        if DDA:
+            task("s", act(T.rsi[:, lanes], T.k1[:, lanes]), 128, r=[nm("k1")] + each("ri0"), w=[nm("rs")])
+            task("s", act(T.DD[:, cg, 1:17], T.rsi[:, lanes]), 128, r=[nm("rs")], w=[nm("DD")])
+        else: task("v", ts(T.DD[:, cg, 1:17], T.k1[:, lanes], 1.5 * 2 ** 23, A.add, 1.5 * 2 ** 23, A.subtract), 128, r=[nm("k1")], w=[nm("DD")])
         task("t", mm(M[:, 0:128], T.I4[:], T.k1[:, lanes], True, False), 512, r=[nm("k1"), "Ib"], w=[Mn], b=[Mn])
         task("t", [mm(K[:, 0:128], T.Ih[:, 0, :], T.DD[:, cg, 0:16], True, False), mm(K[:, 0:128], T.Ih[:, 1, :], T.DD[:, cg, 1:17], False, True)], 256,
              r=[nm("DD"), "Ih"], w=[Kn], b=[Kn])
@@ -380,19 +395,35 @@ def rank_program(g, core, T, topo):
         task("s", act(T.pen[:, lanes], K[:, 0:128], bias=SINK, scale=8192.0), 128, r=[Kn], w=[nm("pen")], b=[Kn])
         task("v", [tt((T.S, T.SB0)[v][:, cg, 0], M[:, v:128:2], T.pen[:, 128 * x + v:128 * x + 128:2], A.max) for v in range(2)], 128,
              r=[Mn, nm("pen")], w=[nm("so0")], b=[Mn, "S"])
-        sort(BEST8, None, lambda mx: T.kz[:, odd, mx:8:2], nm("kz"))
+        yield
         task("v", ts(T.tz[:, odd, :], T.kz[:, odd, :], 1.5 * 2 ** 24, A.add, 1.5 * 2 ** 24, A.subtract), 64, r=[nm("kz")], w=[nm("tz")])
         task("s", act(T.cb[:, cg], T.kz[:, odd, :], bias=180 - 15.0 / 32, scale=1.0 / 32), 64, r=[nm("kz")], w=[nm("cb")])
         for s, z in enumerate(("kz", "tz")):
             task("t", [mm(K[:, 0:64], T[z][:, 16 * x + 1 - b:16 * x + 17 - b, :], T.Df[:, s, b, :], s + b == 0, s + b == 2) for b in range(2)], 512,
                  r=[nm(z), "Df", "Dn", "zeros"], w=[Kn], b=[Kn])
-        task("v", ts(T.xo[:, t, cols], K[:, 0:64], 2048.0, A.add), 64, r=[Kn], w=[xo], b=[Kn])
+        if U17: task("s", act(T.xo[:, t, cols], K[:, 0:64], bias=2048.0), 64, r=[Kn], w=[xo], b=[Kn])
+        else: task("v", ts(T.xo[:, t, cols], K[:, 0:64], 2048.0, A.add), 64, r=[Kn], w=[xo], b=[Kn])
         task("t", mm(M[0:64, 0:128], T.cb[:, cg], T.Ib[:, 0, :]), 128, r=[nm("cb"), "Ib"], w=[Mn], b=[Mn])
         task("s", act(T.ro[0:64, t, lanes], M[0:64, 0:128], F.Abs, bias=-228.0), 128, r=[Mn], w=[ro], b=[Mn])
         if t < V_ - 1:
             sem = "%d%d" % (t + 1, x)
             send(T.xi[:, t + 1, cols], T.xo[:, t, cols], "m" + sem, 1, [xo], ["xi" + sem])
             send(T.ri[:, t + 1, lanes], T.ro[:, t, lanes], "n" + sem, 1, [ro, "roc"], ["ri" + sem])
+        yield
+
+    def sort(xs, second):
+        def view(ys, pp, place):
+            cg = slice(8 * ys[0], 8 * ys[-1] + 8)
+            return T.S[(ALL, cg, pp) + place[1]] if place[0] == 0 else (T.SB0, T.SB1)[pp][(ALL, cg) + place[1]]
+        def last(mx): return T.kz[:, 16 * xs[0] + 1:16 * xs[-1] + 17:2, mx:8:2] if second else T.k1[:, 128 * xs[0] + mx:128 * xs[-1] + 128:2]
+        steps = NETS[min(len(xs), 2)][second]
+        for n, calls in enumerate(steps):
+            pp, head, end = n % 2, n == 0 and not second, n == len(steps) - 1
+            for ys in [(x,) for x in xs] if head else [xs]:
+                Kn = ["K%d" % ys[0]] * head
+                task("v", [tt(last(mx) if end else view(ys, 1 - pp, o), T[Kn[0]][:, 0:128:2] if head else view(ys, pp, i0), view(ys, pp, i1), A.max if mx else A.min)
+                           for mx, o, i0, i1, _ in calls], sum(max(64, 8 * len(ys) * k * (i0[0] + i1[0])) for _, _, i0, i1, k in calls),
+                     r=["so%d%d" % (pp, y) for y in ys] + Kn, w=["%s%d" % (("k1", "kz")[second] if end else "so%d" % (1 - pp), y) for y in ys], b=["S"] + Kn)
 
     def behind(name):
         if name: tasks[-1]["after"] = [max(n for n, k in enumerate(tasks) if name in k["w"])]
@@ -409,8 +440,8 @@ def rank_program(g, core, T, topo):
     def horner(t, j, gate):
         for i in range(0, 512, CUT):
             bk = back(512 * j + i, 512 * j + i + CUT)
-            for S, op, n in ((T.U1, A.add, "U1"), (T.S1, A.max, "S1")):
-                task("v", scan(S[:, bk], T.WW[:, bk], T.GP[:, bk], A.mult, op), CUT, r=["WW%d" % j, "GP%d" % j, "TU7"], w=["%s%d.%d" % (n, j, i)])
+            for S, op, n in ((T.S0, A.add, "S0"), (T.S1, A.max, "S1")):
+                task("v", scan(S[:, bk], T.WW[:, bk], T.GP[:, bk], A.mult, op), CUT, r=["WW%d" % j, "GP%d" % j], w=["%s%d.%d" % (n, j, i)])
                 behind(gate)
         if j % 2: hand_back(t, j // 2)
 
@@ -418,9 +449,9 @@ def rank_program(g, core, T, topo):
         lanes, Kn = slice(128 * x, 128 * x + 128), "K%d" % x
         K = T[Kn]
         def nm(s): return "%s%d" % (s, x)
-        Ss = ["%s%d.%d" % (n, j, i) for n in ("U1", "S1") for j in (2 * x, 2 * x + 1) for i in range(0, 512, CUT)]
+        Ss = ["%s%d.%d" % (n, j, i) for n in ("S0", "S1") for j in (2 * x, 2 * x + 1) for i in range(0, 512, CUT)]
         part, both = [slice(256 * x + 128 * h, 256 * x + 128 * h + 128) for h in range(2)], slice(256 * x, 256 * x + 256)
-        last = [(T.U1, T.S1)[h][:, 1024 * x:1024 * x + 1024:8] for h in range(2)]
+        last = [(T.S0, T.S1)[h][:, 1024 * x:1024 * x + 1024:8] for h in range(2)]
         def turned(s): return T.I2[:, 128 - 16 * (V_ - 1 - s):256 - 16 * (V_ - 1 - s)]
 
         def add_part(s, n):
@@ -429,7 +460,8 @@ def rank_program(g, core, T, topo):
                            mm(T[n][:, 128 * h:128 * h + 128], turned(s), T.XL[:, s - 1, part[h]], False, True)], 1024,
                      r=["I2", "XO0%d" % x, "XL%d%d" % (s, x)], w=[n], b=[n])
         if t < V_ - 1:
-            task("s", [act(T.XO[:, t, part[h]], last[h]) for h in range(2)], 256, r=Ss, w=["XO%d%d" % (t, x)])
+            if XG: task("g", [lambda q, h=h: q.affine_select(T.XO[:, t, part[h]], last[h], [[0, 128]], A.is_gt, 0.0, 1, 0) for h in range(2)], 920, r=Ss, w=["XO%d%d" % (t, x)])
+            else: task("s", [act(T.XO[:, t, part[h]], last[h]) for h in range(2)], 256, r=Ss, w=["XO%d%d" % (t, x)])
             if t: send(T.XL[:, t - 1, both], T.XO[:, t, both], "x%d%d" % (t, x), -t, ["XO%d%d" % (t, x)], ["XL%d%d" % (t, x)])
         if 2 <= t < V_ - 1:
             add_part(t - 1, "D")
@@ -444,13 +476,20 @@ def rank_program(g, core, T, topo):
 
     lead.append(0)
     for t in range(V_ + 1):
-        for x in range(NB if t < V_ else 0): visit(t, x)
+        for xs in GROUPS if t < V_ else ():
+            steps = [visit(t, x) for x in xs]
+            for part in range(3):
+                for x, s in zip(xs, steps):
+                    lead[0] = (LEAD if t < V_ - 1 else LEAD4) * (NB - 1 - x) + CHAIN
+                    next(s)
+                if part < 2: sort(xs, part)
         lead[0] = 0
         for j in range(6 if 2 <= t < V_ else 0):
             if LATE[j][0] == 2: horner(t - 2, j, LATE[j][1])
         for j in range(6 if t else 0):
-            fetch(t - 1, j, GATE if t < V_ - 1 else GATE4 if t < V_ else None)
-            if t >= V_ - 1: horner(t - 1, j, LAST if t < V_ else None)
+            fetch(t - 1, j, None if j < FREE else GATE if t < V_ - 1 else GATE4 if t < V_ else None)
+            if j < FREE: horner(t - 1, j, None)
+            elif t >= V_ - 1: horner(t - 1, j, LAST if t < V_ else None)
             elif LATE[j][0] == 1: horner(t - 1, j, LATE[j][1] % t)
     task("y", [], 0, r=["out%d%d" % (x, h) for x in range(NB) for h in range(2)])
     emit(g, T, arrange(tasks))

from concourse.bass import DstId, RemoteDMATransfer
from concourse.mybir import AluOpType, ActivationFunctionType, AxisListType

A = AluOpType
F = ActivationFunctionType
V_, L_, W_, NB = 5, 384, 4096, 3
f32, bf, f16, i32, u16 = "float32", "bfloat16", "float16", "int32", "uint16"
SCRATCH = {
    "ar": ("sbuf", [128, W_], i32), "a0": ("sbuf", [128, W_], i32), "a1": ("sbuf", [128, 2048], i32),
    "TT": ("sbuf", [128, 2 * W_], i32), "MM": ("sbuf", [128, W_], f32), "pr": ("sbuf", [128, W_], bf),
    "acs": ("sbuf", [128, L_], f32), "acT": ("sbuf", [128, L_], f32),
    "rsi": ("sbuf", [128, L_], i32), "sti": ("sbuf", [128, 192], i32), "sS": ("sbuf", [128, 8, 136], f32),
    "G": ("sbuf", [128, 3072], bf), "GS": ("sbuf", [128, 3072], bf), "GA": ("sbuf", [128, 3072], f32),
    "GP": ("sbuf", [128, 3072], bf), "S0": ("sbuf", [128, 3072], f32), "WW": ("sbuf", [128, 3072], f32), "S1": ("sbuf", [128, 3072], f32),
    "sc": ("sbuf", [128, L_], f32), "UU": ("sbuf", [128, L_], bf), "UT": ("sbuf", [128, L_], bf),
    "MH": ("sbuf", [128, L_], bf), "sth": ("sbuf", [128, 192], f16), "ix2": ("sbuf", [128, 192], u16), "kb": ("sbuf", [128, L_], bf),
    "k1": ("sbuf", [128, L_], f32), "DD": ("sbuf", [128, 24, 17], f16), "pen": ("sbuf", [128, L_], f32), "AF": ("sbuf", [128, L_], f32),
    "SB0": ("sbuf", [128, 24, 2, 2, 2, 2], f32), "SB1": ("sbuf", [128, 24, 2, 2, 2, 2], f32),
    "kz": ("sbuf", [128, 49, 8], f32), "tz": ("sbuf", [128, 49, 8], f32), "cb": ("sbuf", [128, 24, 8], bf),
    "Z": ("sbuf", [128, 896], bf), "Zf": ("sbuf", [128, 256], f32), "I2": ("sbuf", [128, 256], f32), "I4": ("sbuf", [128, 128], f32),
    "Ib": ("sbuf", [128, 3, 128], bf), "Ih": ("sbuf", [128, 4, 128], f16), "Df": ("sbuf", [128, 2, 2, 64], f32),
    "sD": ("sbuf", [128, 8, 128], bf), "sL": ("sbuf", [128, 8, 16], bf), "sP": ("sbuf", [128, 8, 2, 8], bf),
    "Bk": ("sbuf", [128, 9, 16], bf), "sM": ("sbuf", [128, 8, 16], bf), "sC": ("sbuf", [128, 8, 2], f32), "col": ("sbuf", [128, 8], f32),
    "Lh": ("sbuf", [128, 8, 16], bf), "Lm": ("sbuf", [128, 8, 8, 2], bf), "Lp": ("sbuf", [128, 2, 8, 2, 8], bf), "p16": ("sbuf", [128, 128], f32),
    "xi": ("sbuf", [128, V_, 192], u16), "xo": ("sbuf", [128, V_, 192], u16),
    "ri": ("sbuf", [128, V_, L_], bf), "ro": ("sbuf", [128, V_, L_], bf),
    "XO": ("sbuf", [128, 4, 768], f32), "XL": ("sbuf", [128, 3, 768], f32), "YO": ("sbuf", [128, 768], f32),
    "K0": ("psum", [128, 512], f32), "M0": ("psum", [128, 512], f32), "K1": ("psum", [128, 512], f32), "M1": ("psum", [128, 512], f32),
    "K2": ("psum", [128, 512], f32), "M2": ("psum", [128, 512], f32), "D": ("psum", [128, 512], f32),
    "S": ("psum", [128, 32, 2, 2, 2, 2], f32),
}
POOL = {"v": 30, "s": 26, "t": 26, "g": 16, "d": 18}
SEMAPHORES = (["%s%d" % (e, i) for e in POOL for i in range(POOL[e])] + ["gone"]
              + ["%s%d%d" % (n, t, b) for n, k in (("m", 5), ("n", 5), ("x", 4)) for t in range(1, k) for b in range(NB)])
SLACK = 80
GATE = "kb1"
LAST = None
LEAD = 1000
LEAD4 = 3000
GATE4 = "kb2"
SHORT = {"s": 5000, "v": 2000, "t": 0, "g": 0, "y": 0}
CHAIN = 1
T0LEAD = 0
NA = 3
U16 = 1
U17 = 1
XG = 1
STH = 0
APART = 4
SMALL = 8
SLEAD = 0
OWN5 = (1,)
OWN6 = (5,)
BYDMA = 2
DDA = 0
FREE = 0
GROUPS = ((0,), (1,), (2,))
PASSES = 2
EARLY = 2
OWN3 = (1, 5)
OWN4 = (1, 3, 5)
SETUP = 30000
PLEAD = 0
PARTS = ((0, 1), (1, 2), (2, 4), (4, 6), (6, 8))
T0S = (0, 1, 2)
U0G = (0, 1, 2, 3, 4, 5, 6)
U0V = ()
OWN1 = (1,)
OWN2 = (5,)
STAG = 0
SEND = 5
MCUT = 256
KCUT = 2
LATE = ((1, "xo%d0"),) * 6
TLEAD = 2500
CUT = 256
HOP = 230
REMOTE = 2800
ISSUE = 300
PEF = 0.5
LOCAL = 2600
GATHER = 1.56
ALL, REV = slice(None), slice(None, None, -1)


def box(addrs, bits):
    f = len(addrs).bit_length() - 1
    free = [b for b in range(bits - 1, -1, -1) if any((a ^ addrs[0]) >> b & 1 for a in addrs)]
    if len(free) != f: return None
    for i, a in enumerate(addrs):
        if a ^ addrs[0] != sum((i >> (f - 1 - n) & 1) << b for n, b in enumerate(free)): return None
    return tuple((REV if addrs[0] >> b & 1 else ALL) if b in free else addrs[0] >> b & 1 for b in range(bits - 1, -1, -1))


def network(steps, at):
    if not steps: return []
    (mask, kind), bits = steps[0], (3, 4)
    pairs = [(w, w ^ mask) for w in at if w < w ^ mask]
    f = len(pairs).bit_length() - 1
    for fix in range(4):
        side = [sorted(p, key=lambda w: (at[w][0], at[w][1] >> fix & 1)) for p in pairs]
        order = sorted(range(len(pairs)), key=(lambda n: pairs[n][0]) if kind == "e" else (lambda n: at[side[n][0]][1]))
        for key in range(f if kind in "sn" else 1):
            for pos in range(f + 1 if kind == "u" else f if kind == "s" else 1):
                calls, new = [], {}
                for mx in range(1 if kind in "mn" else 2):
                    for v in range(2 if kind in "sn" else 1):
                        part = [n for i, n in enumerate(order) if kind not in "sn" or i >> key & 1 == v]
                        mem = {"b": 1 if mx else 0, "s": v, "n": v}.get(kind, 1)
                        out = [(i >> pos << pos + 1 | mx << pos | i & (1 << pos) - 1) if kind in "us" else i for i in range(len(part))]
                        new.update((pairs[n][mx], (mem, o)) for n, o in zip(part, out))
                        a, b = [(at[side[part[0]][h]][0], box([at[side[n][h]][1] for n in part], bits[at[side[part[0]][h]][0]])) for h in range(2)]
                        ok = all(at[side[n][h]][0] == (a, b)[h][0] for n in part for h in range(2)) and a[0] + b[0] > 0
                        calls.append((mx, (mem, box(out, bits[mem])), a, b, len(part)) if ok and a[1] and b[1] else None)
                if None in calls: continue
                rest = network(steps[1:], new)
                if rest is not None: return [calls] + rest
    return None


def needs(tasks):
    lastw, readers, out = {}, {}, []
    for n, k in enumerate(tasks):
        dep = set(lastw[r] for r in k["r"] + k["w"] if r in lastw)
        for w in k["w"]: dep.update(readers.get(w, ()))
        out.append(dep)
        for r in k["r"]: readers.setdefault(r, []).append(n)
        for w in k["w"]:
            lastw[w] = n; readers[w] = []
    return out


def arrange(tasks):
    dep = needs(tasks)
    for n, k in enumerate(tasks): dep[n].update(k["after"])
    n_ = len(tasks)
    def hop(a, b): return 0 if tasks[a]["e"] == tasks[b]["e"] == "t" or tasks[b]["e"] == "x" else HOP
    way, users = [0] * n_, [[] for _ in tasks]
    for n in range(n_ - 1, -1, -1):
        way[n] = tasks[n]["c"] + tasks[n]["lat"] + max([hop(n, u) + way[u] for u in users[n]] + [0])
        for m in dep[n]: users[m].append(n)
    def run(before, behind, urge, forward):
        left, ready, done, ends = [len(d) for d in before], [0 if forward else k["lat"] for k in tasks], [], [0] * n_
        free, bank, open_ = {}, {}, [n for n in range(n_) if not before[n]]
        while open_:
            def start(n):
                k = tasks[n]
                return max([ready[n], free.get(k["e"], 0)] + [t + HOP for b in k["b"] for e, t in bank.get(b, {}).items() if e != k["e"]])
            first, n = min((start(n), n) for n in open_)
            n = max((m for m in open_ if tasks[m]["e"] == tasks[n]["e"] and start(m) <= first + SLACK), key=lambda m: (urge[m], -m))
            k = tasks[n]
            end = ends[n] = start(n) + k["c"]
            if k["e"] != "x": free[k["e"]] = end
            for b in k["b"]: bank.setdefault(b, {})[k["e"]] = end
            open_.remove(n); done.append(k)
            for u in behind[n]:
                ready[u] = max(ready[u], end + (k["lat"] + hop(n, u) if forward else tasks[u]["lat"] + hop(u, n))); left[u] -= 1
                if not left[u]: open_.append(u)
        return max(e + k["lat"] for e, k in zip(ends, tasks)), done, ends
    best = now = run(dep, users, [way[n] + tasks[n]["lead"] for n in range(n_)], True)
    for _ in range(PASSES):
        now = run(dep, users, run(users, dep, now[2], False)[2], True)
        if now[0] < best[0]: best = now
    return best[1]


def emit(g, T, tasks):
    Q = {"v": g.vector, "s": g.scalar, "t": g.tensor, "g": g, "y": g.sync}
    bank, known = {}, {e: 0 for e in Q}
    for n, (k, dep) in enumerate(zip(tasks, needs(tasks))):
        e = k["e"]
        for b in k["b"]:
            dep.update(m for m in bank.get(b, ()) if tasks[m]["e"] != e)
            bank[b] = [m for m in bank.get(b, ()) if tasks[m]["e"] == e] + [n]
        k["wait"], k["before"] = [], 0
        if e != "x":
            for m in sorted(dep, reverse=True):
                if e == "t" and tasks[m]["e"] == "t": continue
                if not known[e] >> m & 1:
                    k["wait"].append(m); tasks[m]["sig"] = True
                    known[e] |= tasks[m]["before"] | 1 << m
            k["before"] = known[e]
    turn = {e: 0 for e in POOL}
    count, user = {}, {}
    for n, k in enumerate(tasks):
        if k["e"] == "x": continue
        q = Q[k["e"]]
        for m in k["wait"]:
            q.wait_ge(T.sem[tasks[m]["sem"]], tasks[m]["val"])
        sig = k.get("sig") and k["f"]
        if sig:
            p = "d" if k["dma"] else k["e"]
            for _ in range(POOL[p]):
                k["sem"] = "%s%d" % (p, turn[p] % POOL[p]); turn[p] += 1
                if k["sem"] not in user or k["before"] >> user[k["sem"]] & 1: break
            else:
                k["sem"] = min((user[s], s) for s in user if s[0] == p)[1]
                q.wait_ge(T.sem[k["sem"]], count[k["sem"]])
            user[k["sem"]] = n
        for f in k["f"]:
            ins = f(q)
            if sig:
                inc = 16 if k["dma"] else 1
                ins.then_inc(T.sem[k["sem"]], inc)
                count[k["sem"]] = count.get(k["sem"], 0) + inc
        if sig: k["val"] = count[k["sem"]]


def rank_program(g, core, T, topo):
    rank = T.rank_of(core)
    if rank is None:
        return
    N = len(T.cores)
    tasks, lead = [], [0]

    def task(e, f, c, r=(), w=(), b=(), dma=0):
        f = f if isinstance(f, list) else [f]
        tasks.append({"e": e, "f": f, "r": list(r), "w": list(w), "b": list(b), "dma": dma > 0, "c": c * PEF if e == "t" else c, "lat": dma, "after": [], "lead": lead[0] + (SHORT[e] if c <= 256 and lead[0] else 0) + SETUP * (len(lead) == 1)})
        return len(tasks) - 1

    def arrival(sem, val, w, like):
        tasks.append({"e": "x", "f": [], "r": [], "w": list(w), "b": [], "dma": False, "sem": sem, "val": val, "c": 0, "lat": REMOTE, "after": [like], "lead": 0})

    def ms(ap, c): return lambda q: q.memset(ap, c)
    def cp(o, i): return lambda q: q.tensor_copy(o, i)
    def tt(o, a, b, op): return lambda q: q.tensor_tensor(o, a, b, op)
    def ts(o, a, s1, op0, s2=None, op1=None):
        if op1 is None: return lambda q: q.tensor_scalar(o, a, s1, None, op0)
        return lambda q: q.tensor_scalar(o, a, s1, s2, op0, op1)
    def red(o, i): return lambda q: q.tensor_reduce(o, i, AxisListType.X, A.add)
    def scan(o, a, b, op0, op1): return lambda q: q.tensor_tensor_scan(o, a, b, 0.0, op0, op1)
    def act(o, i, fn=F.Identity, bias=0.0, scale=1.0): return lambda q: q.activation(o, i, fn, bias=bias, scale=scale)
    def mm(o, l, r, st=True, sp=True): return lambda q: q.matmul(o, l, r, st, sp)
    def dma(o, i): return lambda q: q.dma_start(o, i)
    def load(e, fs, kib, r=(), w=()): task(e, fs, 60 * len(fs), r=r, w=w, dma=LOCAL + 4 * kib)
    def paint(name, ap, n, pat, val, base, cm, src=None, op=A.not_equal):
        task("g", lambda q: q.affine_select(ap, ap if src is None else src, pat, op, val, base, cm), 200 + 2 * n, r=[name, "Z"], w=[name])
    def ch(j): return slice(512 * j, 512 * j + 512)
    def back(a, b): return slice(b - 1, a - 1 if a else None, -1)
    def each(s): return ["%s%d" % (s, x) for x in range(NB)]

    for a, b in PARTS:
        lead[0] = 10 ** 6 * (8 - a)
        load("y", [dma(T.ar[:, 512 * a:512 * b], T.arcs[:, 512 * a:512 * b])], 256 * b, w=["ar%d" % j for j in range(a, b)])
    lead[0] = 10 ** 5
    load("s", [dma(T.sti[:, :], T.st0[:, :])], 300, w=["sti"])
    lead[0] = 10 ** 6 * (8 - SMALL) + 1
    load("y", [dma(T.rsi[0:64, :], T.rs0[:, :]), dma(T.acs[:, :], T.ac[:, :])], 256 * SMALL + 400, w=["rsi", "acs"])
    lead[0] = 0

    task("v", [ms(T.Z[:], 0.0), ms(T.Zf[:], 0.0)], 704, w=["Z"])
    task("v", [ms(T.sD[64:66, 0:7, :], 0.0), ms(T.sD[64:66, 7, :], 512.0), ms(T.sD[0:64, 7, :], 0.0), ms(T.sL[64:66], -15.5),
               ms(T.ri[64:128, 0, :], 1.0), ms(T.Bk[:], 1.0), ms(T.sP[0:64], 0.0), ms(T.Lp[:], 0.0), ms(T.p16[:], 0.0), ms(T.UU[:, 0:L_:128], 0.0),
               ms(T.sP[64:66], -25.0 / 64), ms(T.kz[:, 0:49:2, :], 0.0), ms(T.tz[:, 0:49:2, :], 0.0)],
         1900, w=["sDc", "sLc", "ri0c", "Bk", "sP", "Lp", "p16", "sPc", "zeros"] + each("UU"))
    task("v", [ms(T.p16[:, 0:128:16], 1000.0), ts(T.DD[:, :, 0], T.Z[:, 0:24], -4096.0, A.add)], 128, r=["Z"], w=["p16"] + each("DD"))
    paint("I2", T.I2[:], 256, [[0, 2], [-1, 128]], 1.0, 0, 1, T.Zf[:])
    paint("sD", T.sD[0:64, 0:7, :], 896, [[-1, 7], [-8, 8], [0, 16]], 1.0, 0, 1, T.Z[0:64, 0:896])
    paint("sD", T.sD[0:64, 0:7, :], 896, [[-1, 7], [-8, 8], [0, 16]], -1.0, -1, 1)
    paint("sL", T.sL[0:64], 128, [[-8, 8], [0, 16]], -1.0, 0, 1, T.Z[0:64, 0:128])
    paint("Bk", T.Bk[:, 1:9, :], 128, [[-16, 8], [0, 16]], 0.0, 0, 1, op=A.is_ge)
    paint("Bk", T.Bk[:, 1:9, :], 128, [[16, 8], [0, 16]], 0.0, 15, -1, op=A.is_ge)
    paint("Bk", T.Bk[:, 0, :], 16, [[0, 16]], 0.0, -112, 1, op=A.is_ge)
    paint("Lh", T.Lh[:], 128, [[-1, 128]], 1.0, 0, 1, T.Z[:, 0:128])
    paint("Lh", T.Lh[:, :, 0:15], 120, [[-16, 8], [-1, 15]], -1.0, -1, 1)
    paint("Lm", T.Lm[:], 128, [[-2, 64], [0, 2]], 1.0, 0, 1, T.Z[:, 0:128])
    paint("Lm", T.Lm[:, :, 0:7, :], 112, [[-16, 8], [-2, 7], [0, 2]], -1.0, -2, 1)
    for a, b, base in ((1, 8, 0), (0, 1, -56)):
        paint("sP", T.sP[0:64, a:b, :, 1:8], 98, [[-8, b - a], [0, 14]], 1.0 / 128, base, 1)
        paint("sP", T.sP[0:64, a:b, :, 1:8], 98, [[-8, b - a], [0, 2], [-1, 7]], -1.0 / 128, base - 1, 1)
    task("g", lambda q: q.iota(T.kb[:, 0:128], [[0, 8], [1, 16]], 0, 0, allow_small_or_imprecise_dtypes=True), 400, w=["kb0"])
    paint("Df", T.Df[:, 0], 128, [[-1, 2], [-2, 64]], 4096.0, 0, 1, T.Zf[:, 0:128])
    I1 = T.I2[:, 0:128]
    task("s", [act(T.Ib[:, n, :], I1, scale=s) for n, s in enumerate((1.0, -4096.0, 2.0 ** -7))] + [act(T.I4[:], I1, scale=4096.0)], 512, r=["I2"], w=["Ib"])
    task("s", act(T.Df[:, 1], T.Df[:, 0], scale=-1.0), 128, r=["Df"], w=["Dn"])
    task("v", [ts(T.Ih[:, n, :], I1, s, A.mult) for n, s in enumerate((1.0, -1.0, -4096.0, 2.0 ** -12))]
         + [red(T.col[:, u:u + 1], T.I2[:, u:128:2]) for u in range(2)] + [red(T.col[:, 2:3], T.I2[:, 0:128:16])], 700, r=["I2"], w=["Ih", "col"])
    task("v", [ts(T.col[:, 4:5], T.col[:, 1:2], 8192.0, A.mult, -4096.0, A.add), ts(T.col[:, 6:7], T.col[:, 2:3], 6144.0, A.mult),
               ts(T.col[:, 3:4], T.col[:, 2:3], -1.0, A.mult, 1.0, A.add), ts(T.sP[64:65], T.kb[64:65, 0:128], 1.0 / 2048, A.mult)], 256,
         r=["col", "kb0"], w=["col4", "sPc"])
    task("v", ts(T.col[:, 5:6], T.col[:, 4:5], T.col[:, 6:7], A.add), 64, r=["col4"], w=["col5"])
    task("s", [act(T.sC[:, :, u], T.Bk[:, 0:8, 0], scale=T.col[:, u:u + 1]) for u in range(2)] + [act(T.sM[:], T.Bk[:, 0:8, :], scale=-1.0 / 128)]
         + [act(T.Lp[:, b, :, b, :], T.Bk[:, 1:9, 0:8], scale=T.col[:, 5:6]) for b in range(2)], 400, r=["Bk", "col", "col5", "Lp"], w=["sC", "Lp"])
    task("s", [act(T.ro[64:128, t, :], T.Z[64:128, 0:L_], F.Exp) for t in range(V_)], V_ * L_ + 1600, r=["Z"], w=["roc"])
    task("s", [act(T.sS[:, a:a + 4], T.Z[:, 0:544]) for a in (0, 4)], 1088, r=["Z"], w=["sS"])
    paint("sS", T.sS[:, :, 7:135:8], 128, [[-2, 8], [-16, 8], [-1, 2]], 1.0, 0, 1)
    lead[0] = 10 ** 5
    task("s", act(T.AF[:, 0:192], T.sti[:]), 192, r=["sti"], w=["kb1"])
    lead[0] = 0
    for q in range(8):
        task("t", [mm(T.K0[:, q:192:8], T.sS[:, q, 7 - k:135 - k], T.AF[:, 24 * k:24 * k + 24], k == 0, k == 7) for k in range(8)], 2048, r=["sS", "kb1"], w=["K0"], b=["K0"])
    task("s", act(T.xi[:, 0, :], T.K0[:, 0:192]), 192, r=["K0"], w=each("xi0"), b=["K0"])

    for j in range(8):
        n = ("K2", "D", "M0", "M1")[j % 4]
        lead[0] = TLEAD * (8 - j)
        a1, h1 = (T.a1, "b") if j < APART else (T.ar, "ar")
        task("v", ts(T.a0[:, ch(j)], T.ar[:, ch(j)], 32767, A.bitwise_and), 512, r=["ar%d" % j], w=["a%d" % j])
        task("v", ts(a1[:, ch(j)], T.ar[:, ch(j)], 15, A.logical_shift_right), 512, r=["ar%d" % j], w=[h1 + str(j)])
        lead[0] += PLEAD
        task("s", act(T[n][:], a1[:, ch(j)]), 512, r=[h1 + str(j)], w=[n], b=[n])
        task("v", tt(T.MM[:, ch(j)], T.a0[:, ch(j)], T[n][:], A.min), 512, r=[n, "a%d" % j], w=["MM%d" % j], b=[n])
        lead[0] = TLEAD * (8 - j)
        if j >= BYDMA:
            task("s", act(T.TT[:, ch(8 + j)], a1[:, ch(j)]), 512, r=[h1 + str(j)], w=["TU%d" % j])
            task("s", act(T.TT[:, ch(j)], T.a0[:, ch(j)]), 512, r=["a%d" % j], w=["TT%d" % j])
        if j % 2:
            c, two = slice(512 * j - 512, 512 * j + 512), (j - 1, j)
            load("y", [dma(T.TT[0:128:2, W_ + c.start:W_ + c.stop], T.a0[1:128:2, c]), dma(T.TT[1:128:2, c], a1[0:128:2, c])]
                 + [dma(T.TT[0:128:2, c], T.a0[0:128:2, c]), dma(T.TT[1:128:2, W_ + c.start:W_ + c.stop], a1[1:128:2, c])] * (j < BYDMA), 512,
                 r=["%s%d" % (h, i) for i in two for h in ("a", h1)], w=["T%s%d" % (h, i) for i in two for h in "TU"])
    lead[0] = SLEAD
    task("s", act(T.ri[0:64, 0, :], T.rsi[0:64, :], bias=98.0, scale=-1.0), 384, r=["rsi", "ri0c"], w=each("ri0"))
    task("t", [lambda q, c=c: q.transpose(T.M2[:, 128 * c:128 * c + 128], T.acs[:, 128 * c:128 * c + 128], I1) for c in range(3)], 1536,
         r=["acs", "I2"], w=["M2"], b=["M2"])
    task("s", act(T.acT[:], T.M2[:, 0:L_]), 384, r=["M2"], w=["acT"], b=["M2"])
    load("y", [dma(T.pr[16:128, :], T.pay[0:112, :]), dma(T.pr[0:16, :], T.pay[112:128, :])], 1024, r=["TU7"], w=["pr"])
    MMs, TTs = ["MM%d" % j for j in range(8)], ["T%s%d" % (h, j) for j in range(8) for h in "TU"]
    sent = [0]

    def send(out, src, sem, step, r, w):
        dst = T.cores[(rank + step) % N]
        rid, pid, _ = topo.addr(dst)
        sent[0] += len(topo.engines(core, dst))
        n = task("g", lambda q: q.remote_dma(out, src, T.sem[sem], T.sem.gone, pid, rid, topo.mask(core, dst)), ISSUE, r=r)
        arrival(sem, len(topo.engines(T.cores[(rank - step) % N], core)), w, n)

    def spread(n, R, t, name, j):
        task("t", [mm(T[n][:, k:512:8], T.sD[0:66, k, :], R[0:66, t, 64 * j:64 * j + 64]) for k in range(8)], 512,
             r=["sD", "sDc", "roc", name], w=[n], b=[n])

    NETS = {n: [network(list(zip((1, 3, 1, 7, 2, 1, 15, 4, 2, 1), kinds)), {i: (i & 1, i >> 1) for i in range(16)}) for kinds in both]
            for n, both in ((1, ("bubusbusue", "bubusbmuue")), (2, ("bsbssbssse", "bsbssbnuse")))}
    UP = 128.5 + 2.0 ** -13
    SINK = 2 * (16 * 132 - 800) + 2047.0 / 4096

    def visit(t, x):
        cg, lanes, cols, odd = slice(8 * x, 8 * x + 8), slice(128 * x, 128 * x + 128), slice(64 * x, 64 * x + 64), slice(16 * x + 1, 16 * x + 17, 2)
        Kn, Mn = "K%d" % x, "M%d" % x
        K, M = T[Kn], T[Mn]
        def nm(s): return "%s%d" % (s, x)
        xi, ri, xo, ro = ["%s%d%d" % (s, t, x) for s in ("xi", "ri", "xo", "ro")]
        pieces = (2 * x, 2 * x + 1)
        GSs, GAs, GS0 = ["GS%d.%d" % (j, i) for j in pieces for i in range(0, 512, MCUT)], ["GA%d" % j for j in pieces], T.GS[:, 1024 * x:1024 * x + 1024:8]

        if STH: task("s", act(T.sth[:, cols], T.xi[:, t, cols], bias=-2048.0), 64, r=[xi], w=[nm("sth")])
        else: task("v", ts(T.sth[:, cols], T.xi[:, t, cols], -2048.0, A.add), 64, r=[xi], w=[nm("sth")])
        for j in pieces:
            n = (Mn, Kn)[j % 2]
            spread(n, T.ri, t, ri, j)
            win = T.MM[:, 0:W_].indirect(T.xi[:, t, 32 * j:32 * j + 32])
            if j in (OWN5 if t == V_ - 1 else OWN1 if t >= EARLY else OWN3): task("v", ts(T.G[:, ch(j)], win, 2.0 ** -12, A.mult, UP, A.add), 60 + 512 * GATHER, r=MMs + [xi], w=["G%d" % j])
            else: task("s", act(T.G[:, ch(j)], win, bias=UP, scale=2.0 ** -12), 80 + 512 * GATHER, r=MMs + [xi], w=["G%d" % j])
            if STAG and (t or x) and t < SEND: tasks[-1]["after"] = [max(n for n, k in enumerate(tasks) if STAG % ((x - 1) % NB) in k["w"])]
            for i in range(0, 512, MCUT):
                bk = back(512 * j + i, 512 * j + i + MCUT)
                task("v", scan(T.GS[:, bk], T[n][:, back(i, i + MCUT)], T.G[:, bk], A.add, A.min), MCUT, r=["G%d" % j, n], w=["GS%d.%d" % (j, i)], b=[n])
        task("t", [mm(K[:, 0:128], T.ri[0:66, t, lanes], T.sL[0:66], True, False), mm(K[:, 0:128], GS0, T.Ib[:, 0, :], False, True)], 256,
             r=[ri, "sL", "sLc", "Ib"] + GSs, w=[Kn], b=[Kn])
        task("v", tt(K[:, 0:128], K[:, 0:128], T.acT[:, lanes], A.add), 128, r=["acT"], w=[Kn], b=[Kn])
        task("v", [scan(T.sc[:, lanes], T.p16[:], K[:, 0:128], A.add, A.min), scan(K[:, 255:127:-1], T.p16[:], K[:, 127::-1], A.add, A.min)], 256,
             r=["p16"], w=[nm("sc"), Kn], b=[Kn])
        task("v", tt(T.UU[:, 128 * x + 1:128 * x + 128], K[:, 129:256], T.sc[:, 128 * x:128 * x + 127], A.is_lt), 128, r=[Kn, nm("sc")], w=[nm("UU")], b=[Kn])
        task("t", mm(K[:, 0:128], T.UU[:, lanes], T.Ib[:, 0, :]), 128, r=[nm("UU"), "Ib"], w=[Kn], b=[Kn])
        task("s", act(T.UT[:, lanes], K[:, 0:128], bias=T.col[:, 2:3], scale=T.col[:, 3:4]), 128, r=[Kn, "col4"], w=[nm("UT")], b=[Kn])
        task("t", [mm(K[:, 256:320], T.Ih[:, 0, :], T.sth[:, cols], True, False)]
             + [mm(K[:, 256:320], T.Lp[:, b], T.UT[:, 128 * x + b:128 * x + 128:2], False, b == 1) for b in range(2)], 192,
             r=[nm("UT"), nm("sth"), "Lp", "Ih"], w=[Kn], b=[Kn])
        task("vs"[U16], (cp, act)[U16](T.ix2[:, cols], K[:, 256:320]), 64, r=[Kn], w=[nm("ix2")], b=[Kn])
        task("t", [mm(M[:, 0:128], T.Lm[:], T.UT[:, lanes]), mm(M[:, 256:384], T.Lh[:], T.UT[:, lanes])], 256, r=[nm("UT"), "Lm", "Lh"], w=[Mn], b=[Mn])
        task("v", tt(T.MH[:, lanes], M[:, 256:384], GS0, A.mult), 128, r=[Mn] + GSs, w=[nm("MH")], b=[Mn])
        for j in pieces:
            e, f = ("v", cp) if j in (OWN6 if t == V_ - 1 else OWN2 if t >= EARLY else OWN4) else ("s", act)
            task(e, f(T.GA[:, ch(j)], T.TT[:, 0:2 * W_].indirect(T.ix2[:, 32 * j:32 * j + 32])), 80 + 512 * GATHER, r=TTs + [nm("ix2")], w=["GA%d" % j])
        ga = [T.GA[:, 1024 * x + k:1024 * x + 1024:8] for k in range(8)]
        for h in range(0, 8, KCUT):
            ks = range(h, h + KCUT)
            task("v", [tt(ga[k], M[:, 0:128], ga[k], A.mult) for k in ks], 128 * KCUT, r=[Mn] + GAs, w=["GB%d%d" % (x, h)], b=[Mn])
            task("t", [mm(K[:, 384 + k:512:8], ga[k], T.sC[:]) for k in ks], 256 * KCUT, r=["sC", "GB%d%d" % (x, h)] + GAs, w=[Kn], b=[Kn])
        task("s", [act(T.kb[:, lanes], K[:, 384:512], bias=UP, scale=2.0 ** -12), act(T.AF[:, lanes], K[:, 384:512], bias=129 * 4096.0 - 2048)], 256,
             r=[Kn], w=[nm("kb")], b=[Kn])
        task("t", [mm(K[:, 0:128], I1, T.AF[:, lanes], True, False)] + [mm(K[:, 0:128], T.Ib[:, i, :], T.kb[:, lanes], False, False) for i in (1, 2)]
             + [mm(K[:, 0:128], T.ri[0:66, t, lanes], T.sP[0:66], False, False), mm(K[:, 0:128], T.MH[:, lanes], T.sM[:], False, True)], 1024,
             r=[nm("kb"), nm("MH"), ri, "sP", "sPc", "sC", "Ib", "I2"], w=[Kn], b=[Kn])
        task("s", act(T.SB0[:, cg, 0], K[:, 1:128:2]), 64, r=[Kn], w=[nm("so0")], b=[Kn])
        yield
        if DDA:
            task("s", act(T.rsi[:, lanes], T.k1[:, lanes]), 128, r=[nm("k1")] + each("ri0"), w=[nm("rs")])
            task("s", act(T.DD[:, cg, 1:17], T.rsi[:, lanes]), 128, r=[nm("rs")], w=[nm("DD")])
        else: task("v", ts(T.DD[:, cg, 1:17], T.k1[:, lanes], 1.5 * 2 ** 23, A.add, 1.5 * 2 ** 23, A.subtract), 128, r=[nm("k1")], w=[nm("DD")])
        task("t", mm(M[:, 0:128], T.I4[:], T.k1[:, lanes], True, False), 512, r=[nm("k1"), "Ib"], w=[Mn], b=[Mn])
        task("t", [mm(K[:, 0:128], T.Ih[:, 0, :], T.DD[:, cg, 0:16], True, False), mm(K[:, 0:128], T.Ih[:, 1, :], T.DD[:, cg, 1:17], False, True)], 256,
             r=[nm("DD"), "Ih"], w=[Kn], b=[Kn])
        task("t", [mm(M[:, 0:128], T.Ih[:, n, :], T.DD[:, cg, 1:17], False, n == 3) for n in (2, 3)], 256, r=[nm("DD"), "Ih"], w=[Mn], b=[Mn])
        task("s", act(T.pen[:, lanes], K[:, 0:128], bias=SINK, scale=8192.0), 128, r=[Kn], w=[nm("pen")], b=[Kn])
        task("v", [tt((T.S, T.SB0)[v][:, cg, 0], M[:, v:128:2], T.pen[:, 128 * x + v:128 * x + 128:2], A.max) for v in range(2)], 128,
             r=[Mn, nm("pen")], w=[nm("so0")], b=[Mn, "S"])
        yield
        task("v", ts(T.tz[:, odd, :], T.kz[:, odd, :], 1.5 * 2 ** 24, A.add, 1.5 * 2 ** 24, A.subtract), 64, r=[nm("kz")], w=[nm("tz")])
        task("s", act(T.cb[:, cg], T.kz[:, odd, :], bias=180 - 15.0 / 32, scale=1.0 / 32), 64, r=[nm("kz")], w=[nm("cb")])
        for s, z in enumerate(("kz", "tz")):
            task("t", [mm(K[:, 0:64], T[z][:, 16 * x + 1 - b:16 * x + 17 - b, :], T.Df[:, s, b, :], s + b == 0, s + b == 2) for b in range(2)], 512,
                 r=[nm(z), "Df", "Dn", "zeros"], w=[Kn], b=[Kn])
        if U17: task("s", act(T.xo[:, t, cols], K[:, 0:64], bias=2048.0), 64, r=[Kn], w=[xo], b=[Kn])
        else: task("v", ts(T.xo[:, t, cols], K[:, 0:64], 2048.0, A.add), 64, r=[Kn], w=[xo], b=[Kn])
        task("t", mm(M[0:64, 0:128], T.cb[:, cg], T.Ib[:, 0, :]), 128, r=[nm("cb"), "Ib"], w=[Mn], b=[Mn])
        task("s", act(T.ro[0:64, t, lanes], M[0:64, 0:128], F.Abs, bias=-228.0), 128, r=[Mn], w=[ro], b=[Mn])
        if t < V_ - 1:
            sem = "%d%d" % (t + 1, x)
            send(T.xi[:, t + 1, cols], T.xo[:, t, cols], "m" + sem, 1, [xo], ["xi" + sem])
            send(T.ri[:, t + 1, lanes], T.ro[:, t, lanes], "n" + sem, 1, [ro, "roc"], ["ri" + sem])
        yield

    def sort(xs, second):
        def view(ys, pp, place):
            cg = slice(8 * ys[0], 8 * ys[-1] + 8)
            return T.S[(ALL, cg, pp) + place[1]] if place[0] == 0 else (T.SB0, T.SB1)[pp][(ALL, cg) + place[1]]
        def last(mx): return T.kz[:, 16 * xs[0] + 1:16 * xs[-1] + 17:2, mx:8:2] if second else T.k1[:, 128 * xs[0] + mx:128 * xs[-1] + 128:2]
        steps = NETS[min(len(xs), 2)][second]
        for n, calls in enumerate(steps):
            pp, head, end = n % 2, n == 0 and not second, n == len(steps) - 1
            for ys in [(x,) for x in xs] if head else [xs]:
                Kn = ["K%d" % ys[0]] * head
                task("v", [tt(last(mx) if end else view(ys, 1 - pp, o), T[Kn[0]][:, 0:128:2] if head else view(ys, pp, i0), view(ys, pp, i1), A.max if mx else A.min)
                           for mx, o, i0, i1, _ in calls], sum(max(64, 8 * len(ys) * k * (i0[0] + i1[0])) for _, _, i0, i1, k in calls),
                     r=["so%d%d" % (pp, y) for y in ys] + Kn, w=["%s%d" % (("k1", "kz")[second] if end else "so%d" % (1 - pp), y) for y in ys], b=["S"] + Kn)

    def behind(name):
        if name: tasks[-1]["after"] = [max(n for n, k in enumerate(tasks) if name in k["w"])]

    def fetch(t, j, gate):
        x = j // 2
        d = "M%d" % x if t == V_ - 1 and j % 2 else "D"
        spread(d, T.ro, t, "ro%d%d" % (t, x), j)
        task("s", act(T.GP[:, ch(j)], T.pr[:, 0:W_].indirect(T.xo[:, t, 32 * j:32 * j + 32])), 80 + 512 * GATHER, r=["pr", "xo%d%d" % (t, x)], w=["GP%d" % j])
        behind(gate)
        task("s", act(T.WW[:, ch(j)], T[d][:], F.Exp, scale=-0.125), 512, r=[d], w=["WW%d" % j], b=[d])
        behind(gate)

    def horner(t, j, gate):
        for i in range(0, 512, CUT):
            bk = back(512 * j + i, 512 * j + i + CUT)
            for S, op, n in ((T.S0, A.add, "S0"), (T.S1, A.max, "S1")):
                task("v", scan(S[:, bk], T.WW[:, bk], T.GP[:, bk], A.mult, op), CUT, r=["WW%d" % j, "GP%d" % j], w=["%s%d.%d" % (n, j, i)])
                behind(gate)
        if j % 2: hand_back(t, j // 2)

    def hand_back(t, x):
        lanes, Kn = slice(128 * x, 128 * x + 128), "K%d" % x
        K = T[Kn]
        def nm(s): return "%s%d" % (s, x)
        Ss = ["%s%d.%d" % (n, j, i) for n in ("S0", "S1") for j in (2 * x, 2 * x + 1) for i in range(0, 512, CUT)]
        part, both = [slice(256 * x + 128 * h, 256 * x + 128 * h + 128) for h in range(2)], slice(256 * x, 256 * x + 256)
        last = [(T.S0, T.S1)[h][:, 1024 * x:1024 * x + 1024:8] for h in range(2)]
        def turned(s): return T.I2[:, 128 - 16 * (V_ - 1 - s):256 - 16 * (V_ - 1 - s)]

        def add_part(s, n):
            for h in range(2):
                task("t", [mm(T[n][:, 128 * h:128 * h + 128], turned(0 if s == 1 else V_ - 1), T.XO[:, 0, part[h]], True, False),
                           mm(T[n][:, 128 * h:128 * h + 128], turned(s), T.XL[:, s - 1, part[h]], False, True)], 1024,
                     r=["I2", "XO0%d" % x, "XL%d%d" % (s, x)], w=[n], b=[n])
        if t < V_ - 1:
            if XG: task("g", [lambda q, h=h: q.affine_select(T.XO[:, t, part[h]], last[h], [[0, 128]], A.is_gt, 0.0, 1, 0) for h in range(2)], 920, r=Ss, w=["XO%d%d" % (t, x)])
            else: task("s", [act(T.XO[:, t, part[h]], last[h]) for h in range(2)], 256, r=Ss, w=["XO%d%d" % (t, x)])
            if t: send(T.XL[:, t - 1, both], T.XO[:, t, both], "x%d%d" % (t, x), -t, ["XO%d%d" % (t, x)], ["XL%d%d" % (t, x)])
        if 2 <= t < V_ - 1:
            add_part(t - 1, "D")
            task("s", act(T.XO[:, 0, both], T.D[:, 0:256]), 256, r=["D"], w=["XO0%d" % x], b=["D"])
        if t == V_ - 1:
            add_part(t - 1, Kn)
            task("v", [tt(T.YO[:, part[h]], K[:, 128 * h:128 * h + 128], last[h], A.add) for h in range(2)], 256, r=Ss + [Kn], w=[nm("YO")], b=[Kn])
            cut = 16 * (V_ % 8)
            for e, y, h in (("y", T.ys, 0), ("s", T.ym, 1)):
                load(e, [dma(y[0:128 - cut, lanes], T.YO[cut:128, part[h]]), dma(y[128 - cut:128, lanes], T.YO[0:cut, part[h]])], 64,
                     r=[nm("YO")], w=["out%d%d" % (x, h)])

    lead.append(0)
    for t in range(V_ + 1):
        for xs in GROUPS if t < V_ else ():
            steps = [visit(t, x) for x in xs]
            for part in range(3):
                for x, s in zip(xs, steps):
                    lead[0] = (LEAD if t < V_ - 1 else LEAD4) * (NB - 1 - x) + CHAIN
                    next(s)
                if part < 2: sort(xs, part)
        lead[0] = 0
        for j in range(6 if 2 <= t < V_ else 0):
            if LATE[j][0] == 2: horner(t - 2, j, LATE[j][1])
        for j in range(6 if t else 0):
            fetch(t - 1, j, None if j < FREE else GATE if t < V_ - 1 else GATE4 if t < V_ else None)
            if j < FREE: horner(t - 1, j, None)
            elif t >= V_ - 1: horner(t - 1, j, LAST if t < V_ else None)
            elif LATE[j][0] == 1: horner(t - 1, j, LATE[j][1] % t)
    task("y", [], 0, r=["out%d%d" % (x, h) for x in range(NB) for h in range(2)])
    emit(g, T, arrange(tasks))
    g.wait_ge(T.sem.gone, sent[0])
